import numpy as np
import ml_dtypes


def mxq(x, axis, fmt="e4m3"):
    dtype, down = {"e4m3": (ml_dtypes.float8_e4m3fn, 7), "e5m2": (ml_dtypes.float8_e5m2, 14)}[fmt]
    v = np.moveaxis(np.asarray(x, np.float32).astype(ml_dtypes.bfloat16).astype(np.float64), axis, -1)
    blocks = v.reshape(v.shape[:-1] + (-1, 32))
    amax = np.abs(blocks).max(-1, keepdims=True)
    byte = np.maximum(np.where(amax > 0, np.frexp(amax)[1] - 1 + 127, 0) - down, 1)
    scale = np.exp2(byte - 127.0)
    codes = (blocks / scale).astype(np.float32).astype(dtype).astype(np.float64)
    return np.moveaxis((codes * scale).reshape(v.shape), -1, axis)


WIDE = False


def mx_kscale(k):
    if not WIDE:
        return np.ones(k)
    levels = np.array([30, -30])
    if k % 512:
        return np.exp2(np.random.permutation(np.resize(levels, k // 32))).repeat(32)
    a = np.empty((k // 512, 16))
    for p in range(k // 512):
        a[p, :8] = np.random.permutation(np.resize(levels, 8))
        for g in range(8):
            far = levels[np.abs(levels - a[p, g]) >= 10]
            a[p, g + 8] = far[np.random.randint(len(far))]
    return np.exp2(a.ravel()).repeat(32)


def f64(x):
    return np.asarray(x).astype(np.float64)


def striped(idx):
    return np.tile(idx.reshape(-1, 16).T, (8, 1)).astype(np.uint16)


def unstriped(offs):
    return offs[:16].T.reshape(-1).astype(np.int64)


E2M1 = np.array([0.0, 0.5, 1.0, 1.5, 2.0, 3.0, 4.0, 6.0, -0.0, -0.5, -1.0, -1.5, -2.0, -3.0, -4.0, -6.0])


def pack_weight(w, fmt):
    k, n = w.shape
    w = f64(np.asarray(w, np.float32).astype(ml_dtypes.bfloat16)).reshape(k // 32, 32, n)
    amax = np.abs(w).max(1)
    if fmt == "e4m3":
        byte = np.frexp(amax)[1] - 1 + 127 - 7
    elif fmt == "e5m2":
        byte = np.frexp(amax)[1] - 1 + 127 - 14
    else:
        mant, ex = np.frexp(amax / 6.0)
        byte = np.where(mant > 0.5, ex, ex - 1) + 127
    byte = np.clip(np.where(amax > 0, byte, 1), 1, 254)
    scaled = (w * np.exp2(127.0 - byte)[:, None, :]).reshape(k, n).astype(np.float32)
    by_word = np.ascontiguousarray(scaled.reshape(k // 512, 128, 4, n).transpose(0, 1, 3, 2))
    if fmt == "e4m3":
        words = by_word.astype(ml_dtypes.float8_e4m3fn).view(np.uint8)
    elif fmt == "e5m2":
        words = by_word.astype(ml_dtypes.float8_e5m2).view(np.uint8)
    else:
        c = by_word.astype(ml_dtypes.float4_e2m1fn).view(np.uint8) & 0xF
        words = (c[..., 0::2] | (c[..., 1::2] << 4)).reshape(k // 512, 128, 2 * n)
    return np.ascontiguousarray(words), np.ascontiguousarray(byte.astype(np.uint8).reshape(k // 512, 16, n))


def unpack_weight(words, scales, fmt):
    g, _, n = scales.shape
    words = np.ascontiguousarray(words).reshape(g, 128, n, -1)
    if fmt == "e4m3":
        vals = words.view(ml_dtypes.float8_e4m3fn).astype(np.float64)
    elif fmt == "e5m2":
        vals = words.view(ml_dtypes.float8_e5m2).astype(np.float64)
    else:
        nib = np.empty((g, 128, n, 4), np.uint8)
        nib[..., 0::2] = words & 0xF
        nib[..., 1::2] = words >> 4
        vals = E2M1[nib]
    vals = vals * np.repeat(np.exp2(scales.astype(np.float64) - 127.0), 8, axis=1)[..., None]
    return vals.transpose(0, 1, 3, 2).reshape(g * 512, n)


def d_silu(v):
    s = 1.0 / (1.0 + np.exp(-np.maximum(v, -700.0)))
    return s * (1.0 + v * (1.0 - s))


K, T, E, C, H, N = 256, 1024, 2, 512, 512, 512


def by_expert(wq, xq):
    return np.concatenate([wq[e].T @ xq[:, e * C:(e + 1) * C] for e in range(E)], axis=1)


def setup_inputs():
    n = np.random.standard_normal
    v = mx_kscale(N)
    u = mx_kscale(H)
    slot_token = np.random.permutation(T)[:E * C]
    w_slot = np.random.uniform(0.2, 1.0, E * C)
    dy = pack_weight(n((N, T)) * v[:, None], "e5m2")
    wt = pack_weight(n((N, K)) / np.sqrt(N) / v[:, None], "e2m1")
    wbt = [pack_weight(m, "e4m3") for m in n((E, N, H)) / np.sqrt(N) / v[None, :, None] * u]
    wat = [pack_weight(m, "e4m3") for m in n((E, H, K)) / np.sqrt(H) / u[None, :, None]]
    return {
        "dy_words": dy[0],
        "dy_scales": dy[1],
        "wt_words": wt[0],
        "wt_scales": wt[1],
        "wbt_words": np.stack([m[0] for m in wbt]),
        "wbt_scales": np.stack([m[1] for m in wbt]),
        "wat_words": np.stack([m[0] for m in wat]),
        "wat_scales": np.stack([m[1] for m in wat]),
        "a": (n((H, E * C))).astype(np.float32),
        "gate": (np.tile(w_slot, (128, 1))).astype(np.float32),
        "offs": striped(slot_token),
    }


def reference(dy_words, dy_scales, wt_words, wt_scales, wbt_words, wbt_scales, wat_words, wat_scales, a, gate, offs):
    wt = unpack_weight(wt_words, wt_scales, "e2m1")
    wbt = np.stack([unpack_weight(wbt_words[e], wbt_scales[e], "e4m3") for e in range(E)])
    wat = np.stack([unpack_weight(wat_words[e], wat_scales[e], "e4m3") for e in range(E)])
    idx = unstriped(offs)
    dy = unpack_weight(dy_words, dy_scales, "e5m2")
    base = wt.T @ dy
    dh = f64(gate[:1]) * by_expert(wbt, dy[:, idx]) * d_silu(f64(a))
    dx = by_expert(wat, mxq(dh, 0, "e5m2"))
    c = np.zeros((K, T))
    c[:, idx] = dx
    return base + c

@@ -1,0 +1,192 @@
+from contextlib import ExitStack
+
+import concourse.mybir as mybir
+from concourse.masks import make_identity
+
+K, T, E, C, H, N = 256, 1024, 2, 512, 512, 512
+FLOPS = 2 * N * K * T + 2 * N * H * E * C + 2 * H * K * E * C
+BYTES = (N * T + N * T // 32 + N * K // 2 + N * K // 32 + E * N * H + E * N * H // 32 + E * H * K + E * H * K // 32
+         + 4 * H * E * C + 4 * E * C + 2 * 128 * (E * C // 16) + 4 * K * T)
+
+F32 = mybir.dt.float32
+BF16 = mybir.dt.bfloat16
+I32 = mybir.dt.int32
+U32 = mybir.dt.uint32
+U16 = mybir.dt.uint16
+U8 = mybir.dt.uint8
+E4M3 = mybir.dt.float8_e4m3fn_x4
+E5M2 = mybir.dt.float8_e5m2_x4
+E2M1 = mybir.dt.float4_e2m1fn_x4
+ACT = mybir.ActivationFunctionType
+ALU = mybir.AluOpType
+
+P = 128
+CH = 128
+NCH = E * C // CH
+BANK = 512
+A_LOAD = 256
+GATHERS = (128, 128, 256, 256, 256)
+
+
+def tile_moe_adb_silu_kernel(
+    tc, dy_words, dy_scales, wt_words, wt_scales, wbt_words, wbt_scales, wat_words, wat_scales, a, gate, offs, out
+):
+    nc = tc.nc
+    with ExitStack() as ctx:
+        keep = ctx.enter_context(tc.tile_pool(name="keep", bufs=1))
+        ring = ctx.enter_context(tc.tile_pool(name="ring", bufs=3))
+        psum = ctx.enter_context(tc.psum_pool(name="psum", bufs=2))
+
+        offsets = keep.tile([P, E * C // 16], U16, name="offsets")
+        dy_w = keep.tile([P, T], I32, name="dy_w", align_bytes=64)
+        dy_s = keep.tile([P, T], U8, name="dy_s", align_bytes=64)
+        wb_w = [keep.tile([P, H], I32, name="wb_w%d" % e, align_bytes=64) for e in range(E)]
+        wb_s = keep.tile([P, E, H], U8, name="wb_s", align_bytes=64)
+        wa_w = keep.tile([P, E, K], I32, name="wa_w", align_bytes=64)
+        wa_s = keep.tile([P, E, K], U8, name="wa_s", align_bytes=64)
+        wt_w = keep.tile([P, 2 * K], U8, name="wt_w", align_bytes=64)
+        wt_s = keep.tile([P, K], U8, name="wt_s", align_bytes=64)
+        a_sb = [keep.tile([P, 4, A_LOAD], F32, name="a_sb%d" % u) for u in range(E * C // A_LOAD)]
+        gate_rows = keep.tile([P, P], F32, name="gate_rows")
+        gate_cols = keep.tile([P, NCH], F32, name="gate_cols")
+        ident = keep.tile([P, P], F32, name="ident")
+        warm = keep.tile([P, 8], F32, name="warm")
+
+        nc.gpsimd.memset(dy_s[:].bitcast(I32), 0)
+        nc.vector.memset(wb_s[:].bitcast(I32), 0)
+        nc.vector.memset(warm[:], 0.0)
+        nc.scalar.activation(warm[:, 0:1], warm[:, 4:5], ACT.Silu)
+        nc.vector.memset(wa_s[:].bitcast(I32), 0)
+        nc.vector.memset(wt_s[:].bitcast(I32), 0)
+
+        def load_scales(plane, rows, queue=nc.sync):
+            for r in range(4):
+                queue.dma_start(out=plane[r:P:32].bitcast(I32), in_=rows[r].bitcast(I32))
+
+        def load_a(u):
+            nc.sync.dma_start(
+                out=a_sb[u][:], in_=a[:, u * A_LOAD : (u + 1) * A_LOAD].rearrange("(p t) j -> p t j", t=4)
+            )
+
+        def load_wb(e):
+            nc.sync.dma_start(out=wb_w[e][:], in_=wbt_words[e, 0].rearrange("p i d -> p (i d)").bitcast(I32))
+
+        nc.sync.dma_start(out=dy_w[:], in_=dy_words[0].rearrange("p t d -> p (t d)").bitcast(I32))
+        nc.sync.dma_start(offsets[:], offs)
+        load_scales(dy_s, dy_scales[0].rearrange("(q r) t -> r q t", r=4))
+        load_a(0)
+        load_wb(0)
+        nc.sync.dma_start(out=gate_rows[:], in_=gate[0 : P // NCH, :].rearrange("r (c p) -> (r c) p", p=CH))
+        load_scales(wb_s, wbt_scales.rearrange("e s (q r) i -> r q (e s) i", r=4))
+        load_a(1)
+        load_wb(1)
+        load_a(2)
+        load_a(3)
+        make_identity(nc, ident[:])
+        nc.sync.dma_start(out=wa_w[:], in_=wat_words.rearrange("e s p k d -> p (e s) (k d)").bitcast(I32))
+        load_scales(wa_s, wat_scales.rearrange("e s (q r) k -> r q (e s) k", r=4))
+        nc.sync.dma_start(out=wt_w[:].bitcast(I32), in_=wt_words[0].bitcast(I32))
+        load_scales(wt_s, wt_scales[0].rearrange("(q r) k -> r q k", r=4))
+
+        chunk_w, chunk_s = [], []
+        j0 = 0
+        for u, n in enumerate(GATHERS):
+            gw = keep.tile([P, n], U32, name="gw%d" % u, align_bytes=64)
+            gs = keep.tile([P, n], U8, name="gs%d" % u, align_bytes=64)
+            cols = offsets[:, j0 // 16 : (j0 + n) // 16]
+            nc.vector.tensor_copy(gw[:], dy_w[:].bitcast(U32).indirect(cols))
+            nc.vector.tensor_copy(gs[:], dy_s[:].indirect(cols))
+            for c in range(0, n, CH):
+                chunk_w.append(gw[:, c : c + CH])
+                chunk_s.append(gs[:, c : c + CH])
+            j0 += n
+
+
+        dh = [keep.tile([P, C, 4], BF16, name="dh%d" % e, tag="wide%d" % e, align_bytes=64) for e in range(E)]
+        dh_w = [keep.tile([P, C], U32, name="dh_w%d" % e, align_bytes=64) for e in range(E)]
+        dh_s = [keep.tile([P, C], U8, name="dh_s%d" % e, align_bytes=64) for e in range(E)]
+        window = {}
+        dx = {}
+
+        def chunk(c):
+            e, j0 = divmod(c * CH, C)
+            u, v0 = divmod(c * CH, A_LOAD)
+            v = a_sb[u][:, :, v0 : v0 + CH]
+            sums = psum.tile([P, H], F32, name="sums")
+            nc.tensor.matmul_mx(
+                out=sums[:], lhsT=chunk_w[c].bitcast(E5M2), lhsT_scale=chunk_s[c],
+                rhs=wb_w[e][:].bitcast(E4M3), rhs_scale=wb_s[:, e, :], start=True, stop=True,
+            )
+            m = keep.tile([P, 4, CH], F32, name="m%d" % c)
+            nc.scalar.activation(m[:], v, ACT.Silu, scale=-1.0)
+            if c == 0:
+                gate_t = psum.tile([P, 4, CH], F32, name="turned")
+                nc.tensor.transpose(gate_t[:, 0, :], gate_rows[:], ident[:])
+                nc.scalar.activation(gate_cols[:], gate_t[:, 0, 0:NCH], ACT.Copy, scale=-0.5)
+            gated = ring.tile([P, 4, P], F32, name="gated")
+            nc.scalar.activation(
+                gated[:], sums[:].rearrange("j (m t) -> j t m", t=4), ACT.Copy, scale=gate_cols[:, c : c + 1]
+            )
+            th = keep.tile([P, 4, CH], F32, name="th%d" % c)
+            nc.scalar.activation(th[:], v, ACT.Tanh, scale=0.5)
+            turned = psum.tile([P, 4, CH], F32, name="turned")
+            for t in range(4):
+                nc.tensor.transpose(turned[:, t, :], gated[:, t, :], ident[:])
+            x = ring.tile([P, 4, CH], F32, name="x")
+            nc.vector.scalar_tensor_tensor(x[:], m[:], -1.0, turned[:], ALU.add, ALU.mult)
+            nc.vector.scalar_tensor_tensor(
+                dh[e][:, j0 : j0 + CH, :], th[:].rearrange("p t j -> p j t"), 1.0,
+                x[:].rearrange("p t j -> p j t"), ALU.add, ALU.mult,
+            )
+
+        def quantise(e, j0, n):
+            nc.vector.quantize_mx(
+                out=dh_w[e][:, j0 : j0 + n].bitcast(E5M2), scales=dh_s[e][:, j0 : j0 + n],
+                in_=dh[e][:, j0 : j0 + n, :].rearrange("p j t -> p (j t)"),
+            )
+
+        def adapter(e):
+            c0 = e * C // CH
+            chunk(c0)
+            chunk(c0 + 1)
+            chunk(c0 + 2)
+            quantise(e, 0, 256)
+            chunk(c0 + 3)
+            quantise(e, 256, 256)
+            for kt in range(K // P):
+                acc = psum.tile([P, C], F32, name="acc")
+                nc.tensor.matmul_mx(
+                    out=acc[:], lhsT=wa_w[:, e, kt * P : (kt + 1) * P].bitcast(E4M3),
+                    lhsT_scale=wa_s[:, e, kt * P : (kt + 1) * P],
+                    rhs=dh_w[e][:].bitcast(E5M2), rhs_scale=dh_s[e][:], start=True, stop=True,
+                )
+                dx[e, kt] = keep.tile([P, C], F32, name="dx%d_%d" % (e, kt))
+                nc.scalar.copy(dx[e, kt][:], acc[:])
+
+        def scatter(e, kt):
+            if e == 0:
+                window[kt] = keep.tile([P, T], F32, name="window%d" % kt, tag="wide%d" % kt, align_bytes=64)
+            cols = offsets[:, e * C // 16 : (e + 1) * C // 16]
+            nc.vector.tensor_copy(window[kt][:].indirect(cols), dx[e, kt][:])
+
+        def finish(kt):
+            for h in range(T // BANK):
+                toks = slice(h * BANK, (h + 1) * BANK)
+                base = psum.tile([P, BANK], F32, name="base")
+                nc.tensor.matmul_mx(
+                    out=base[:], lhsT=wt_w[:, 2 * kt * P : 2 * (kt + 1) * P].bitcast(E2M1),
+                    lhsT_scale=wt_s[:, kt * P : (kt + 1) * P],
+                    rhs=dy_w[:, toks].bitcast(E5M2), rhs_scale=dy_s[:, toks], start=True, stop=True,
+                )
+                res = keep.tile([P, BANK], F32, name="res%d_%d" % (kt, h))
+                nc.vector.tensor_tensor(res[:], base[:], window[kt][:, toks], ALU.add)
+                nc.sync.dma_start(out=out[kt * P : (kt + 1) * P, toks], in_=res[:])
+
+        adapter(0)
+        scatter(0, 0)
+        adapter(1)
+        scatter(0, 1)
+        scatter(1, 0)
+        finish(0)
+        scatter(1, 1)
+        finish(1)

@@ -24,8 +24,10 @@ P = 128
 CH = 128
 NCH = E * C // CH
 BANK = 512
-A_LOAD = 256
-GATHERS = (128, 128, 256, 256, 256)
+A_LOADS = (128, 128, 256, 256, 256)
+QS = 256
+NQ = E * C // QS
+GATHERS = (("s", 0, 512), ("w", 0, 128), ("w", 128, 128), ("w", 256, 256), ("w", 512, 512), ("s", 512, 512))
 
 
 def tile_moe_adb_silu_kernel(
@@ -46,16 +48,17 @@ def tile_moe_adb_silu_kernel(
         wa_s = keep.tile([P, E, K], U8, name="wa_s", align_bytes=64)
         wt_w = keep.tile([P, 2 * K], U8, name="wt_w", align_bytes=64)
         wt_s = keep.tile([P, K], U8, name="wt_s", align_bytes=64)
-        a_sb = [keep.tile([P, 4, A_LOAD], F32, name="a_sb%d" % u) for u in range(E * C // A_LOAD)]
+        a_sb = [keep.tile([P, 4, n], F32, name="a_sb%d" % u) for u, n in enumerate(A_LOADS)]
+        a_at = [sum(A_LOADS[:u]) for u in range(len(A_LOADS))]
         gate_rows = keep.tile([P, P], F32, name="gate_rows")
-        gate_cols = keep.tile([P, NCH], F32, name="gate_cols")
         ident = keep.tile([P, P], F32, name="ident")
+        zero = keep.tile([P, 8], F32, name="zero", tag="small")
         warm = keep.tile([P, 8], F32, name="warm")
 
         nc.gpsimd.memset(dy_s[:].bitcast(I32), 0)
         nc.vector.memset(wb_s[:].bitcast(I32), 0)
-        nc.vector.memset(warm[:], 0.0)
-        nc.scalar.activation(warm[:, 0:1], warm[:, 4:5], ACT.Silu)
+        nc.vector.memset(zero[:], 0.0)
+        nc.scalar.activation(warm[:, 0:1], zero[:, 0:1], ACT.Silu)
         nc.vector.memset(wa_s[:].bitcast(I32), 0)
         nc.vector.memset(wt_s[:].bitcast(I32), 0)
 
@@ -65,23 +68,24 @@ def tile_moe_adb_silu_kernel(
 
         def load_a(u):
             nc.sync.dma_start(
-                out=a_sb[u][:], in_=a[:, u * A_LOAD : (u + 1) * A_LOAD].rearrange("(p t) j -> p t j", t=4)
+                out=a_sb[u][:], in_=a[:, a_at[u] : a_at[u] + A_LOADS[u]].rearrange("(p t) j -> p t j", t=4)
             )
 
         def load_wb(e):
             nc.sync.dma_start(out=wb_w[e][:], in_=wbt_words[e, 0].rearrange("p i d -> p (i d)").bitcast(I32))
 
-        nc.sync.dma_start(out=dy_w[:], in_=dy_words[0].rearrange("p t d -> p (t d)").bitcast(I32))
         nc.sync.dma_start(offsets[:], offs)
-        load_scales(dy_s, dy_scales[0].rearrange("(q r) t -> r q t", r=4))
         load_a(0)
+        load_scales(dy_s, dy_scales[0].rearrange("(q r) t -> r q t", r=4))
+        nc.sync.dma_start(out=dy_w[:], in_=dy_words[0].rearrange("p t d -> p (t d)").bitcast(I32))
         load_wb(0)
-        nc.sync.dma_start(out=gate_rows[:], in_=gate[0 : P // NCH, :].rearrange("r (c p) -> (r c) p", p=CH))
         load_scales(wb_s, wbt_scales.rearrange("e s (q r) i -> r q (e s) i", r=4))
+        nc.sync.dma_start(out=gate_rows[:], in_=gate[0 : P // NCH, :].rearrange("r (c p) -> (r c) p", p=CH))
         load_a(1)
-        load_wb(1)
         load_a(2)
+        load_wb(1)
         load_a(3)
+        load_a(4)
         make_identity(nc, ident[:])
         nc.sync.dma_start(out=wa_w[:], in_=wat_words.rearrange("e s p k d -> p (e s) (k d)").bitcast(I32))
         load_scales(wa_s, wat_scales.rearrange("e s (q r) k -> r q (e s) k", r=4))
@@ -89,104 +93,203 @@ def tile_moe_adb_silu_kernel(
         load_scales(wt_s, wt_scales[0].rearrange("(q r) k -> r q k", r=4))
 
         chunk_w, chunk_s = [], []
-        j0 = 0
-        for u, n in enumerate(GATHERS):
-            gw = keep.tile([P, n], U32, name="gw%d" % u, align_bytes=64)
-            gs = keep.tile([P, n], U8, name="gs%d" % u, align_bytes=64)
+
+        def gather(sort, j0, n):
             cols = offsets[:, j0 // 16 : (j0 + n) // 16]
-            nc.vector.tensor_copy(gw[:], dy_w[:].bitcast(U32).indirect(cols))
-            nc.vector.tensor_copy(gs[:], dy_s[:].indirect(cols))
-            for c in range(0, n, CH):
-                chunk_w.append(gw[:, c : c + CH])
-                chunk_s.append(gs[:, c : c + CH])
-            j0 += n
+            if sort == "w":
+                got = keep.tile([P, n], U32, name="gw%d" % j0, tag="got%d" % j0, align_bytes=64)
+                nc.vector.tensor_copy(got[:], dy_w[:].bitcast(U32).indirect(cols))
+                chunk_w.extend(got[:, c : c + CH] for c in range(0, n, CH))
+            else:
+                got = keep.tile([P, n], U8, name="gs%d" % j0, tag="got0" if j0 else "gs0", align_bytes=64)
+                nc.vector.tensor_copy(got[:], dy_s[:].indirect(cols))
+                chunk_s.extend(got[:, c : c + CH] for c in range(0, n, CH))
 
+        codes = keep.tile([P, QS + E * C], I32, name="codes", align_bytes=64)
+        planes = keep.tile([P, QS + E * C], U8, name="planes", align_bytes=64)
+        nc.gpsimd.memset(codes[:, 0:QS], 0)
+        nc.gpsimd.memset(planes[:, 0:QS].bitcast(I32), 0)
+        window = [keep.tile([P, T + 8], F32, name="window%d" % kt) for kt in range(K // P)]
+        for w in window:
+            nc.gpsimd.memset(w[:, T : T + 1], -1.0)
+        dh, dx, th, xs, ms, turned, gate_cols = {}, {}, {}, {}, {}, {}, []
 
-        dh = [keep.tile([P, C, 4], BF16, name="dh%d" % e, tag="wide%d" % e, align_bytes=64) for e in range(E)]
-        dh_w = [keep.tile([P, C], U32, name="dh_w%d" % e, align_bytes=64) for e in range(E)]
-        dh_s = [keep.tile([P, C], U8, name="dh_s%d" % e, align_bytes=64) for e in range(E)]
-        window = {}
-        dx = {}
+        def saved(c):
+            u = max(u for u, at in enumerate(a_at) if at <= c * CH)
+            v0 = c * CH - a_at[u]
+            return a_sb[u][:, :, v0 : v0 + CH].rearrange("p t (j i) -> p j t i", i=2)
 
-        def chunk(c):
-            e, j0 = divmod(c * CH, C)
-            u, v0 = divmod(c * CH, A_LOAD)
-            v = a_sb[u][:, :, v0 : v0 + CH]
+        def part(tiles, name, c, dtype, tag=None):
+            q, j0 = divmod(c * CH, QS)
+            if j0 == 0:
+                tiles[q] = keep.tile([P, QS, 4], dtype, name="%s%d" % (name, q), tag="%s%d" % (name, q), align_bytes=64)
+            return tiles[q][:, j0 : j0 + CH, :]
+
+        def silu(c):
+            ms[c] = keep.tile([P, CH, 4], F32, name="m%d" % c)
+            nc.scalar.activation(
+                ms[c][:].rearrange("p (j i) t -> p j t i", i=2), saved(c), ACT.Silu, scale=-1.0,
+                bias=zero[:, 0:1] if c == 0 else 0.0,
+            )
+
+        def tanh(c):
+            nc.scalar.activation(
+                part(th, "th", c, F32).rearrange("p (j i) t -> p j t i", i=2), saved(c), ACT.Tanh, scale=0.5,
+                bias=zero[:, 0:1] if c == 0 else 0.0,
+            )
+
+        def gates():
+            gate_t = psum.tile([P, 4, CH], F32, name="turned", bufs=3)
+            nc.tensor.transpose(gate_t[:, 0, :], gate_rows[:], ident[:])
+            gate_cols.append(keep.tile([P, NCH], F32, name="gate_cols", tag="small"))
+            nc.scalar.activation(gate_cols[0][:], gate_t[:, 0, 0:NCH], ACT.Copy, scale=-0.5)
+
+        def ahead(c):
+            e = c * CH // C
             sums = psum.tile([P, H], F32, name="sums")
             nc.tensor.matmul_mx(
                 out=sums[:], lhsT=chunk_w[c].bitcast(E5M2), lhsT_scale=chunk_s[c],
                 rhs=wb_w[e][:].bitcast(E4M3), rhs_scale=wb_s[:, e, :], start=True, stop=True,
             )
-            m = keep.tile([P, 4, CH], F32, name="m%d" % c)
-            nc.scalar.activation(m[:], v, ACT.Silu, scale=-1.0)
-            if c == 0:
-                gate_t = psum.tile([P, 4, CH], F32, name="turned")
-                nc.tensor.transpose(gate_t[:, 0, :], gate_rows[:], ident[:])
-                nc.scalar.activation(gate_cols[:], gate_t[:, 0, 0:NCH], ACT.Copy, scale=-0.5)
-            gated = ring.tile([P, 4, P], F32, name="gated")
+            gated = keep.tile([P, 4, P], F32, name="gated%d" % c)
             nc.scalar.activation(
-                gated[:], sums[:].rearrange("j (m t) -> j t m", t=4), ACT.Copy, scale=gate_cols[:, c : c + 1]
+                gated[:], sums[:].rearrange("j (m t) -> j t m", t=4), ACT.Copy, scale=gate_cols[0][:, c : c + 1]
             )
-            th = keep.tile([P, 4, CH], F32, name="th%d" % c)
-            nc.scalar.activation(th[:], v, ACT.Tanh, scale=0.5)
-            turned = psum.tile([P, 4, CH], F32, name="turned")
+            turned[c] = psum.tile([P, 4, CH], F32, name="turned", bufs=3)
             for t in range(4):
-                nc.tensor.transpose(turned[:, t, :], gated[:, t, :], ident[:])
-            x = ring.tile([P, 4, CH], F32, name="x")
-            nc.vector.scalar_tensor_tensor(x[:], m[:], -1.0, turned[:], ALU.add, ALU.mult)
+                nc.tensor.transpose(turned[c][:, t, :], gated[:, t, :], ident[:])
+
+        def front(c, pinned=False):
+            dst = part(xs, "x", c, F32)
+            src = turned[c][:].rearrange("p t j -> p j t")
+            if not pinned:
+                nc.vector.scalar_tensor_tensor(dst, ms[c][:], -1.0, src, ALU.add, ALU.mult)
+                return
+            for kt, js in ((1, slice(0, CH // 2)), (0, slice(CH // 2, CH))):
+                nc.vector.scalar_tensor_tensor(
+                    dst[:, js, :], ms[c][:, js, :], window[kt][:, T : T + 1], src[:, js, :], ALU.add, ALU.mult
+                )
+
+        def product(c):
+            q, j0 = divmod(c * CH, QS)
+            js = slice(j0, j0 + CH)
             nc.vector.scalar_tensor_tensor(
-                dh[e][:, j0 : j0 + CH, :], th[:].rearrange("p t j -> p j t"), 1.0,
-                x[:].rearrange("p t j -> p j t"), ALU.add, ALU.mult,
+                part(dh, "dh", c, BF16), th[q][:, js, :], 1.0, xs[q][:, js, :], ALU.add, ALU.mult
             )
 
-        def quantise(e, j0, n):
+        def product_on_gpsimd(q):
+            th1 = keep.tile([P, QS, 4], F32, name="th1_%d" % q, tag="dh%d" % (q - 1), align_bytes=64)
+            nc.gpsimd.tensor_scalar(th1[:], th[q][:], 1.0, 1.0, ALU.mult, ALU.add)
+            dh[q] = keep.tile([P, QS, 4], BF16, name="dh%d" % q, tag="dh%d" % q, align_bytes=64)
+            nc.gpsimd.tensor_tensor(dh[q][:], th1[:], xs[q][:], ALU.mult)
+
+        def quantise(q):
+            own = slice((q + 1) * QS, (q + 2) * QS)
             nc.vector.quantize_mx(
-                out=dh_w[e][:, j0 : j0 + n].bitcast(E5M2), scales=dh_s[e][:, j0 : j0 + n],
-                in_=dh[e][:, j0 : j0 + n, :].rearrange("p j t -> p (j t)"),
+                out=codes[:, own].bitcast(E5M2), scales=planes[:, own], in_=dh[q][:].rearrange("p j t -> p (j t)")
             )
 
-        def adapter(e):
-            c0 = e * C // CH
-            chunk(c0)
-            chunk(c0 + 1)
-            chunk(c0 + 2)
-            quantise(e, 0, 256)
-            chunk(c0 + 3)
-            quantise(e, 256, 256)
-            for kt in range(K // P):
-                acc = psum.tile([P, C], F32, name="acc")
-                nc.tensor.matmul_mx(
-                    out=acc[:], lhsT=wa_w[:, e, kt * P : (kt + 1) * P].bitcast(E4M3),
-                    lhsT_scale=wa_s[:, e, kt * P : (kt + 1) * P],
-                    rhs=dh_w[e][:].bitcast(E5M2), rhs_scale=dh_s[e][:], start=True, stop=True,
-                )
-                dx[e, kt] = keep.tile([P, C], F32, name="dx%d_%d" % (e, kt))
-                nc.scalar.copy(dx[e, kt][:], acc[:])
+        def back(q, kt, n=QS, tag=None):
+            e = q * QS // C
+            span = slice(q * QS, (q + 2) * QS)
+            acc = psum.tile([P, BANK], F32, name="acc", bufs=3)
+            nc.tensor.matmul_mx(
+                out=acc[:], lhsT=wa_w[:, e, kt * P : (kt + 1) * P].bitcast(E4M3),
+                lhsT_scale=wa_s[:, e, kt * P : (kt + 1) * P],
+                rhs=codes[:, span].bitcast(E5M2), rhs_scale=planes[:, span], start=True, stop=True,
+            )
+            name = "dx%d_%d" % (q, kt)
+            dx[q, kt] = keep.tile([P, n], F32, name=name, tag=tag or name, align_bytes=64)
+            nc.scalar.copy(dx[q, kt][:], acc[:, BANK - n : BANK])
 
-        def scatter(e, kt):
-            if e == 0:
-                window[kt] = keep.tile([P, T], F32, name="window%d" % kt, tag="wide%d" % kt, align_bytes=64)
-            cols = offsets[:, e * C // 16 : (e + 1) * C // 16]
-            nc.vector.tensor_copy(window[kt][:].indirect(cols), dx[e, kt][:])
+        def scatter(q, kt):
+            n = dx[q, kt].shape[1]
+            cols = offsets[:, ((q + 1) * QS - n) // 16 : (q + 1) * QS // 16]
+            nc.vector.tensor_copy(window[kt][:].indirect(cols), dx[q, kt][:])
 
-        def finish(kt):
-            for h in range(T // BANK):
-                toks = slice(h * BANK, (h + 1) * BANK)
-                base = psum.tile([P, BANK], F32, name="base")
-                nc.tensor.matmul_mx(
-                    out=base[:], lhsT=wt_w[:, 2 * kt * P : 2 * (kt + 1) * P].bitcast(E2M1),
-                    lhsT_scale=wt_s[:, kt * P : (kt + 1) * P],
-                    rhs=dy_w[:, toks].bitcast(E5M2), rhs_scale=dy_s[:, toks], start=True, stop=True,
-                )
+        def frozen(kt, toks):
+            base = psum.tile([P, BANK], F32, name="sums")
+            nc.tensor.matmul_mx(
+                out=base[:], lhsT=wt_w[:, 2 * kt * P : 2 * (kt + 1) * P].bitcast(E2M1),
+                lhsT_scale=wt_s[:, kt * P : (kt + 1) * P],
+                rhs=dy_w[:, toks].bitcast(E5M2), rhs_scale=dy_s[:, toks], start=True, stop=True,
+            )
+            return base
+
+        halves = [slice(h * BANK, (h + 1) * BANK) for h in range(T // BANK)]
+
+        def finish(kt, add, bases):
+            for h, toks in enumerate(halves):
                 res = keep.tile([P, BANK], F32, name="res%d_%d" % (kt, h))
-                nc.vector.tensor_tensor(res[:], base[:], window[kt][:, toks], ALU.add)
+                add(res[:], bases[h][:], window[kt][:, toks], ALU.add)
                 nc.sync.dma_start(out=out[kt * P : (kt + 1) * P, toks], in_=res[:])
 
-        adapter(0)
+        for g in GATHERS[:4]:
+            gather(*g)
+        silu(0)
+        tanh(0)
+        gates()
+        ahead(0)
+        for g in GATHERS[4:]:
+            gather(*g)
+        silu(1)
+        ahead(1)
+        tanh(1)
+        front(0)
+        front(1)
+        product(0)
+        product(1)
+        silu(2)
+        ahead(2)
+        tanh(2)
+        front(2)
+        quantise(0)
+        silu(3)
+        ahead(3)
+        tanh(3)
+        front(3)
+        product(2)
+        product(3)
+        silu(4)
+        ahead(4)
+        front(4)
+        quantise(1)
+        silu(5)
+        ahead(5)
+        tanh(4)
+        tanh(5)
+        front(5, pinned=True)
+        product_on_gpsimd(2)
+        back(0, 0)
+        back(0, 1)
         scatter(0, 0)
-        adapter(1)
         scatter(0, 1)
+        quantise(2)
+        silu(6)
+        ahead(6)
+        silu(7)
+        ahead(7)
+        tanh(6)
+        tanh(7)
+        front(6)
+        front(7, pinned=True)
+        product_on_gpsimd(3)
+        back(1, 0)
+        back(1, 1)
         scatter(1, 0)
-        finish(0)
         scatter(1, 1)
-        finish(1)
+        base0 = []
+        for h, toks in enumerate(halves):
+            held = keep.tile([P, BANK], F32, name="held%d" % h)
+            nc.scalar.copy(held[:], frozen(0, toks)[:])
+            base0.append(held)
+        base1 = [frozen(1, toks) for toks in halves]
+        quantise(3)
+        back(2, 0, tag="x3")
+        back(3, 0)
+        back(3, 1, n=2 * QS)
+        scatter(2, 0)
+        scatter(3, 0)
+        finish(0, nc.gpsimd.tensor_tensor, base0)
+        scatter(3, 1)
+        finish(1, nc.vector.tensor_tensor, base1)

@@ -36,7 +36,6 @@ def tile_moe_adb_silu_kernel(
     nc = tc.nc
     with ExitStack() as ctx:
         keep = ctx.enter_context(tc.tile_pool(name="keep", bufs=1))
-        ring = ctx.enter_context(tc.tile_pool(name="ring", bufs=3))
         psum = ctx.enter_context(tc.psum_pool(name="psum", bufs=2))
 
         offsets = keep.tile([P, E * C // 16], U16, name="offsets")
@@ -52,13 +51,13 @@ def tile_moe_adb_silu_kernel(
         a_at = [sum(A_LOADS[:u]) for u in range(len(A_LOADS))]
         gate_rows = keep.tile([P, P], F32, name="gate_rows")
         ident = keep.tile([P, P], F32, name="ident")
-        zero = keep.tile([P, 8], F32, name="zero", tag="small")
-        warm = keep.tile([P, 8], F32, name="warm")
+        zero = keep.tile([P, 1], F32, name="zero", tag="small")
+        zero_in = keep.tile([P, 1], F32, name="zero_in")
 
         nc.gpsimd.memset(dy_s[:].bitcast(I32), 0)
         nc.vector.memset(wb_s[:].bitcast(I32), 0)
-        nc.vector.memset(zero[:], 0.0)
-        nc.scalar.activation(warm[:, 0:1], zero[:, 0:1], ACT.Silu)
+        nc.vector.memset(zero_in[:], 0.0)
+        nc.scalar.activation(zero[:], zero_in[:], ACT.Silu)
         nc.vector.memset(wa_s[:].bitcast(I32), 0)
         nc.vector.memset(wt_s[:].bitcast(I32), 0)
 
@@ -117,7 +116,7 @@ def tile_moe_adb_silu_kernel(
         def saved(c):
             u = max(u for u, at in enumerate(a_at) if at <= c * CH)
             v0 = c * CH - a_at[u]
-            return a_sb[u][:, :, v0 : v0 + CH].rearrange("p t (j i) -> p j t i", i=2)
+            return a_sb[u][:, :, v0 : v0 + CH].rearrange("p t (j i) -> p j t i", i=4)
 
         def part(tiles, name, c, dtype, tag=None):
             q, j0 = divmod(c * CH, QS)
@@ -128,14 +127,14 @@ def tile_moe_adb_silu_kernel(
         def silu(c):
             ms[c] = keep.tile([P, CH, 4], F32, name="m%d" % c)
             nc.scalar.activation(
-                ms[c][:].rearrange("p (j i) t -> p j t i", i=2), saved(c), ACT.Silu, scale=-1.0,
-                bias=zero[:, 0:1] if c == 0 else 0.0,
+                ms[c][:].rearrange("p (j i) t -> p j t i", i=4), saved(c), ACT.Silu, scale=-1.0,
+                bias=zero[:] if c == 0 else 0.0,
             )
 
         def tanh(c):
             nc.scalar.activation(
-                part(th, "th", c, F32).rearrange("p (j i) t -> p j t i", i=2), saved(c), ACT.Tanh, scale=0.5,
-                bias=zero[:, 0:1] if c == 0 else 0.0,
+                part(th, "th", c, F32).rearrange("p (j i) t -> p j t i", i=4), saved(c), ACT.Tanh, scale=0.5,
+                bias=zero[:] if c == 0 else 0.0,
             )
 
         def gates():

@@ -21,13 +21,14 @@ ACT = mybir.ActivationFunctionType
 ALU = mybir.AluOpType
 
 P = 128
-CH = 128
-NCH = E * C // CH
+PACK = 4
+LIST_ROWS = 16
+CHUNK = 128
+CHUNKS = E * C // CHUNK
+QUARTER = 2 * CHUNK
 BANK = 512
-A_LOADS = (128, 128, 256, 256, 256)
-QS = 256
-NQ = E * C // QS
-GATHERS = (("s", 0, 512), ("w", 0, 128), ("w", 128, 128), ("w", 256, 256), ("w", 512, 512), ("s", 512, 512))
+RUN = 4
+A_LOADS = (CHUNK, CHUNK, QUARTER, QUARTER, QUARTER)
 
 
 def tile_moe_adb_silu_kernel(
@@ -38,7 +39,7 @@ def tile_moe_adb_silu_kernel(
         keep = ctx.enter_context(tc.tile_pool(name="keep", bufs=1))
         psum = ctx.enter_context(tc.psum_pool(name="psum", bufs=2))
 
-        offsets = keep.tile([P, E * C // 16], U16, name="offsets")
+        offsets = keep.tile([P, E * C // LIST_ROWS], U16, name="offsets")
         dy_w = keep.tile([P, T], I32, name="dy_w", align_bytes=64)
         dy_s = keep.tile([P, T], U8, name="dy_s", align_bytes=64)
         wb_w = [keep.tile([P, H], I32, name="wb_w%d" % e, align_bytes=64) for e in range(E)]
@@ -47,27 +48,27 @@ def tile_moe_adb_silu_kernel(
         wa_s = keep.tile([P, E, K], U8, name="wa_s", align_bytes=64)
         wt_w = keep.tile([P, 2 * K], U8, name="wt_w", align_bytes=64)
         wt_s = keep.tile([P, K], U8, name="wt_s", align_bytes=64)
-        a_sb = [keep.tile([P, 4, n], F32, name="a_sb%d" % u) for u, n in enumerate(A_LOADS)]
+        a_sb = [keep.tile([P, PACK, n], F32, name="a_sb%d" % u) for u, n in enumerate(A_LOADS)]
         a_at = [sum(A_LOADS[:u]) for u in range(len(A_LOADS))]
         gate_rows = keep.tile([P, P], F32, name="gate_rows")
         ident = keep.tile([P, P], F32, name="ident")
-        zero = keep.tile([P, 1], F32, name="zero", tag="small")
+        zero_bias = keep.tile([P, 1], F32, name="zero_bias", tag="small")
         zero_in = keep.tile([P, 1], F32, name="zero_in")
 
         nc.gpsimd.memset(dy_s[:].bitcast(I32), 0)
         nc.vector.memset(wb_s[:].bitcast(I32), 0)
         nc.vector.memset(zero_in[:], 0.0)
-        nc.scalar.activation(zero[:], zero_in[:], ACT.Silu)
+        nc.scalar.activation(zero_bias[:], zero_in[:], ACT.Silu)
         nc.vector.memset(wa_s[:].bitcast(I32), 0)
         nc.vector.memset(wt_s[:].bitcast(I32), 0)
 
-        def load_scales(plane, rows, queue=nc.sync):
+        def load_scales(tile, rows):
             for r in range(4):
-                queue.dma_start(out=plane[r:P:32].bitcast(I32), in_=rows[r].bitcast(I32))
+                nc.sync.dma_start(out=tile[r:P:32].bitcast(I32), in_=rows[r].bitcast(I32))
 
         def load_a(u):
             nc.sync.dma_start(
-                out=a_sb[u][:], in_=a[:, a_at[u] : a_at[u] + A_LOADS[u]].rearrange("(p t) j -> p t j", t=4)
+                out=a_sb[u][:], in_=a[:, a_at[u] : a_at[u] + A_LOADS[u]].rearrange("(p t) j -> p t j", t=PACK)
             )
 
         def load_wb(e):
@@ -79,7 +80,7 @@ def tile_moe_adb_silu_kernel(
         nc.sync.dma_start(out=dy_w[:], in_=dy_words[0].rearrange("p t d -> p (t d)").bitcast(I32))
         load_wb(0)
         load_scales(wb_s, wbt_scales.rearrange("e s (q r) i -> r q (e s) i", r=4))
-        nc.sync.dma_start(out=gate_rows[:], in_=gate[0 : P // NCH, :].rearrange("r (c p) -> (r c) p", p=CH))
+        nc.sync.dma_start(out=gate_rows[:], in_=gate[0 : P // CHUNKS, :].rearrange("r (c p) -> (r c) p", p=CHUNK))
         load_a(1)
         load_a(2)
         load_wb(1)
@@ -91,122 +92,127 @@ def tile_moe_adb_silu_kernel(
         nc.sync.dma_start(out=wt_w[:].bitcast(I32), in_=wt_words[0].bitcast(I32))
         load_scales(wt_s, wt_scales[0].rearrange("(q r) k -> r q k", r=4))
 
+        def entries(j0, n):
+            return offsets[:, j0 // LIST_ROWS : (j0 + n) // LIST_ROWS]
+
         chunk_w, chunk_s = [], []
 
-        def gather(sort, j0, n):
-            cols = offsets[:, j0 // 16 : (j0 + n) // 16]
-            if sort == "w":
-                got = keep.tile([P, n], U32, name="gw%d" % j0, tag="got%d" % j0, align_bytes=64)
-                nc.vector.tensor_copy(got[:], dy_w[:].bitcast(U32).indirect(cols))
-                chunk_w.extend(got[:, c : c + CH] for c in range(0, n, CH))
-            else:
-                got = keep.tile([P, n], U8, name="gs%d" % j0, tag="got0" if j0 else "gs0", align_bytes=64)
-                nc.vector.tensor_copy(got[:], dy_s[:].indirect(cols))
-                chunk_s.extend(got[:, c : c + CH] for c in range(0, n, CH))
+        def gather_words(j0, n):
+            got = keep.tile([P, n], U32, name="got_w%d" % j0, tag="got_w%d" % j0, align_bytes=64)
+            nc.vector.tensor_copy(got[:], dy_w[:].bitcast(U32).indirect(entries(j0, n)))
+            chunk_w.extend(got[:, c : c + CHUNK] for c in range(0, n, CHUNK))
 
-        codes = keep.tile([P, QS + E * C], I32, name="codes", align_bytes=64)
-        planes = keep.tile([P, QS + E * C], U8, name="planes", align_bytes=64)
-        nc.gpsimd.memset(codes[:, 0:QS], 0)
-        nc.gpsimd.memset(planes[:, 0:QS].bitcast(I32), 0)
-        window = [keep.tile([P, T + 8], F32, name="window%d" % kt) for kt in range(K // P)]
-        for w in window:
-            nc.gpsimd.memset(w[:, T : T + 1], -1.0)
-        dh, dx, th, xs, ms, turned, gate_cols = {}, {}, {}, {}, {}, {}, []
+        def gather_scales(j0, n, tag):
+            got = keep.tile([P, n], U8, name="got_s%d" % j0, tag=tag, align_bytes=64)
+            nc.vector.tensor_copy(got[:], dy_s[:].indirect(entries(j0, n)))
+            chunk_s.extend(got[:, c : c + CHUNK] for c in range(0, n, CHUNK))
+
+        dh_w = keep.tile([P, QUARTER + E * C], I32, name="dh_w", align_bytes=64)
+        dh_s = keep.tile([P, QUARTER + E * C], U8, name="dh_s", align_bytes=64)
+        nc.gpsimd.memset(dh_w[:, 0:QUARTER], 0)
+        nc.gpsimd.memset(dh_s[:, 0:QUARTER].bitcast(I32), 0)
+        window = [keep.tile([P, T], F32, name="window%d" % kt) for kt in range(K // P)]
+        tanhs, partial, dh = {}, {}, {}
+        silus, turned = {}, {}
+        dx = {}
 
         def saved(c):
-            u = max(u for u, at in enumerate(a_at) if at <= c * CH)
-            v0 = c * CH - a_at[u]
-            return a_sb[u][:, :, v0 : v0 + CH].rearrange("p t (j i) -> p j t i", i=4)
+            u = max(u for u, at in enumerate(a_at) if at <= c * CHUNK)
+            j0 = c * CHUNK - a_at[u]
+            return a_sb[u][:, :, j0 : j0 + CHUNK].rearrange("p t (j i) -> p j t i", i=RUN)
 
-        def part(tiles, name, c, dtype, tag=None):
-            q, j0 = divmod(c * CH, QS)
+        def chunk_of(tiles, name, c, dtype):
+            q, j0 = divmod(c * CHUNK, QUARTER)
             if j0 == 0:
-                tiles[q] = keep.tile([P, QS, 4], dtype, name="%s%d" % (name, q), tag="%s%d" % (name, q), align_bytes=64)
-            return tiles[q][:, j0 : j0 + CH, :]
+                tag = "%s%d" % (name, q)
+                tiles[q] = keep.tile([P, QUARTER, PACK], dtype, name=tag, tag=tag, align_bytes=64)
+            return tiles[q][:, j0 : j0 + CHUNK, :]
+
+        def activate(dst, c, func, scale):
+            nc.scalar.activation(
+                dst.rearrange("p (j i) t -> p j t i", i=RUN), saved(c), func, scale=scale,
+                bias=zero_bias[:] if c == 0 else 0.0,
+            )
 
         def silu(c):
-            ms[c] = keep.tile([P, CH, 4], F32, name="m%d" % c)
-            nc.scalar.activation(
-                ms[c][:].rearrange("p (j i) t -> p j t i", i=4), saved(c), ACT.Silu, scale=-1.0,
-                bias=zero[:] if c == 0 else 0.0,
-            )
+            silus[c] = keep.tile([P, CHUNK, PACK], F32, name="silu%d" % c)
+            activate(silus[c][:], c, ACT.Silu, -1.0)
 
         def tanh(c):
-            nc.scalar.activation(
-                part(th, "th", c, F32).rearrange("p (j i) t -> p j t i", i=4), saved(c), ACT.Tanh, scale=0.5,
-                bias=zero[:] if c == 0 else 0.0,
-            )
+            activate(chunk_of(tanhs, "tanh", c, F32), c, ACT.Tanh, 0.5)
 
-        def gates():
-            gate_t = psum.tile([P, 4, CH], F32, name="turned", bufs=3)
-            nc.tensor.transpose(gate_t[:, 0, :], gate_rows[:], ident[:])
-            gate_cols.append(keep.tile([P, NCH], F32, name="gate_cols", tag="small"))
-            nc.scalar.activation(gate_cols[0][:], gate_t[:, 0, 0:NCH], ACT.Copy, scale=-0.5)
+        def make_gate_cols():
+            bank = psum.tile([P, PACK, CHUNK], F32, name="turned", bufs=3)
+            nc.tensor.transpose(bank[:, 0, :], gate_rows[:], ident[:])
+            cols = keep.tile([P, CHUNKS], F32, name="gate_cols", tag="small")
+            nc.scalar.activation(cols[:], bank[:, 0, 0:CHUNKS], ACT.Copy, scale=-0.5)
+            return cols
 
-        def ahead(c):
-            e = c * CH // C
+        def first_product(c):
+            e = c * CHUNK // C
             sums = psum.tile([P, H], F32, name="sums")
             nc.tensor.matmul_mx(
                 out=sums[:], lhsT=chunk_w[c].bitcast(E5M2), lhsT_scale=chunk_s[c],
                 rhs=wb_w[e][:].bitcast(E4M3), rhs_scale=wb_s[:, e, :], start=True, stop=True,
             )
-            gated = keep.tile([P, 4, P], F32, name="gated%d" % c)
+            gated = keep.tile([P, PACK, P], F32, name="gated%d" % c)
             nc.scalar.activation(
-                gated[:], sums[:].rearrange("j (m t) -> j t m", t=4), ACT.Copy, scale=gate_cols[0][:, c : c + 1]
+                gated[:], sums[:].rearrange("j (m t) -> j t m", t=PACK), ACT.Copy, scale=gate_cols[:, c : c + 1]
             )
-            turned[c] = psum.tile([P, 4, CH], F32, name="turned", bufs=3)
-            for t in range(4):
+            turned[c] = psum.tile([P, PACK, CHUNK], F32, name="turned", bufs=3)
+            for t in range(PACK):
                 nc.tensor.transpose(turned[c][:, t, :], gated[:, t, :], ident[:])
 
-        def front(c, pinned=False):
-            dst = part(xs, "x", c, F32)
-            src = turned[c][:].rearrange("p t j -> p j t")
-            if not pinned:
-                nc.vector.scalar_tensor_tensor(dst, ms[c][:], -1.0, src, ALU.add, ALU.mult)
-                return
-            for kt, js in ((1, slice(0, CH // 2)), (0, slice(CH // 2, CH))):
-                nc.vector.scalar_tensor_tensor(
-                    dst[:, js, :], ms[c][:, js, :], window[kt][:, T : T + 1], src[:, js, :], ALU.add, ALU.mult
-                )
-
-        def product(c):
-            q, j0 = divmod(c * CH, QS)
-            js = slice(j0, j0 + CH)
+        def times_silu(c):
             nc.vector.scalar_tensor_tensor(
-                part(dh, "dh", c, BF16), th[q][:, js, :], 1.0, xs[q][:, js, :], ALU.add, ALU.mult
+                chunk_of(partial, "partial", c, F32), silus[c][:], -1.0,
+                turned[c][:].rearrange("p t j -> p j t"), ALU.add, ALU.mult,
             )
 
-        def product_on_gpsimd(q):
-            th1 = keep.tile([P, QS, 4], F32, name="th1_%d" % q, tag="dh%d" % (q - 1), align_bytes=64)
-            nc.gpsimd.tensor_scalar(th1[:], th[q][:], 1.0, 1.0, ALU.mult, ALU.add)
-            dh[q] = keep.tile([P, QS, 4], BF16, name="dh%d" % q, tag="dh%d" % q, align_bytes=64)
-            nc.gpsimd.tensor_tensor(dh[q][:], th1[:], xs[q][:], ALU.mult)
+        def times_tanh(c):
+            q, j0 = divmod(c * CHUNK, QUARTER)
+            js = slice(j0, j0 + CHUNK)
+            nc.vector.scalar_tensor_tensor(
+                chunk_of(dh, "dh", c, BF16), tanhs[q][:, js, :], 1.0, partial[q][:, js, :], ALU.add, ALU.mult
+            )
+
+        def times_tanh_on_gpsimd(q):
+            plus_one = keep.tile([P, QUARTER, PACK], F32, name="plus_one%d" % q, tag="dh%d" % (q - 1), align_bytes=64)
+            nc.gpsimd.tensor_scalar(plus_one[:], tanhs[q][:], 1.0, 1.0, ALU.mult, ALU.add)
+            dh[q] = keep.tile([P, QUARTER, PACK], BF16, name="dh%d" % q, tag="dh%d" % q, align_bytes=64)
+            for js in (slice(0, CHUNK), slice(CHUNK, QUARTER)):
+                nc.gpsimd.tensor_tensor(dh[q][:, js, :], plus_one[:, js, :], partial[q][:, js, :], ALU.mult)
 
         def quantise(q):
-            own = slice((q + 1) * QS, (q + 2) * QS)
+            own = slice((q + 1) * QUARTER, (q + 2) * QUARTER)
             nc.vector.quantize_mx(
-                out=codes[:, own].bitcast(E5M2), scales=planes[:, own], in_=dh[q][:].rearrange("p j t -> p (j t)")
+                out=dh_w[:, own].bitcast(E5M2), scales=dh_s[:, own], in_=dh[q][:].rearrange("p j t -> p (j t)")
             )
 
-        def back(q, kt, n=QS, tag=None):
-            e = q * QS // C
-            span = slice(q * QS, (q + 2) * QS)
+        def second_product(q, kt, dst):
+            e = q * QUARTER // C
+            span = slice(q * QUARTER, (q + 2) * QUARTER)
             acc = psum.tile([P, BANK], F32, name="acc", bufs=3)
             nc.tensor.matmul_mx(
                 out=acc[:], lhsT=wa_w[:, e, kt * P : (kt + 1) * P].bitcast(E4M3),
                 lhsT_scale=wa_s[:, e, kt * P : (kt + 1) * P],
-                rhs=codes[:, span].bitcast(E5M2), rhs_scale=planes[:, span], start=True, stop=True,
+                rhs=dh_w[:, span].bitcast(E5M2), rhs_scale=dh_s[:, span], start=True, stop=True,
             )
-            name = "dx%d_%d" % (q, kt)
-            dx[q, kt] = keep.tile([P, n], F32, name=name, tag=tag or name, align_bytes=64)
-            nc.scalar.copy(dx[q, kt][:], acc[:, BANK - n : BANK])
+            dx[q, kt] = dst
+            nc.scalar.copy(dst, acc[:, BANK - dst.shape[1] : BANK])
 
         def scatter(q, kt):
             n = dx[q, kt].shape[1]
-            cols = offsets[:, ((q + 1) * QS - n) // 16 : (q + 1) * QS // 16]
-            nc.vector.tensor_copy(window[kt][:].indirect(cols), dx[q, kt][:])
+            nc.vector.tensor_copy(window[kt][:].indirect(entries((q + 1) * QUARTER - n, n)), dx[q, kt])
 
-        def frozen(kt, toks):
+        def back_to_tokens(q):
+            both = keep.tile([P, K // P, QUARTER], F32, name="dx%d" % q, tag="partial%d" % (q + 1), align_bytes=64)
+            for kt in range(K // P):
+                second_product(q, kt, both[:, kt, :])
+            for kt in range(K // P):
+                scatter(q, kt)
+
+        def frozen_product(kt, toks):
             base = psum.tile([P, BANK], F32, name="sums")
             nc.tensor.matmul_mx(
                 out=base[:], lhsT=wt_w[:, 2 * kt * P : 2 * (kt + 1) * P].bitcast(E2M1),
@@ -215,80 +221,79 @@ def tile_moe_adb_silu_kernel(
             )
             return base
 
-        halves = [slice(h * BANK, (h + 1) * BANK) for h in range(T // BANK)]
+        token_halves = [slice(h * BANK, (h + 1) * BANK) for h in range(T // BANK)]
 
-        def finish(kt, add, bases):
-            for h, toks in enumerate(halves):
+        def add_and_store(kt, add, bases):
+            for h, toks in enumerate(token_halves):
                 res = keep.tile([P, BANK], F32, name="res%d_%d" % (kt, h))
                 add(res[:], bases[h][:], window[kt][:, toks], ALU.add)
                 nc.sync.dma_start(out=out[kt * P : (kt + 1) * P, toks], in_=res[:])
 
-        for g in GATHERS[:4]:
-            gather(*g)
+        gather_scales(0, C, "got_s0")
+        gather_words(0, CHUNK)
+        gather_words(CHUNK, CHUNK)
+        gather_words(QUARTER, QUARTER)
         silu(0)
         tanh(0)
-        gates()
-        ahead(0)
-        for g in GATHERS[4:]:
-            gather(*g)
+        gate_cols = make_gate_cols()
+        first_product(0)
+        gather_words(C, C)
+        gather_scales(C, C, "got_w0")
+
         silu(1)
-        ahead(1)
+        first_product(1)
         tanh(1)
-        front(0)
-        front(1)
-        product(0)
-        product(1)
+        times_silu(0)
+        times_silu(1)
+        times_tanh(0)
+        times_tanh(1)
         silu(2)
-        ahead(2)
+        first_product(2)
         tanh(2)
-        front(2)
+        times_silu(2)
         quantise(0)
         silu(3)
-        ahead(3)
+        first_product(3)
         tanh(3)
-        front(3)
-        product(2)
-        product(3)
+        times_silu(3)
+        times_tanh(2)
+        times_tanh(3)
         silu(4)
-        ahead(4)
-        front(4)
+        first_product(4)
+        times_silu(4)
         quantise(1)
+
         silu(5)
-        ahead(5)
+        first_product(5)
         tanh(4)
         tanh(5)
-        front(5, pinned=True)
-        product_on_gpsimd(2)
-        back(0, 0)
-        back(0, 1)
-        scatter(0, 0)
-        scatter(0, 1)
+        times_silu(5)
+        times_tanh_on_gpsimd(2)
+        back_to_tokens(0)
         quantise(2)
-        silu(6)
-        ahead(6)
-        silu(7)
-        ahead(7)
-        tanh(6)
-        tanh(7)
-        front(6)
-        front(7, pinned=True)
-        product_on_gpsimd(3)
-        back(1, 0)
-        back(1, 1)
-        scatter(1, 0)
-        scatter(1, 1)
-        base0 = []
-        for h, toks in enumerate(halves):
+        for c in (6, 7):
+            silu(c)
+            first_product(c)
+        for c in (6, 7):
+            tanh(c)
+        for c in (6, 7):
+            times_silu(c)
+        times_tanh_on_gpsimd(3)
+        back_to_tokens(1)
+
+        base_first = []
+        for h, toks in enumerate(token_halves):
             held = keep.tile([P, BANK], F32, name="held%d" % h)
-            nc.scalar.copy(held[:], frozen(0, toks)[:])
-            base0.append(held)
-        base1 = [frozen(1, toks) for toks in halves]
+            nc.scalar.copy(held[:], frozen_product(0, toks)[:])
+            base_first.append(held)
+        base_second = [frozen_product(1, toks) for toks in token_halves]
+
         quantise(3)
-        back(2, 0, tag="x3")
-        back(3, 0)
-        back(3, 1, n=2 * QS)
+        second_product(2, 0, keep.tile([P, QUARTER], F32, name="dx2", tag="partial3", align_bytes=64)[:])
+        second_product(3, 0, keep.tile([P, QUARTER], F32, name="dx3")[:])
+        second_product(3, 1, keep.tile([P, 2 * QUARTER], F32, name="dx23")[:])
         scatter(2, 0)
         scatter(3, 0)
-        finish(0, nc.gpsimd.tensor_tensor, base0)
+        add_and_store(0, nc.gpsimd.tensor_tensor, base_first)
         scatter(3, 1)
-        finish(1, nc.vector.tensor_tensor, base1)
+        add_and_store(1, nc.vector.tensor_tensor, base_second)

@@ -78,9 +78,9 @@ def tile_moe_adb_silu_kernel(
         load_a(0)
         load_scales(dy_s, dy_scales[0].rearrange("(q r) t -> r q t", r=4))
         nc.sync.dma_start(out=dy_w[:], in_=dy_words[0].rearrange("p t d -> p (t d)").bitcast(I32))
+        nc.sync.dma_start(out=gate_rows[:], in_=gate[0 : P // CHUNKS, :].rearrange("r (c p) -> (r c) p", p=CHUNK))
         load_wb(0)
         load_scales(wb_s, wbt_scales.rearrange("e s (q r) i -> r q (e s) i", r=4))
-        nc.sync.dma_start(out=gate_rows[:], in_=gate[0 : P // CHUNKS, :].rearrange("r (c p) -> (r c) p", p=CHUNK))
         load_a(1)
         load_a(2)
         load_wb(1)

@@ -28,7 +28,7 @@ CHUNKS = E * C // CHUNK
 QUARTER = 2 * CHUNK
 BANK = 512
 RUN = 4
-A_LOADS = (CHUNK, CHUNK, QUARTER, QUARTER, QUARTER)
+A_LOADS = (QUARTER, QUARTER, QUARTER, QUARTER)
 
 
 def tile_moe_adb_silu_kernel(
@@ -52,7 +52,7 @@ def tile_moe_adb_silu_kernel(
         a_at = [sum(A_LOADS[:u]) for u in range(len(A_LOADS))]
         gate_rows = keep.tile([P, P], F32, name="gate_rows")
         ident = keep.tile([P, P], F32, name="ident")
-        zero_bias = keep.tile([P, 1], F32, name="zero_bias", tag="small")
+        zero_bias = keep.tile([P, 1], F32, name="zero_bias", tag="small", align_bytes=64)
         zero_in = keep.tile([P, 1], F32, name="zero_in")
 
         nc.gpsimd.memset(dy_s[:].bitcast(I32), 0)
@@ -62,9 +62,9 @@ def tile_moe_adb_silu_kernel(
         nc.vector.memset(wa_s[:].bitcast(I32), 0)
         nc.vector.memset(wt_s[:].bitcast(I32), 0)
 
-        def load_scales(tile, rows):
+        def load_scales(queue, tile, rows):
             for r in range(4):
-                nc.sync.dma_start(out=tile[r:P:32].bitcast(I32), in_=rows[r].bitcast(I32))
+                queue.dma_start(out=tile[r:P:32].bitcast(I32), in_=rows[r].bitcast(I32))
 
         def load_a(u):
             nc.sync.dma_start(
@@ -74,23 +74,22 @@ def tile_moe_adb_silu_kernel(
         def load_wb(e):
             nc.sync.dma_start(out=wb_w[e][:], in_=wbt_words[e, 0].rearrange("p i d -> p (i d)").bitcast(I32))
 
+        make_identity(nc, ident[:])
         nc.sync.dma_start(offsets[:], offs)
         load_a(0)
-        load_scales(dy_s, dy_scales[0].rearrange("(q r) t -> r q t", r=4))
+        load_scales(nc.sync, dy_s, dy_scales[0].rearrange("(q r) t -> r q t", r=4))
         nc.sync.dma_start(out=dy_w[:], in_=dy_words[0].rearrange("p t d -> p (t d)").bitcast(I32))
         nc.sync.dma_start(out=gate_rows[:], in_=gate[0 : P // CHUNKS, :].rearrange("r (c p) -> (r c) p", p=CHUNK))
         load_wb(0)
-        load_scales(wb_s, wbt_scales.rearrange("e s (q r) i -> r q (e s) i", r=4))
+        load_scales(nc.sync, wb_s, wbt_scales.rearrange("e s (q r) i -> r q (e s) i", r=4))
         load_a(1)
-        load_a(2)
-        load_wb(1)
-        load_a(3)
-        load_a(4)
-        make_identity(nc, ident[:])
         nc.sync.dma_start(out=wa_w[:], in_=wat_words.rearrange("e s p k d -> p (e s) (k d)").bitcast(I32))
-        load_scales(wa_s, wat_scales.rearrange("e s (q r) k -> r q (e s) k", r=4))
+        load_scales(nc.sync, wa_s, wat_scales.rearrange("e s (q r) k -> r q (e s) k", r=4))
+        load_wb(1)
+        load_a(2)
+        load_a(3)
         nc.sync.dma_start(out=wt_w[:].bitcast(I32), in_=wt_words[0].bitcast(I32))
-        load_scales(wt_s, wt_scales[0].rearrange("(q r) k -> r q k", r=4))
+        load_scales(nc.sync, wt_s, wt_scales[0].rearrange("(q r) k -> r q k", r=4))
 
         def entries(j0, n):
             return offsets[:, j0 // LIST_ROWS : (j0 + n) // LIST_ROWS]
@@ -124,8 +123,8 @@ def tile_moe_adb_silu_kernel(
         def chunk_of(tiles, name, c, dtype):
             q, j0 = divmod(c * CHUNK, QUARTER)
             if j0 == 0:
-                tag = "%s%d" % (name, q)
-                tiles[q] = keep.tile([P, QUARTER, PACK], dtype, name=tag, tag=tag, align_bytes=64)
+                tag = "dh2" if (name, q) == ("dh", 3) else "%s%d" % (name, q)
+                tiles[q] = keep.tile([P, QUARTER, PACK], dtype, name="%s%d" % (name, q), tag=tag, align_bytes=64)
             return tiles[q][:, j0 : j0 + CHUNK, :]
 
         def activate(dst, c, func, scale):
@@ -135,16 +134,17 @@ def tile_moe_adb_silu_kernel(
             )
 
         def silu(c):
-            silus[c] = keep.tile([P, CHUNK, PACK], F32, name="silu%d" % c)
+            silus[c] = keep.tile([P, CHUNK, PACK], F32, name="silu%d" % c, tag="silu%d" % c, align_bytes=64)
             activate(silus[c][:], c, ACT.Silu, -1.0)
 
         def tanh(c):
-            activate(chunk_of(tanhs, "tanh", c, F32), c, ACT.Tanh, 0.5)
+            tanhs[c] = keep.tile([P, CHUNK, PACK], F32, name="tanh%d" % c, tag="tanh%d" % c, align_bytes=64)
+            activate(tanhs[c][:], c, ACT.Tanh, 0.5)
 
         def make_gate_cols():
             bank = psum.tile([P, PACK, CHUNK], F32, name="turned", bufs=3)
             nc.tensor.transpose(bank[:, 0, :], gate_rows[:], ident[:])
-            cols = keep.tile([P, CHUNKS], F32, name="gate_cols", tag="small")
+            cols = keep.tile([P, CHUNKS], F32, name="gate_cols")
             nc.scalar.activation(cols[:], bank[:, 0, 0:CHUNKS], ACT.Copy, scale=-0.5)
             return cols
 
@@ -155,7 +155,7 @@ def tile_moe_adb_silu_kernel(
                 out=sums[:], lhsT=chunk_w[c].bitcast(E5M2), lhsT_scale=chunk_s[c],
                 rhs=wb_w[e][:].bitcast(E4M3), rhs_scale=wb_s[:, e, :], start=True, stop=True,
             )
-            gated = keep.tile([P, PACK, P], F32, name="gated%d" % c)
+            gated = keep.tile([P, PACK, P], F32, name="gated%d" % c, tag="gated%d" % c, align_bytes=64)
             nc.scalar.activation(
                 gated[:], sums[:].rearrange("j (m t) -> j t m", t=PACK), ACT.Copy, scale=gate_cols[:, c : c + 1]
             )
@@ -173,15 +173,19 @@ def tile_moe_adb_silu_kernel(
             q, j0 = divmod(c * CHUNK, QUARTER)
             js = slice(j0, j0 + CHUNK)
             nc.vector.scalar_tensor_tensor(
-                chunk_of(dh, "dh", c, BF16), tanhs[q][:, js, :], 1.0, partial[q][:, js, :], ALU.add, ALU.mult
+                chunk_of(dh, "dh", c, BF16), tanhs[c][:], 1.0, partial[q][:, js, :], ALU.add, ALU.mult
             )
 
-        def times_tanh_on_gpsimd(q):
-            plus_one = keep.tile([P, QUARTER, PACK], F32, name="plus_one%d" % q, tag="dh%d" % (q - 1), align_bytes=64)
-            nc.gpsimd.tensor_scalar(plus_one[:], tanhs[q][:], 1.0, 1.0, ALU.mult, ALU.add)
-            dh[q] = keep.tile([P, QUARTER, PACK], BF16, name="dh%d" % q, tag="dh%d" % q, align_bytes=64)
-            for js in (slice(0, CHUNK), slice(CHUNK, QUARTER)):
-                nc.gpsimd.tensor_tensor(dh[q][:, js, :], plus_one[:, js, :], partial[q][:, js, :], ALU.mult)
+        def times_tanh_on_gpsimd(c, tag):
+            q, j0 = divmod(c * CHUNK, QUARTER)
+            plus_one = keep.tile([P, CHUNK, PACK], F32, name="plus_one%d" % c, tag=tag, align_bytes=64)
+            if q == 3:
+                nc.scalar.activation(plus_one[:], tanhs[c][:], ACT.Identity, bias=1.0)
+            else:
+                nc.gpsimd.tensor_scalar(plus_one[:], tanhs[c][:], 1.0, 1.0, ALU.mult, ALU.add)
+            nc.gpsimd.tensor_tensor(
+                chunk_of(dh, "dh", c, BF16), plus_one[:], partial[q][:, j0 : j0 + CHUNK, :], ALU.mult
+            )
 
         def quantise(q):
             own = slice((q + 1) * QUARTER, (q + 2) * QUARTER)
@@ -189,7 +193,7 @@ def tile_moe_adb_silu_kernel(
                 out=dh_w[:, own].bitcast(E5M2), scales=dh_s[:, own], in_=dh[q][:].rearrange("p j t -> p (j t)")
             )
 
-        def second_product(q, kt, dst):
+        def back(q, kt, j0, dst):
             e = q * QUARTER // C
             span = slice(q * QUARTER, (q + 2) * QUARTER)
             acc = psum.tile([P, BANK], F32, name="acc", bufs=3)
@@ -198,19 +202,13 @@ def tile_moe_adb_silu_kernel(
                 lhsT_scale=wa_s[:, e, kt * P : (kt + 1) * P],
                 rhs=dh_w[:, span].bitcast(E5M2), rhs_scale=dh_s[:, span], start=True, stop=True,
             )
-            dx[q, kt] = dst
-            nc.scalar.copy(dst, acc[:, BANK - dst.shape[1] : BANK])
+            n = dst.shape[1]
+            at = j0 - (q - 1) * QUARTER
+            nc.scalar.copy(dst, acc[:, at : at + n])
+            nc.vector.tensor_copy(window[kt][:].indirect(entries(j0, n)), dst)
 
-        def scatter(q, kt):
-            n = dx[q, kt].shape[1]
-            nc.vector.tensor_copy(window[kt][:].indirect(entries((q + 1) * QUARTER - n, n)), dx[q, kt])
-
-        def back_to_tokens(q):
-            both = keep.tile([P, K // P, QUARTER], F32, name="dx%d" % q, tag="partial%d" % (q + 1), align_bytes=64)
-            for kt in range(K // P):
-                second_product(q, kt, both[:, kt, :])
-            for kt in range(K // P):
-                scatter(q, kt)
+        def dx_tile(name, shape, tag):
+            return keep.tile([P] + shape, F32, name=name, tag=tag, align_bytes=64)
 
         def frozen_product(kt, toks):
             base = psum.tile([P, BANK], F32, name="sums")
@@ -223,11 +221,12 @@ def tile_moe_adb_silu_kernel(
 
         token_halves = [slice(h * BANK, (h + 1) * BANK) for h in range(T // BANK)]
 
-        def add_and_store(kt, add, bases):
-            for h, toks in enumerate(token_halves):
-                res = keep.tile([P, BANK], F32, name="res%d_%d" % (kt, h))
-                add(res[:], bases[h][:], window[kt][:, toks], ALU.add)
-                nc.sync.dma_start(out=out[kt * P : (kt + 1) * P, toks], in_=res[:])
+        def add_and_store(kt, add, bases, n):
+            for t0 in range(0, T, n):
+                h, at = divmod(t0, BANK)
+                res = keep.tile([P, n], F32, name="res%d_%d" % (kt, t0))
+                add(res[:], bases[h][:, at : at + n], window[kt][:, t0 : t0 + n], ALU.add)
+                nc.sync.dma_start(out=out[kt * P : (kt + 1) * P, t0 : t0 + n], in_=res[:])
 
         gather_scales(0, C, "got_s0")
         gather_words(0, CHUNK)
@@ -235,14 +234,13 @@ def tile_moe_adb_silu_kernel(
         gather_words(QUARTER, QUARTER)
         silu(0)
         tanh(0)
+        silu(1)
+        tanh(1)
         gate_cols = make_gate_cols()
         first_product(0)
         gather_words(C, C)
         gather_scales(C, C, "got_w0")
-
-        silu(1)
         first_product(1)
-        tanh(1)
         times_silu(0)
         times_silu(1)
         times_tanh(0)
@@ -252,34 +250,22 @@ def tile_moe_adb_silu_kernel(
         tanh(2)
         times_silu(2)
         quantise(0)
+        times_tanh(2)
         silu(3)
         first_product(3)
         tanh(3)
         times_silu(3)
-        times_tanh(2)
         times_tanh(3)
-        silu(4)
-        first_product(4)
-        times_silu(4)
         quantise(1)
-
-        silu(5)
-        first_product(5)
-        tanh(4)
-        tanh(5)
-        times_silu(5)
-        times_tanh_on_gpsimd(2)
-        back_to_tokens(0)
-        quantise(2)
-        for c in (6, 7):
-            silu(c)
-            first_product(c)
-        for c in (6, 7):
-            tanh(c)
-        for c in (6, 7):
-            times_silu(c)
-        times_tanh_on_gpsimd(3)
-        back_to_tokens(1)
+        for q in (2, 3):
+            for kt, c in enumerate((2 * q, 2 * q + 1)):
+                silu(c)
+                first_product(c)
+                times_silu(c)
+                tanh(c)
+                times_tanh_on_gpsimd(c, "dh1" if c == 4 else "plus_one%d" % c)
+                back(q - 2, kt, (q - 2) * QUARTER, dx_tile("dx%d" % c, [QUARTER], "gated%d" % c)[:])
+            quantise(q)
 
         base_first = []
         for h, toks in enumerate(token_halves):
@@ -287,13 +273,8 @@ def tile_moe_adb_silu_kernel(
             nc.scalar.copy(held[:], frozen_product(0, toks)[:])
             base_first.append(held)
         base_second = [frozen_product(1, toks) for toks in token_halves]
-
-        quantise(3)
-        second_product(2, 0, keep.tile([P, QUARTER], F32, name="dx2", tag="partial3", align_bytes=64)[:])
-        second_product(3, 0, keep.tile([P, QUARTER], F32, name="dx3")[:])
-        second_product(3, 1, keep.tile([P, 2 * QUARTER], F32, name="dx23")[:])
-        scatter(2, 0)
-        scatter(3, 0)
-        add_and_store(0, nc.gpsimd.tensor_tensor, base_first)
-        scatter(3, 1)
-        add_and_store(1, nc.vector.tensor_tensor, base_second)
+        back(2, 0, 2 * QUARTER, dx_tile("dx8", [QUARTER], "partial3")[:])
+        back(3, 0, 3 * QUARTER, dx_tile("dx9", [QUARTER], "dx9")[:])
+        add_and_store(0, nc.gpsimd.tensor_tensor, base_first, BANK)
+        back(3, 1, 2 * QUARTER, dx_tile("dx10", [2 * QUARTER], "dx10")[:])
+        add_and_store(1, nc.vector.tensor_tensor, base_second, BANK)

@@ -187,6 +187,21 @@ def tile_moe_adb_silu_kernel(
                 chunk_of(dh, "dh", c, BF16), plus_one[:], partial[q][:, j0 : j0 + CHUNK, :], ALU.mult
             )
 
+        factor = {}
+
+        def whole_factor(c):
+            plus_one = keep.tile([P, CHUNK, PACK], F32, name="plus_one%d" % c)
+            less_one = keep.tile([P, CHUNK, PACK], F32, name="less_one%d" % c)
+            nc.gpsimd.tensor_scalar(less_one[:], silus[c][:], 1.0, -1.0, ALU.mult, ALU.add)
+            nc.gpsimd.tensor_scalar(plus_one[:], tanhs[c][:], 1.0, 1.0, ALU.mult, ALU.add)
+            factor[c] = keep.tile([P, CHUNK, PACK], F32, name="factor%d" % c)
+            nc.gpsimd.tensor_tensor(factor[c][:], plus_one[:], less_one[:], ALU.mult)
+
+        def times_factor(c):
+            nc.vector.tensor_tensor(
+                chunk_of(dh, "dh", c, BF16), factor[c][:], turned[c][:].rearrange("p t j -> p j t"), ALU.mult
+            )
+
         def quantise(q):
             own = slice((q + 1) * QUARTER, (q + 2) * QUARTER)
             nc.vector.quantize_mx(
@@ -234,6 +249,7 @@ def tile_moe_adb_silu_kernel(
         gather_words(QUARTER, QUARTER)
         silu(0)
         tanh(0)
+        whole_factor(0)
         silu(1)
         tanh(1)
         gate_cols = make_gate_cols()
@@ -241,9 +257,9 @@ def tile_moe_adb_silu_kernel(
         gather_words(C, C)
         gather_scales(C, C, "got_w0")
         first_product(1)
-        times_silu(0)
+        times_factor(0)
+        partial[0] = keep.tile([P, QUARTER, PACK], F32, name="partial0", tag="partial0", align_bytes=64)
         times_silu(1)
-        times_tanh(0)
         times_tanh(1)
         silu(2)
         first_product(2)

@@ -28,7 +28,6 @@ CHUNKS = E * C // CHUNK
 QUARTER = 2 * CHUNK
 BANK = 512
 RUN = 4
-A_LOADS = (QUARTER, QUARTER, QUARTER, QUARTER)
 
 
 def tile_moe_adb_silu_kernel(
@@ -48,11 +47,10 @@ def tile_moe_adb_silu_kernel(
         wa_s = keep.tile([P, E, K], U8, name="wa_s", align_bytes=64)
         wt_w = keep.tile([P, 2 * K], U8, name="wt_w", align_bytes=64)
         wt_s = keep.tile([P, K], U8, name="wt_s", align_bytes=64)
-        a_sb = [keep.tile([P, PACK, n], F32, name="a_sb%d" % u) for u, n in enumerate(A_LOADS)]
-        a_at = [sum(A_LOADS[:u]) for u in range(len(A_LOADS))]
+        a_sb = [keep.tile([P, PACK, QUARTER], F32, name="a_sb%d" % q) for q in range(E * C // QUARTER)]
         gate_rows = keep.tile([P, P], F32, name="gate_rows")
         ident = keep.tile([P, P], F32, name="ident")
-        zero_bias = keep.tile([P, 1], F32, name="zero_bias", tag="small", align_bytes=64)
+        zero_bias = keep.tile([P, 1], F32, name="zero_bias", align_bytes=64)
         zero_in = keep.tile([P, 1], F32, name="zero_in")
 
         nc.gpsimd.memset(dy_s[:].bitcast(I32), 0)
@@ -62,34 +60,35 @@ def tile_moe_adb_silu_kernel(
         nc.vector.memset(wa_s[:].bitcast(I32), 0)
         nc.vector.memset(wt_s[:].bitcast(I32), 0)
 
-        def load_scales(queue, tile, rows):
+        def load_scales(tile, rows):
             for r in range(4):
-                queue.dma_start(out=tile[r:P:32].bitcast(I32), in_=rows[r].bitcast(I32))
+                nc.sync.dma_start(out=tile[r:P:32].bitcast(I32), in_=rows[r].bitcast(I32))
 
-        def load_a(u):
+        def load_a(q):
             nc.sync.dma_start(
-                out=a_sb[u][:], in_=a[:, a_at[u] : a_at[u] + A_LOADS[u]].rearrange("(p t) j -> p t j", t=PACK)
+                out=a_sb[q][:], in_=a[:, q * QUARTER : (q + 1) * QUARTER].rearrange("(p t) j -> p t j", t=PACK)
             )
 
         def load_wb(e):
             nc.sync.dma_start(out=wb_w[e][:], in_=wbt_words[e, 0].rearrange("p i d -> p (i d)").bitcast(I32))
 
         make_identity(nc, ident[:])
+
         nc.sync.dma_start(offsets[:], offs)
         load_a(0)
-        load_scales(nc.sync, dy_s, dy_scales[0].rearrange("(q r) t -> r q t", r=4))
+        load_scales(dy_s, dy_scales[0].rearrange("(q r) t -> r q t", r=4))
         nc.sync.dma_start(out=dy_w[:], in_=dy_words[0].rearrange("p t d -> p (t d)").bitcast(I32))
         nc.sync.dma_start(out=gate_rows[:], in_=gate[0 : P // CHUNKS, :].rearrange("r (c p) -> (r c) p", p=CHUNK))
         load_wb(0)
-        load_scales(nc.sync, wb_s, wbt_scales.rearrange("e s (q r) i -> r q (e s) i", r=4))
+        load_scales(wb_s, wbt_scales.rearrange("e s (q r) i -> r q (e s) i", r=4))
         load_a(1)
         nc.sync.dma_start(out=wa_w[:], in_=wat_words.rearrange("e s p k d -> p (e s) (k d)").bitcast(I32))
-        load_scales(nc.sync, wa_s, wat_scales.rearrange("e s (q r) k -> r q (e s) k", r=4))
+        load_scales(wa_s, wat_scales.rearrange("e s (q r) k -> r q (e s) k", r=4))
         load_wb(1)
         load_a(2)
         load_a(3)
         nc.sync.dma_start(out=wt_w[:].bitcast(I32), in_=wt_words[0].bitcast(I32))
-        load_scales(nc.sync, wt_s, wt_scales[0].rearrange("(q r) k -> r q k", r=4))
+        load_scales(wt_s, wt_scales[0].rearrange("(q r) k -> r q k", r=4))
 
         def entries(j0, n):
             return offsets[:, j0 // LIST_ROWS : (j0 + n) // LIST_ROWS]
@@ -111,14 +110,13 @@ def tile_moe_adb_silu_kernel(
         nc.gpsimd.memset(dh_w[:, 0:QUARTER], 0)
         nc.gpsimd.memset(dh_s[:, 0:QUARTER].bitcast(I32), 0)
         window = [keep.tile([P, T], F32, name="window%d" % kt) for kt in range(K // P)]
-        tanhs, partial, dh = {}, {}, {}
-        silus, turned = {}, {}
-        dx = {}
+        partial, dh = {}, {}
+        silus, tanhs = {}, {}
+        turned = {}
 
         def saved(c):
-            u = max(u for u, at in enumerate(a_at) if at <= c * CHUNK)
-            j0 = c * CHUNK - a_at[u]
-            return a_sb[u][:, :, j0 : j0 + CHUNK].rearrange("p t (j i) -> p j t i", i=RUN)
+            q, j0 = divmod(c * CHUNK, QUARTER)
+            return a_sb[q][:, :, j0 : j0 + CHUNK].rearrange("p t (j s) -> p j t s", s=RUN)
 
         def chunk_of(tiles, name, c, dtype):
             q, j0 = divmod(c * CHUNK, QUARTER)
@@ -129,16 +127,16 @@ def tile_moe_adb_silu_kernel(
 
         def activate(dst, c, func, scale):
             nc.scalar.activation(
-                dst.rearrange("p (j i) t -> p j t i", i=RUN), saved(c), func, scale=scale,
+                dst.rearrange("p (j s) t -> p j t s", s=RUN), saved(c), func, scale=scale,
                 bias=zero_bias[:] if c == 0 else 0.0,
             )
 
         def silu(c):
-            silus[c] = keep.tile([P, CHUNK, PACK], F32, name="silu%d" % c, tag="silu%d" % c, align_bytes=64)
+            silus[c] = keep.tile([P, CHUNK, PACK], F32, name="silu%d" % c, align_bytes=64)
             activate(silus[c][:], c, ACT.Silu, -1.0)
 
         def tanh(c):
-            tanhs[c] = keep.tile([P, CHUNK, PACK], F32, name="tanh%d" % c, tag="tanh%d" % c, align_bytes=64)
+            tanhs[c] = keep.tile([P, CHUNK, PACK], F32, name="tanh%d" % c, align_bytes=64)
             activate(tanhs[c][:], c, ACT.Tanh, 0.5)
 
         def make_gate_cols():
@@ -156,9 +154,11 @@ def tile_moe_adb_silu_kernel(
                 rhs=wb_w[e][:].bitcast(E4M3), rhs_scale=wb_s[:, e, :], start=True, stop=True,
             )
             gated = keep.tile([P, PACK, P], F32, name="gated%d" % c, tag="gated%d" % c, align_bytes=64)
-            nc.scalar.activation(
-                gated[:], sums[:].rearrange("j (m t) -> j t m", t=PACK), ACT.Copy, scale=gate_cols[:, c : c + 1]
-            )
+            sorted_sums = sums[:].rearrange("j (m t) -> j t m", t=PACK)
+            if c == 1:
+                nc.vector.tensor_scalar_mul(gated[:], sorted_sums, gate_cols[:, c : c + 1])
+            else:
+                nc.scalar.activation(gated[:], sorted_sums, ACT.Copy, scale=gate_cols[:, c : c + 1])
             turned[c] = psum.tile([P, PACK, CHUNK], F32, name="turned", bufs=3)
             for t in range(PACK):
                 nc.tensor.transpose(turned[c][:, t, :], gated[:, t, :], ident[:])
@@ -171,13 +171,13 @@ def tile_moe_adb_silu_kernel(
 
         def times_tanh(c):
             q, j0 = divmod(c * CHUNK, QUARTER)
-            js = slice(j0, j0 + CHUNK)
             nc.vector.scalar_tensor_tensor(
-                chunk_of(dh, "dh", c, BF16), tanhs[c][:], 1.0, partial[q][:, js, :], ALU.add, ALU.mult
+                chunk_of(dh, "dh", c, BF16), tanhs[c][:], 1.0, partial[q][:, j0 : j0 + CHUNK, :], ALU.add, ALU.mult
             )
 
-        def times_tanh_on_gpsimd(c, tag):
+        def times_tanh_on_gpsimd(c):
             q, j0 = divmod(c * CHUNK, QUARTER)
+            tag = "dh1" if c == 4 else "plus_one%d" % c
             plus_one = keep.tile([P, CHUNK, PACK], F32, name="plus_one%d" % c, tag=tag, align_bytes=64)
             if q == 3:
                 nc.scalar.activation(plus_one[:], tanhs[c][:], ACT.Identity, bias=1.0)
@@ -193,7 +193,10 @@ def tile_moe_adb_silu_kernel(
             plus_one = keep.tile([P, CHUNK, PACK], F32, name="plus_one%d" % c)
             less_one = keep.tile([P, CHUNK, PACK], F32, name="less_one%d" % c)
             nc.gpsimd.tensor_scalar(less_one[:], silus[c][:], 1.0, -1.0, ALU.mult, ALU.add)
-            nc.gpsimd.tensor_scalar(plus_one[:], tanhs[c][:], 1.0, 1.0, ALU.mult, ALU.add)
+            if c == 0:
+                nc.gpsimd.tensor_scalar(plus_one[:], tanhs[c][:], 1.0, 1.0, ALU.mult, ALU.add)
+            else:
+                nc.scalar.activation(plus_one[:], tanhs[c][:], ACT.Identity, bias=1.0)
             factor[c] = keep.tile([P, CHUNK, PACK], F32, name="factor%d" % c)
             nc.gpsimd.tensor_tensor(factor[c][:], plus_one[:], less_one[:], ALU.mult)
 
@@ -208,7 +211,8 @@ def tile_moe_adb_silu_kernel(
                 out=dh_w[:, own].bitcast(E5M2), scales=dh_s[:, own], in_=dh[q][:].rearrange("p j t -> p (j t)")
             )
 
-        def back(q, kt, j0, dst):
+        def back_to_tokens(q, kt, n, tag):
+            dx = keep.tile([P, n], F32, name="dx%d_%d" % (q, kt), tag=tag, align_bytes=64)
             e = q * QUARTER // C
             span = slice(q * QUARTER, (q + 2) * QUARTER)
             acc = psum.tile([P, BANK], F32, name="acc", bufs=3)
@@ -217,13 +221,8 @@ def tile_moe_adb_silu_kernel(
                 lhsT_scale=wa_s[:, e, kt * P : (kt + 1) * P],
                 rhs=dh_w[:, span].bitcast(E5M2), rhs_scale=dh_s[:, span], start=True, stop=True,
             )
-            n = dst.shape[1]
-            at = j0 - (q - 1) * QUARTER
-            nc.scalar.copy(dst, acc[:, at : at + n])
-            nc.vector.tensor_copy(window[kt][:].indirect(entries(j0, n)), dst)
-
-        def dx_tile(name, shape, tag):
-            return keep.tile([P] + shape, F32, name=name, tag=tag, align_bytes=64)
+            nc.scalar.copy(dx[:], acc[:, BANK - n : BANK])
+            nc.vector.tensor_copy(window[kt][:].indirect(entries((q + 1) * QUARTER - n, n)), dx[:])
 
         def frozen_product(kt, toks):
             base = psum.tile([P, BANK], F32, name="sums")
@@ -236,31 +235,26 @@ def tile_moe_adb_silu_kernel(
 
         token_halves = [slice(h * BANK, (h + 1) * BANK) for h in range(T // BANK)]
 
-        def add_and_store(kt, add, bases, n):
-            for t0 in range(0, T, n):
-                h, at = divmod(t0, BANK)
-                res = keep.tile([P, n], F32, name="res%d_%d" % (kt, t0))
-                add(res[:], bases[h][:, at : at + n], window[kt][:, t0 : t0 + n], ALU.add)
-                nc.sync.dma_start(out=out[kt * P : (kt + 1) * P, t0 : t0 + n], in_=res[:])
+        def add_and_store(kt, add, bases):
+            for h, toks in enumerate(token_halves):
+                res = keep.tile([P, BANK], F32, name="res%d_%d" % (kt, h))
+                add(res[:], bases[h][:], window[kt][:, toks], ALU.add)
+                nc.sync.dma_start(out=out[kt * P : (kt + 1) * P, toks], in_=res[:])
 
         gather_scales(0, C, "got_s0")
-        gather_words(0, CHUNK)
-        gather_words(CHUNK, CHUNK)
-        gather_words(QUARTER, QUARTER)
-        silu(0)
-        tanh(0)
-        whole_factor(0)
-        silu(1)
-        tanh(1)
+        gather_words(0, QUARTER)
+        gather_words(QUARTER, 3 * QUARTER)
+        for c in (0, 1):
+            silu(c)
+            tanh(c)
+            whole_factor(c)
         gate_cols = make_gate_cols()
         first_product(0)
-        gather_words(C, C)
-        gather_scales(C, C, "got_w0")
         first_product(1)
+        gather_scales(C, C, "got_w0")
         times_factor(0)
-        partial[0] = keep.tile([P, QUARTER, PACK], F32, name="partial0", tag="partial0", align_bytes=64)
-        times_silu(1)
-        times_tanh(1)
+        times_factor(1)
+
         silu(2)
         first_product(2)
         tanh(2)
@@ -273,14 +267,15 @@ def tile_moe_adb_silu_kernel(
         times_silu(3)
         times_tanh(3)
         quantise(1)
+
         for q in (2, 3):
             for kt, c in enumerate((2 * q, 2 * q + 1)):
                 silu(c)
                 first_product(c)
                 times_silu(c)
                 tanh(c)
-                times_tanh_on_gpsimd(c, "dh1" if c == 4 else "plus_one%d" % c)
-                back(q - 2, kt, (q - 2) * QUARTER, dx_tile("dx%d" % c, [QUARTER], "gated%d" % c)[:])
+                times_tanh_on_gpsimd(c)
+                back_to_tokens(q - 2, kt, QUARTER, "gated%d" % c)
             quantise(q)
 
         base_first = []
@@ -289,8 +284,9 @@ def tile_moe_adb_silu_kernel(
             nc.scalar.copy(held[:], frozen_product(0, toks)[:])
             base_first.append(held)
         base_second = [frozen_product(1, toks) for toks in token_halves]
-        back(2, 0, 2 * QUARTER, dx_tile("dx8", [QUARTER], "partial3")[:])
-        back(3, 0, 3 * QUARTER, dx_tile("dx9", [QUARTER], "dx9")[:])
-        add_and_store(0, nc.gpsimd.tensor_tensor, base_first, BANK)
-        back(3, 1, 2 * QUARTER, dx_tile("dx10", [2 * QUARTER], "dx10")[:])
-        add_and_store(1, nc.vector.tensor_tensor, base_second, BANK)
+
+        back_to_tokens(2, 0, QUARTER, "partial3")
+        back_to_tokens(3, 0, QUARTER, "dx3_0")
+        add_and_store(0, nc.gpsimd.tensor_tensor, base_first)
+        back_to_tokens(3, 1, 2 * QUARTER, "dx3_1")
+        add_and_store(1, nc.vector.tensor_tensor, base_second)

@@ -36,6 +36,7 @@ def tile_moe_adb_silu_kernel(
     nc = tc.nc
     with ExitStack() as ctx:
         keep = ctx.enter_context(tc.tile_pool(name="keep", bufs=1))
+        shared = ctx.enter_context(tc.tile_pool(name="shared", bufs=1))
         psum = ctx.enter_context(tc.psum_pool(name="psum", bufs=2))
 
         offsets = keep.tile([P, E * C // LIST_ROWS], U16, name="offsets")
@@ -44,10 +45,10 @@ def tile_moe_adb_silu_kernel(
         wb_w = [keep.tile([P, H], I32, name="wb_w%d" % e, align_bytes=64) for e in range(E)]
         wb_s = keep.tile([P, E, H], U8, name="wb_s", align_bytes=64)
         wa_w = keep.tile([P, E, K], I32, name="wa_w", align_bytes=64)
-        wa_s = keep.tile([P, E, K], U8, name="wa_s", align_bytes=64)
         wt_w = keep.tile([P, 2 * K], U8, name="wt_w", align_bytes=64)
         wt_s = keep.tile([P, K], U8, name="wt_s", align_bytes=64)
-        a_sb = [keep.tile([P, PACK, QUARTER], F32, name="a_sb%d" % q) for q in range(E * C // QUARTER)]
+        pieces = [(0, 2), (2, 2), (4, 2), (6, 2)]
+        a_sb = [keep.tile([P, PACK, n * CHUNK], F32, name="a_sb%d" % c) for c, n in pieces]
         gate_rows = keep.tile([P, P], F32, name="gate_rows")
         ident = keep.tile([P, P], F32, name="ident")
         zero_bias = keep.tile([P, 1], F32, name="zero_bias", align_bytes=64)
@@ -57,51 +58,72 @@ def tile_moe_adb_silu_kernel(
         nc.vector.memset(wb_s[:].bitcast(I32), 0)
         nc.vector.memset(zero_in[:], 0.0)
         nc.scalar.activation(zero_bias[:], zero_in[:], ACT.Silu)
-        nc.vector.memset(wa_s[:].bitcast(I32), 0)
         nc.vector.memset(wt_s[:].bitcast(I32), 0)
 
-        def load_scales(tile, rows):
+        def load_scales(tile, rows, queue=nc.sync):
             for r in range(4):
-                nc.sync.dma_start(out=tile[r:P:32].bitcast(I32), in_=rows[r].bitcast(I32))
+                queue.dma_start(out=tile[r:P:32].bitcast(I32), in_=rows[r].bitcast(I32))
 
         def load_a(q):
+            c, n = pieces[q]
             nc.sync.dma_start(
-                out=a_sb[q][:], in_=a[:, q * QUARTER : (q + 1) * QUARTER].rearrange("(p t) j -> p t j", t=PACK)
+                out=a_sb[q][:], in_=a[:, c * CHUNK : (c + n) * CHUNK].rearrange("(p t) j -> p t j", t=PACK)
             )
 
         def load_wb(e):
             nc.sync.dma_start(out=wb_w[e][:], in_=wbt_words[e, 0].rearrange("p i d -> p (i d)").bitcast(I32))
 
+        def load_gate():
+            nc.sync.dma_start(
+                out=gate_rows[:], in_=gate[0 : P // CHUNKS, :].rearrange("r (c p) -> (r c) p", p=CHUNK)
+            )
+
+        def load_dy_w():
+            nc.sync.dma_start(out=dy_w[:], in_=dy_words[0].rearrange("p t d -> p (t d)").bitcast(I32))
+
+        def load_dy_s():
+            load_scales(dy_s, dy_scales[0].rearrange("(q r) t -> r q t", r=4))
+
+        def load_wb_s():
+            load_scales(wb_s, wbt_scales.rearrange("e s (q r) i -> r q (e s) i", r=4))
+
+        def load_wa():
+            nc.sync.dma_start(out=wa_w[:], in_=wat_words.rearrange("e s p k d -> p (e s) (k d)").bitcast(I32))
+
+        def load_wt():
+            nc.sync.dma_start(out=wt_w[:].bitcast(I32), in_=wt_words[0].bitcast(I32))
+            load_scales(wt_s, wt_scales[0].rearrange("(q r) k -> r q k", r=4))
+
         make_identity(nc, ident[:])
 
         nc.sync.dma_start(offsets[:], offs)
         load_a(0)
-        load_scales(dy_s, dy_scales[0].rearrange("(q r) t -> r q t", r=4))
-        nc.sync.dma_start(out=dy_w[:], in_=dy_words[0].rearrange("p t d -> p (t d)").bitcast(I32))
-        nc.sync.dma_start(out=gate_rows[:], in_=gate[0 : P // CHUNKS, :].rearrange("r (c p) -> (r c) p", p=CHUNK))
+        load_dy_s()
+        load_dy_w()
+        load_gate()
         load_wb(0)
-        load_scales(wb_s, wbt_scales.rearrange("e s (q r) i -> r q (e s) i", r=4))
+        load_wb_s()
         load_a(1)
-        nc.sync.dma_start(out=wa_w[:], in_=wat_words.rearrange("e s p k d -> p (e s) (k d)").bitcast(I32))
-        load_scales(wa_s, wat_scales.rearrange("e s (q r) k -> r q (e s) k", r=4))
-        load_wb(1)
+        load_wa()
         load_a(2)
+        load_wb(1)
         load_a(3)
-        nc.sync.dma_start(out=wt_w[:].bitcast(I32), in_=wt_words[0].bitcast(I32))
-        load_scales(wt_s, wt_scales[0].rearrange("(q r) k -> r q k", r=4))
+        load_wt()
 
         def entries(j0, n):
             return offsets[:, j0 // LIST_ROWS : (j0 + n) // LIST_ROWS]
 
         chunk_w, chunk_s = [], []
 
-        def gather_words(j0, n):
-            got = keep.tile([P, n], U32, name="got_w%d" % j0, tag="got_w%d" % j0, align_bytes=64)
+        def gather_words(j0, n, tag):
+            if tag is None:
+                got = shared.tile([P, n], U32, name="got_w%d" % j0, offset=QB // 2, align_bytes=64)
+            else:
+                got = keep.tile([P, n], U32, name="got_w%d" % j0, tag=tag, align_bytes=64)
             nc.vector.tensor_copy(got[:], dy_w[:].bitcast(U32).indirect(entries(j0, n)))
             chunk_w.extend(got[:, c : c + CHUNK] for c in range(0, n, CHUNK))
 
-        def gather_scales(j0, n, tag):
-            got = keep.tile([P, n], U8, name="got_s%d" % j0, tag=tag, align_bytes=64)
+        def gather_scales(j0, n, got):
             nc.vector.tensor_copy(got[:], dy_s[:].indirect(entries(j0, n)))
             chunk_s.extend(got[:, c : c + CHUNK] for c in range(0, n, CHUNK))
 
@@ -110,122 +132,102 @@ def tile_moe_adb_silu_kernel(
         nc.gpsimd.memset(dh_w[:, 0:QUARTER], 0)
         nc.gpsimd.memset(dh_s[:, 0:QUARTER].bitcast(I32), 0)
         window = [keep.tile([P, T], F32, name="window%d" % kt) for kt in range(K // P)]
-        partial, dh = {}, {}
-        silus, tanhs = {}, {}
-        turned = {}
+        a_t, silus, tanhs, gated, partial, dh, packed = {}, {}, {}, {}, {}, {}, {}
 
-        def saved(c):
-            q, j0 = divmod(c * CHUNK, QUARTER)
-            return a_sb[q][:, :, j0 : j0 + CHUNK].rearrange("p t (j s) -> p j t s", s=RUN)
-
-        def chunk_of(tiles, name, c, dtype):
-            q, j0 = divmod(c * CHUNK, QUARTER)
-            if j0 == 0:
-                tag = "dh2" if (name, q) == ("dh", 3) else "%s%d" % (name, q)
-                tiles[q] = keep.tile([P, QUARTER, PACK], dtype, name="%s%d" % (name, q), tag=tag, align_bytes=64)
-            return tiles[q][:, j0 : j0 + CHUNK, :]
+        def turn_a(c):
+            q = max(i for i, piece in enumerate(pieces) if piece[0] <= c)
+            j0 = (c - pieces[q][0]) * CHUNK
+            a_t[c] = psum.tile([P, PACK, P], F32, name="a_t", tag="01340125"[c], bufs=1)
+            for t in range(PACK):
+                nc.tensor.transpose(a_t[c][:, t, :], a_sb[q][:, t, j0 : j0 + CHUNK], ident[:])
 
         def activate(dst, c, func, scale):
             nc.scalar.activation(
-                dst.rearrange("p (j s) t -> p j t s", s=RUN), saved(c), func, scale=scale,
+                dst.rearrange("j (m t) -> j m t", t=PACK), a_t[c][:].rearrange("j t m -> j m t"), func, scale=scale,
                 bias=zero_bias[:] if c == 0 else 0.0,
             )
 
-        def silu(c):
-            silus[c] = keep.tile([P, CHUNK, PACK], F32, name="silu%d" % c, align_bytes=64)
+        def silu(c, tag=None):
+            silus[c] = keep.tile([P, H], F32, name="silu%d" % c, tag=tag or "silu%d" % c, align_bytes=64)
             activate(silus[c][:], c, ACT.Silu, -1.0)
 
         def tanh(c):
-            tanhs[c] = keep.tile([P, CHUNK, PACK], F32, name="tanh%d" % c, align_bytes=64)
+            tanhs[c] = keep.tile([P, H], F32, name="tanh%d" % c, tag="tanh%d" % c, align_bytes=64)
             activate(tanhs[c][:], c, ACT.Tanh, 0.5)
 
         def make_gate_cols():
-            bank = psum.tile([P, PACK, CHUNK], F32, name="turned", bufs=3)
+            bank = psum.tile([P, 2, CHUNK], F32, name="gate_t", tag="2", bufs=1)
             nc.tensor.transpose(bank[:, 0, :], gate_rows[:], ident[:])
             cols = keep.tile([P, CHUNKS], F32, name="gate_cols")
             nc.scalar.activation(cols[:], bank[:, 0, 0:CHUNKS], ACT.Copy, scale=-0.5)
             return cols
 
-        def first_product(c):
+        def gate_step(c, tag=None):
+            g = gate_cols[:, c : c + 1]
+            gated[c] = keep.tile([P, H], F32, name="gated%d" % c, tag=tag or "gated%d" % c, align_bytes=64)
+            if tag is None:
+                nc.scalar.activation(gated[c][:], tanhs[c][:], ACT.Identity, bias=g, scale=g)
+            else:
+                nc.gpsimd.tensor_scalar(gated[c][:], tanhs[c][:], g, g, ALU.mult, ALU.add)
+
+        def times_silu(c):
             e = c * CHUNK // C
             sums = psum.tile([P, H], F32, name="sums")
             nc.tensor.matmul_mx(
                 out=sums[:], lhsT=chunk_w[c].bitcast(E5M2), lhsT_scale=chunk_s[c],
                 rhs=wb_w[e][:].bitcast(E4M3), rhs_scale=wb_s[:, e, :], start=True, stop=True,
             )
-            gated = keep.tile([P, PACK, P], F32, name="gated%d" % c, tag="gated%d" % c, align_bytes=64)
-            sorted_sums = sums[:].rearrange("j (m t) -> j t m", t=PACK)
-            if c == 1:
-                nc.vector.tensor_scalar_mul(gated[:], sorted_sums, gate_cols[:, c : c + 1])
+            partial[c] = keep.tile([P, H], F32, name="partial%d" % c, tag="partial%d" % c, align_bytes=64)
+            nc.vector.scalar_tensor_tensor(partial[c][:], silus[c][:], -1.0, sums[:], ALU.add, ALU.mult)
+
+        HELD = {2: 0, 6: 2}
+        QB = QUARTER * 2 * 4
+
+        def times_gated(c, engine):
+            if c in HELD:
+                dh[c] = shared.tile([P, H], BF16, name="dh%d" % c, offset=HELD[c] * QB, align_bytes=64)
             else:
-                nc.scalar.activation(gated[:], sorted_sums, ACT.Copy, scale=gate_cols[:, c : c + 1])
-            turned[c] = psum.tile([P, PACK, CHUNK], F32, name="turned", bufs=3)
-            for t in range(PACK):
-                nc.tensor.transpose(turned[c][:, t, :], gated[:, t, :], ident[:])
+                dh[c] = keep.tile([P, H], BF16, name="dh%d" % c, tag="gated0" if c == 1 else "dh%d" % c, align_bytes=64)
+            engine.tensor_tensor(dh[c][:], gated[c][:], partial[c][:], ALU.mult)
 
-        def times_silu(c):
-            nc.vector.scalar_tensor_tensor(
-                chunk_of(partial, "partial", c, F32), silus[c][:], -1.0,
-                turned[c][:].rearrange("p t j -> p j t"), ALU.add, ALU.mult,
-            )
-
-        def times_tanh(c):
+        def turn_dh(c):
             q, j0 = divmod(c * CHUNK, QUARTER)
-            nc.vector.scalar_tensor_tensor(
-                chunk_of(dh, "dh", c, BF16), tanhs[c][:], 1.0, partial[q][:, j0 : j0 + CHUNK, :], ALU.add, ALU.mult
-            )
-
-        def times_tanh_on_gpsimd(c):
-            q, j0 = divmod(c * CHUNK, QUARTER)
-            tag = "dh1" if c == 4 else "plus_one%d" % c
-            plus_one = keep.tile([P, CHUNK, PACK], F32, name="plus_one%d" % c, tag=tag, align_bytes=64)
-            if q == 3:
-                nc.scalar.activation(plus_one[:], tanhs[c][:], ACT.Identity, bias=1.0)
-            else:
-                nc.gpsimd.tensor_scalar(plus_one[:], tanhs[c][:], 1.0, 1.0, ALU.mult, ALU.add)
-            nc.gpsimd.tensor_tensor(
-                chunk_of(dh, "dh", c, BF16), plus_one[:], partial[q][:, j0 : j0 + CHUNK, :], ALU.mult
-            )
-
-        factor = {}
-
-        def whole_factor(c):
-            plus_one = keep.tile([P, CHUNK, PACK], F32, name="plus_one%d" % c)
-            less_one = keep.tile([P, CHUNK, PACK], F32, name="less_one%d" % c)
-            nc.gpsimd.tensor_scalar(less_one[:], silus[c][:], 1.0, -1.0, ALU.mult, ALU.add)
-            if c == 0:
-                nc.gpsimd.tensor_scalar(plus_one[:], tanhs[c][:], 1.0, 1.0, ALU.mult, ALU.add)
-            else:
-                nc.scalar.activation(plus_one[:], tanhs[c][:], ACT.Identity, bias=1.0)
-            factor[c] = keep.tile([P, CHUNK, PACK], F32, name="factor%d" % c)
-            nc.gpsimd.tensor_tensor(factor[c][:], plus_one[:], less_one[:], ALU.mult)
-
-        def times_factor(c):
-            nc.vector.tensor_tensor(
-                chunk_of(dh, "dh", c, BF16), factor[c][:], turned[c][:].rearrange("p t j -> p j t"), ALU.mult
-            )
+            bank = psum.tile([P, 2, CHUNK], F32, name="dh_t", tag="34"[c % 2], bufs=1)
+            words = dh[c][:].bitcast(F32)
+            for u in range(2):
+                nc.tensor.transpose(bank[:, u, :], words[:, u : H // 2 : 2], ident[:])
+            if j0 == 0:
+                packed[q] = shared.tile([P, QUARTER, 2], F32, name="packed%d" % q, offset=q * QB, align_bytes=64)
+            nc.scalar.copy(packed[q][:, j0 : j0 + CHUNK, :], bank[:].rearrange("p u j -> p j u"))
 
         def quantise(q):
             own = slice((q + 1) * QUARTER, (q + 2) * QUARTER)
             nc.vector.quantize_mx(
-                out=dh_w[:, own].bitcast(E5M2), scales=dh_s[:, own], in_=dh[q][:].rearrange("p j t -> p (j t)")
+                out=dh_w[:, own].bitcast(E5M2), scales=dh_s[:, own],
+                in_=packed[q][:].rearrange("p j u -> p (j u)").bitcast(BF16),
             )
 
-        def back_to_tokens(q, kt, n, tag):
-            dx = keep.tile([P, n], F32, name="dx%d_%d" % (q, kt), tag=tag, align_bytes=64)
+        def back_to_tokens(q, kt, j0, n, bank, behind=None):
+            if behind is None:
+                dx = keep.tile([P, n], F32, name="dx%d_%d" % (q, kt), align_bytes=64)
+            elif isinstance(behind, str):
+                dx = keep.tile([P, n], F32, name="dx%d_%d" % (q, kt), tag=behind, align_bytes=64)
+            else:
+                dx = shared.tile([P, n], F32, name="dx%d_%d" % (q, kt), offset=behind * QB, align_bytes=64)
             e = q * QUARTER // C
             span = slice(q * QUARTER, (q + 2) * QUARTER)
-            acc = psum.tile([P, BANK], F32, name="acc", bufs=3)
+            acc = psum.tile([P, BANK], F32, name="acc", tag=bank, bufs=1)
             nc.tensor.matmul_mx(
                 out=acc[:], lhsT=wa_w[:, e, kt * P : (kt + 1) * P].bitcast(E4M3),
                 lhsT_scale=wa_s[:, e, kt * P : (kt + 1) * P],
                 rhs=dh_w[:, span].bitcast(E5M2), rhs_scale=dh_s[:, span], start=True, stop=True,
             )
-            nc.scalar.copy(dx[:], acc[:, BANK - n : BANK])
-            nc.vector.tensor_copy(window[kt][:].indirect(entries((q + 1) * QUARTER - n, n)), dx[:])
+            first = j0 - (q - 1) * QUARTER
+            nc.scalar.copy(dx[:], acc[:, first : first + n])
+            nc.vector.tensor_copy(window[kt][:].indirect(entries(j0, n)), dx[:])
 
-        def frozen_product(kt, toks):
-            base = psum.tile([P, BANK], F32, name="sums")
+        def frozen_product(kt, toks, name):
+            base = psum.tile([P, BANK], F32, name="base", tag=name, bufs=2 if name == "sums" else 1)
             nc.tensor.matmul_mx(
                 out=base[:], lhsT=wt_w[:, 2 * kt * P : 2 * (kt + 1) * P].bitcast(E2M1),
                 lhsT_scale=wt_s[:, kt * P : (kt + 1) * P],
@@ -241,52 +243,99 @@ def tile_moe_adb_silu_kernel(
                 add(res[:], bases[h][:], window[kt][:, toks], ALU.add)
                 nc.sync.dma_start(out=out[kt * P : (kt + 1) * P, toks], in_=res[:])
 
-        gather_scales(0, C, "got_s0")
-        gather_words(0, QUARTER)
-        gather_words(QUARTER, 3 * QUARTER)
-        for c in (0, 1):
-            silu(c)
-            tanh(c)
-            whole_factor(c)
+        def load_wa_s():
+            tile = keep.tile([P, E, K], U8, name="wa_s", tag="tanh0", align_bytes=64)
+            nc.gpsimd.memset(tile[:].bitcast(I32), 0)
+            load_scales(tile, wat_scales.rearrange("e s (q r) k -> r q (e s) k", r=4), nc.scalar)
+            return tile
+
+        def held_base():
+            held = []
+            for h, toks in enumerate(token_halves):
+                held.append(keep.tile([P, BANK], F32, name="held%d" % h))
+                nc.scalar.copy(held[h][:], frozen_product(0, toks, "sums")[:])
+            return held
+
+        def clock(name, src):
+            tick = keep.tile([P, 1], F32, name=name)
+            nc.gpsimd.tensor_copy(tick[:], src)
+
+        gather_scales(0, 5 * CHUNK, keep.tile([P, 5 * CHUNK], U8, name="got_s0", align_bytes=64))
+        gather_words(0, QUARTER, "got_w0")
+        gather_words(QUARTER, C, "got_w1")
+        turn_a(0)
+        silu(0)
+        tanh(0)
+        turn_a(1)
         gate_cols = make_gate_cols()
-        first_product(0)
-        first_product(1)
-        gather_scales(C, C, "got_w0")
-        times_factor(0)
-        times_factor(1)
-
+        gate_step(0, "gated0")
+        silu(1)
+        tanh(1)
+        gate_step(1)
+        wa_s = load_wa_s()
+        times_silu(0)
+        times_gated(0, nc.gpsimd)
+        times_silu(1)
+        gather_scales(5 * CHUNK, 3 * CHUNK, keep.tile([P, 3 * CHUNK], U8, name="got_s1", tag="got_w0", align_bytes=64))
+        times_gated(1, nc.vector)
+        turn_a(2)
         silu(2)
-        first_product(2)
-        tanh(2)
         times_silu(2)
-        quantise(0)
-        times_tanh(2)
+        tanh(2)
+        gate_step(2, "partial1")
+        turn_a(3)
         silu(3)
-        first_product(3)
-        tanh(3)
         times_silu(3)
-        times_tanh(3)
+        tanh(3)
+        gate_step(3, "gated3")
+        turn_dh(0)
+        turn_a(4)
+        silu(4)
+        times_silu(4)
+        turn_dh(1)
+        quantise(0)
+        gather_words(3 * QUARTER, QUARTER, None)
+        times_gated(2, nc.gpsimd)
+        times_gated(3, nc.gpsimd)
+        turn_a(5)
+        silu(5, "gated0")
+        times_silu(5)
+        tanh(4)
+        back_to_tokens(0, 0, 0, QUARTER, "3")
+        back_to_tokens(0, 1, 0, QUARTER, "4")
+        gate_step(4)
+        times_gated(4, nc.gpsimd)
+        turn_dh(2)
+        tanh(5)
+        gate_step(5)
+        times_gated(5, nc.gpsimd)
+        turn_dh(3)
         quantise(1)
-
-        for q in (2, 3):
-            for kt, c in enumerate((2 * q, 2 * q + 1)):
-                silu(c)
-                first_product(c)
-                times_silu(c)
-                tanh(c)
-                times_tanh_on_gpsimd(c)
-                back_to_tokens(q - 2, kt, QUARTER, "gated%d" % c)
-            quantise(q)
-
-        base_first = []
-        for h, toks in enumerate(token_halves):
-            held = keep.tile([P, BANK], F32, name="held%d" % h)
-            nc.scalar.copy(held[:], frozen_product(0, toks)[:])
-            base_first.append(held)
-        base_second = [frozen_product(1, toks) for toks in token_halves]
-
-        back_to_tokens(2, 0, QUARTER, "partial3")
-        back_to_tokens(3, 0, QUARTER, "dx3_0")
+        turn_a(6)
+        silu(6)
+        times_silu(6)
+        turn_a(7)
+        silu(7)
+        times_silu(7)
+        turn_dh(4)
+        tanh(6)
+        turn_dh(5)
+        quantise(2)
+        back_to_tokens(1, 0, QUARTER, QUARTER, "0", "dh5")
+        gate_step(6)
+        times_gated(6, nc.gpsimd)
+        tanh(7)
+        back_to_tokens(1, 1, QUARTER, QUARTER, "1")
+        gate_step(7)
+        times_gated(7, nc.gpsimd)
+        back_to_tokens(2, 1, 2 * QUARTER, CHUNK, "4")
+        turn_dh(6)
+        base_first = held_base()
+        base_second = [frozen_product(1, toks, "25"[h]) for h, toks in enumerate(token_halves)]
+        turn_dh(7)
+        quantise(3)
+        back_to_tokens(2, 0, 2 * QUARTER, QUARTER, "0", "dh7")
+        back_to_tokens(3, 0, 3 * QUARTER, QUARTER, "1")
         add_and_store(0, nc.gpsimd.tensor_tensor, base_first)
-        back_to_tokens(3, 1, 2 * QUARTER, "dx3_1")
+        back_to_tokens(3, 1, 5 * CHUNK, 3 * CHUNK, "3")
         add_and_store(1, nc.vector.tensor_tensor, base_second)

@@ -141,19 +141,22 @@ def tile_moe_adb_silu_kernel(
             for t in range(PACK):
                 nc.tensor.transpose(a_t[c][:, t, :], a_sb[q][:, t, j0 : j0 + CHUNK], ident[:])
 
-        def activate(dst, c, func, scale):
-            nc.scalar.activation(
-                dst.rearrange("j (m t) -> j m t", t=PACK), a_t[c][:].rearrange("j t m -> j m t"), func, scale=scale,
-                bias=zero_bias[:] if c == 0 else 0.0,
-            )
+        def activate(dst, src, c, func, scale):
+            nc.scalar.activation(dst, src, func, scale=scale, bias=zero_bias[:] if c == 0 else 0.0)
 
         def silu(c, tag=None):
             silus[c] = keep.tile([P, H], F32, name="silu%d" % c, tag=tag or "silu%d" % c, align_bytes=64)
-            activate(silus[c][:], c, ACT.Silu, -1.0)
+            activate(
+                silus[c][:].rearrange("j (m t) -> j m t", t=PACK), a_t[c][:].rearrange("j t m -> j m t"),
+                c, ACT.Silu, -1.0,
+            )
 
         def tanh(c):
             tanhs[c] = keep.tile([P, H], F32, name="tanh%d" % c, tag="tanh%d" % c, align_bytes=64)
-            activate(tanhs[c][:], c, ACT.Tanh, 0.5)
+            activate(
+                tanhs[c][:].rearrange("j (u m e) -> j u m e", u=2, e=2),
+                a_t[c][:].rearrange("j (u e) m -> j u m e", u=2), c, ACT.Tanh, 0.5,
+            )
 
         def make_gate_cols():
             bank = psum.tile([P, 2, CHUNK], F32, name="gate_t", tag="2", bufs=1)
@@ -188,14 +191,18 @@ def tile_moe_adb_silu_kernel(
                 dh[c] = shared.tile([P, H], BF16, name="dh%d" % c, offset=HELD[c] * QB, align_bytes=64)
             else:
                 dh[c] = keep.tile([P, H], BF16, name="dh%d" % c, tag="gated0" if c == 1 else "dh%d" % c, align_bytes=64)
-            engine.tensor_tensor(dh[c][:], gated[c][:], partial[c][:], ALU.mult)
+            engine.tensor_tensor(
+                dh[c][:].rearrange("j (u m e) -> j u m e", u=2, e=2),
+                gated[c][:].rearrange("j (u m e) -> j u m e", u=2, e=2),
+                partial[c][:].rearrange("j (m u e) -> j u m e", u=2, e=2), ALU.mult,
+            )
 
         def turn_dh(c):
             q, j0 = divmod(c * CHUNK, QUARTER)
             bank = psum.tile([P, 2, CHUNK], F32, name="dh_t", tag="34"[c % 2], bufs=1)
             words = dh[c][:].bitcast(F32)
             for u in range(2):
-                nc.tensor.transpose(bank[:, u, :], words[:, u : H // 2 : 2], ident[:])
+                nc.tensor.transpose(bank[:, u, :], words[:, u * P : (u + 1) * P], ident[:])
             if j0 == 0:
                 packed[q] = shared.tile([P, QUARTER, 2], F32, name="packed%d" % q, offset=q * QB, align_bytes=64)
             nc.scalar.copy(packed[q][:, j0 : j0 + CHUNK, :], bank[:].rearrange("p u j -> p j u"))

@@ -45,6 +45,7 @@ def tile_moe_adb_silu_kernel(
         wb_w = [keep.tile([P, H], I32, name="wb_w%d" % e, align_bytes=64) for e in range(E)]
         wb_s = keep.tile([P, E, H], U8, name="wb_s", align_bytes=64)
         wa_w = keep.tile([P, E, K], I32, name="wa_w", align_bytes=64)
+        wa_s = keep.tile([P, E, K], U8, name="wa_s", align_bytes=64)
         wt_w = keep.tile([P, 2 * K], U8, name="wt_w", align_bytes=64)
         wt_s = keep.tile([P, K], U8, name="wt_s", align_bytes=64)
         pieces = [(0, 2), (2, 2), (4, 2), (6, 2)]
@@ -58,11 +59,12 @@ def tile_moe_adb_silu_kernel(
         nc.vector.memset(wb_s[:].bitcast(I32), 0)
         nc.vector.memset(zero_in[:], 0.0)
         nc.scalar.activation(zero_bias[:], zero_in[:], ACT.Silu)
+        nc.vector.memset(wa_s[:].bitcast(I32), 0)
         nc.vector.memset(wt_s[:].bitcast(I32), 0)
 
-        def load_scales(tile, rows, queue=nc.sync):
+        def load_scales(tile, rows):
             for r in range(4):
-                queue.dma_start(out=tile[r:P:32].bitcast(I32), in_=rows[r].bitcast(I32))
+                nc.sync.dma_start(out=tile[r:P:32].bitcast(I32), in_=rows[r].bitcast(I32))
 
         def load_a(q):
             c, n = pieces[q]
@@ -89,6 +91,7 @@ def tile_moe_adb_silu_kernel(
 
         def load_wa():
             nc.sync.dma_start(out=wa_w[:], in_=wat_words.rearrange("e s p k d -> p (e s) (k d)").bitcast(I32))
+            load_scales(wa_s, wat_scales.rearrange("e s (q r) k -> r q (e s) k", r=4))
 
         def load_wt():
             nc.sync.dma_start(out=wt_w[:].bitcast(I32), in_=wt_words[0].bitcast(I32))
@@ -104,9 +107,9 @@ def tile_moe_adb_silu_kernel(
         load_wb(0)
         load_wb_s()
         load_a(1)
-        load_wa()
         load_a(2)
         load_wb(1)
+        load_wa()
         load_a(3)
         load_wt()
 
@@ -152,7 +155,7 @@ def tile_moe_adb_silu_kernel(
             )
 
         def tanh(c):
-            tanhs[c] = keep.tile([P, H], F32, name="tanh%d" % c, tag="tanh%d" % c, align_bytes=64)
+            tanhs[c] = keep.tile([P, H], F32, name="tanh%d" % c, align_bytes=64)
             activate(
                 tanhs[c][:].rearrange("j (u m e) -> j u m e", u=2, e=2),
                 a_t[c][:].rearrange("j (u e) m -> j u m e", u=2), c, ACT.Tanh, 0.5,
@@ -250,12 +253,6 @@ def tile_moe_adb_silu_kernel(
                 add(res[:], bases[h][:], window[kt][:, toks], ALU.add)
                 nc.sync.dma_start(out=out[kt * P : (kt + 1) * P, toks], in_=res[:])
 
-        def load_wa_s():
-            tile = keep.tile([P, E, K], U8, name="wa_s", tag="tanh0", align_bytes=64)
-            nc.gpsimd.memset(tile[:].bitcast(I32), 0)
-            load_scales(tile, wat_scales.rearrange("e s (q r) k -> r q (e s) k", r=4), nc.scalar)
-            return tile
-
         def held_base():
             held = []
             for h, toks in enumerate(token_halves):
@@ -279,7 +276,6 @@ def tile_moe_adb_silu_kernel(
         silu(1)
         tanh(1)
         gate_step(1)
-        wa_s = load_wa_s()
         times_silu(0)
         times_gated(0, nc.gpsimd)
         times_silu(1)

@@ -27,7 +27,12 @@ CHUNK = 128
 CHUNKS = E * C // CHUNK
 QUARTER = 2 * CHUNK
 BANK = 512
-RUN = 4
+QUARTERS = E * C // QUARTER
+QUARTER_BYTES = QUARTER * PACK * 2
+
+SPARE = ("spare0", "spare1", "spare2", "spare3")
+DH_BANK = ("dh_even", "dh_odd")
+A_BANK = (SPARE[0], SPARE[1], DH_BANK[0], DH_BANK[1], SPARE[0], SPARE[1], SPARE[2], SPARE[3])
 
 
 def tile_moe_adb_silu_kernel(
@@ -36,7 +41,7 @@ def tile_moe_adb_silu_kernel(
     nc = tc.nc
     with ExitStack() as ctx:
         keep = ctx.enter_context(tc.tile_pool(name="keep", bufs=1))
-        shared = ctx.enter_context(tc.tile_pool(name="shared", bufs=1))
+        reused = ctx.enter_context(tc.tile_pool(name="reused", bufs=1))
         psum = ctx.enter_context(tc.psum_pool(name="psum", bufs=2))
 
         offsets = keep.tile([P, E * C // LIST_ROWS], U16, name="offsets")
@@ -48,14 +53,14 @@ def tile_moe_adb_silu_kernel(
         wa_s = keep.tile([P, E, K], U8, name="wa_s", align_bytes=64)
         wt_w = keep.tile([P, 2 * K], U8, name="wt_w", align_bytes=64)
         wt_s = keep.tile([P, K], U8, name="wt_s", align_bytes=64)
-        pieces = [(0, 2), (2, 2), (4, 2), (6, 2)]
-        a_sb = [keep.tile([P, PACK, n * CHUNK], F32, name="a_sb%d" % c) for c, n in pieces]
+        a_sb = [keep.tile([P, PACK, QUARTER], F32, name="a_sb%d" % q) for q in range(QUARTERS)]
         gate_rows = keep.tile([P, P], F32, name="gate_rows")
         ident = keep.tile([P, P], F32, name="ident")
         zero_bias = keep.tile([P, 1], F32, name="zero_bias", align_bytes=64)
         zero_in = keep.tile([P, 1], F32, name="zero_in")
 
         nc.gpsimd.memset(dy_s[:].bitcast(I32), 0)
+        nc.vector.memset(gate_rows[:], 0.0)
         nc.vector.memset(wb_s[:].bitcast(I32), 0)
         nc.vector.memset(zero_in[:], 0.0)
         nc.scalar.activation(zero_bias[:], zero_in[:], ACT.Silu)
@@ -67,80 +72,55 @@ def tile_moe_adb_silu_kernel(
                 nc.sync.dma_start(out=tile[r:P:32].bitcast(I32), in_=rows[r].bitcast(I32))
 
         def load_a(q):
-            c, n = pieces[q]
             nc.sync.dma_start(
-                out=a_sb[q][:], in_=a[:, c * CHUNK : (c + n) * CHUNK].rearrange("(p t) j -> p t j", t=PACK)
+                out=a_sb[q][:], in_=a[:, q * QUARTER : (q + 1) * QUARTER].rearrange("(m t) j -> m t j", t=PACK)
             )
 
         def load_wb(e):
             nc.sync.dma_start(out=wb_w[e][:], in_=wbt_words[e, 0].rearrange("p i d -> p (i d)").bitcast(I32))
 
-        def load_gate():
-            nc.sync.dma_start(
-                out=gate_rows[:], in_=gate[0 : P // CHUNKS, :].rearrange("r (c p) -> (r c) p", p=CHUNK)
-            )
-
-        def load_dy_w():
-            nc.sync.dma_start(out=dy_w[:], in_=dy_words[0].rearrange("p t d -> p (t d)").bitcast(I32))
-
-        def load_dy_s():
-            load_scales(dy_s, dy_scales[0].rearrange("(q r) t -> r q t", r=4))
-
-        def load_wb_s():
-            load_scales(wb_s, wbt_scales.rearrange("e s (q r) i -> r q (e s) i", r=4))
-
-        def load_wa():
-            nc.sync.dma_start(out=wa_w[:], in_=wat_words.rearrange("e s p k d -> p (e s) (k d)").bitcast(I32))
-            load_scales(wa_s, wat_scales.rearrange("e s (q r) k -> r q (e s) k", r=4))
-
-        def load_wt():
-            nc.sync.dma_start(out=wt_w[:].bitcast(I32), in_=wt_words[0].bitcast(I32))
-            load_scales(wt_s, wt_scales[0].rearrange("(q r) k -> r q k", r=4))
-
         make_identity(nc, ident[:])
 
         nc.sync.dma_start(offsets[:], offs)
         load_a(0)
-        load_dy_s()
-        load_dy_w()
-        load_gate()
-        load_wb(0)
-        load_wb_s()
+        load_scales(dy_s, dy_scales[0].rearrange("(s r) t -> r s t", r=4))
+        nc.sync.dma_start(out=dy_w[:], in_=dy_words[0].rearrange("p t d -> p (t d)").bitcast(I32))
+        nc.sync.dma_start(out=gate_rows[0:CHUNKS, :], in_=gate[0, :].rearrange("(c p) -> c p", p=CHUNK))
         load_a(1)
+        load_wb(0)
+        load_scales(wb_s, wbt_scales.rearrange("e g (s r) i -> r s (e g) i", r=4))
         load_a(2)
         load_wb(1)
-        load_wa()
+        nc.sync.dma_start(out=wa_w[:], in_=wat_words.rearrange("e g p k d -> p (e g) (k d)").bitcast(I32))
+        load_scales(wa_s, wat_scales.rearrange("e g (s r) k -> r s (e g) k", r=4))
         load_a(3)
-        load_wt()
+        nc.sync.dma_start(out=wt_w[:].bitcast(I32), in_=wt_words[0].bitcast(I32))
+        load_scales(wt_s, wt_scales[0].rearrange("(s r) k -> r s k", r=4))
 
         def entries(j0, n):
             return offsets[:, j0 // LIST_ROWS : (j0 + n) // LIST_ROWS]
 
         chunk_w, chunk_s = [], []
 
-        def gather_words(j0, n, tag):
-            if tag is None:
-                got = shared.tile([P, n], U32, name="got_w%d" % j0, offset=QB // 2, align_bytes=64)
-            else:
-                got = keep.tile([P, n], U32, name="got_w%d" % j0, tag=tag, align_bytes=64)
-            nc.vector.tensor_copy(got[:], dy_w[:].bitcast(U32).indirect(entries(j0, n)))
-            chunk_w.extend(got[:, c : c + CHUNK] for c in range(0, n, CHUNK))
-
-        def gather_scales(j0, n, got):
-            nc.vector.tensor_copy(got[:], dy_s[:].indirect(entries(j0, n)))
-            chunk_s.extend(got[:, c : c + CHUNK] for c in range(0, n, CHUNK))
+        def gather(table, got, by_chunk):
+            n = got.shape[1]
+            nc.vector.tensor_copy(got[:], table.indirect(entries(len(by_chunk) * CHUNK, n)))
+            by_chunk.extend(got[:, j : j + CHUNK] for j in range(0, n, CHUNK))
 
         dh_w = keep.tile([P, QUARTER + E * C], I32, name="dh_w", align_bytes=64)
         dh_s = keep.tile([P, QUARTER + E * C], U8, name="dh_s", align_bytes=64)
         nc.gpsimd.memset(dh_w[:, 0:QUARTER], 0)
         nc.gpsimd.memset(dh_s[:, 0:QUARTER].bitcast(I32), 0)
         window = [keep.tile([P, T], F32, name="window%d" % kt) for kt in range(K // P)]
-        a_t, silus, tanhs, gated, partial, dh, packed = {}, {}, {}, {}, {}, {}, {}
+        a_t, silus, tanhs, gated, partial, dh = {}, {}, {}, {}, {}, {}
+        grouped = {}
+
+        def chunk_tile(name, c, dtype, tag=None):
+            return keep.tile([P, H], dtype, name="%s%d" % (name, c), tag=tag or "%s%d" % (name, c), align_bytes=64)
 
         def turn_a(c):
-            q = max(i for i, piece in enumerate(pieces) if piece[0] <= c)
-            j0 = (c - pieces[q][0]) * CHUNK
-            a_t[c] = psum.tile([P, PACK, P], F32, name="a_t", tag="01340125"[c], bufs=1)
+            q, j0 = divmod(c * CHUNK, QUARTER)
+            a_t[c] = psum.tile([P, PACK, P], F32, name="a_t", tag=A_BANK[c], bufs=1)
             for t in range(PACK):
                 nc.tensor.transpose(a_t[c][:, t, :], a_sb[q][:, t, j0 : j0 + CHUNK], ident[:])
 
@@ -148,33 +128,35 @@ def tile_moe_adb_silu_kernel(
             nc.scalar.activation(dst, src, func, scale=scale, bias=zero_bias[:] if c == 0 else 0.0)
 
         def silu(c, tag=None):
-            silus[c] = keep.tile([P, H], F32, name="silu%d" % c, tag=tag or "silu%d" % c, align_bytes=64)
+            silus[c] = chunk_tile("silu", c, F32, tag)
             activate(
                 silus[c][:].rearrange("j (m t) -> j m t", t=PACK), a_t[c][:].rearrange("j t m -> j m t"),
                 c, ACT.Silu, -1.0,
             )
 
+        def by_pair(tile):
+            return tile[:].rearrange("j (u m o) -> j u m o", u=2, o=2)
+
         def tanh(c):
-            tanhs[c] = keep.tile([P, H], F32, name="tanh%d" % c, align_bytes=64)
-            activate(
-                tanhs[c][:].rearrange("j (u m e) -> j u m e", u=2, e=2),
-                a_t[c][:].rearrange("j (u e) m -> j u m e", u=2), c, ACT.Tanh, 0.5,
-            )
+            tanhs[c] = chunk_tile("tanh", c, F32)
+            activate(by_pair(tanhs[c]), a_t[c][:].rearrange("j (u o) m -> j u m o", u=2), c, ACT.Tanh, 0.5)
 
         def make_gate_cols():
-            bank = psum.tile([P, 2, CHUNK], F32, name="gate_t", tag="2", bufs=1)
+            bank = psum.tile([P, 2, CHUNK], F32, name="gate_t", tag=SPARE[2], bufs=1)
             nc.tensor.transpose(bank[:, 0, :], gate_rows[:], ident[:])
             cols = keep.tile([P, CHUNKS], F32, name="gate_cols")
             nc.scalar.activation(cols[:], bank[:, 0, 0:CHUNKS], ACT.Copy, scale=-0.5)
             return cols
 
-        def gate_step(c, tag=None):
+        def gate_on_scalar(c):
             g = gate_cols[:, c : c + 1]
-            gated[c] = keep.tile([P, H], F32, name="gated%d" % c, tag=tag or "gated%d" % c, align_bytes=64)
-            if tag is None:
-                nc.scalar.activation(gated[c][:], tanhs[c][:], ACT.Identity, bias=g, scale=g)
-            else:
-                nc.gpsimd.tensor_scalar(gated[c][:], tanhs[c][:], g, g, ALU.mult, ALU.add)
+            gated[c] = chunk_tile("gated", c, F32)
+            nc.scalar.activation(gated[c][:], tanhs[c][:], ACT.Identity, bias=g, scale=g)
+
+        def gate_on_gpsimd(c, tag=None):
+            g = gate_cols[:, c : c + 1]
+            gated[c] = chunk_tile("gated", c, F32, tag)
+            nc.gpsimd.tensor_scalar(gated[c][:], tanhs[c][:], g, g, ALU.mult, ALU.add)
 
         def times_silu(c):
             e = c * CHUNK // C
@@ -183,47 +165,40 @@ def tile_moe_adb_silu_kernel(
                 out=sums[:], lhsT=chunk_w[c].bitcast(E5M2), lhsT_scale=chunk_s[c],
                 rhs=wb_w[e][:].bitcast(E4M3), rhs_scale=wb_s[:, e, :], start=True, stop=True,
             )
-            partial[c] = keep.tile([P, H], F32, name="partial%d" % c, tag="partial%d" % c, align_bytes=64)
+            partial[c] = chunk_tile("partial", c, F32)
             nc.vector.scalar_tensor_tensor(partial[c][:], silus[c][:], -1.0, sums[:], ALU.add, ALU.mult)
 
-        HELD = {2: 0, 6: 2}
-        QB = QUARTER * 2 * 4
-
-        def times_gated(c, engine):
-            if c in HELD:
-                dh[c] = shared.tile([P, H], BF16, name="dh%d" % c, offset=HELD[c] * QB, align_bytes=64)
-            else:
-                dh[c] = keep.tile([P, H], BF16, name="dh%d" % c, tag="gated0" if c == 1 else "dh%d" % c, align_bytes=64)
+        def times_gated(c, engine, dst):
+            dh[c] = dst
             engine.tensor_tensor(
-                dh[c][:].rearrange("j (u m e) -> j u m e", u=2, e=2),
-                gated[c][:].rearrange("j (u m e) -> j u m e", u=2, e=2),
-                partial[c][:].rearrange("j (m u e) -> j u m e", u=2, e=2), ALU.mult,
+                by_pair(dst), by_pair(gated[c]), partial[c][:].rearrange("j (m u o) -> j u m o", u=2, o=2), ALU.mult
             )
+
+        def dh_behind_quantise(c, q):
+            return reused.tile([P, H], BF16, name="dh%d" % c, offset=q * QUARTER_BYTES, align_bytes=64)
 
         def turn_dh(c):
             q, j0 = divmod(c * CHUNK, QUARTER)
-            bank = psum.tile([P, 2, CHUNK], F32, name="dh_t", tag="34"[c % 2], bufs=1)
-            words = dh[c][:].bitcast(F32)
+            bank = psum.tile([P, 2, CHUNK], F32, name="dh_t", tag=DH_BANK[c % 2], bufs=1)
+            pairs = dh[c][:].bitcast(F32)
             for u in range(2):
-                nc.tensor.transpose(bank[:, u, :], words[:, u * P : (u + 1) * P], ident[:])
+                nc.tensor.transpose(bank[:, u, :], pairs[:, u * P : (u + 1) * P], ident[:])
             if j0 == 0:
-                packed[q] = shared.tile([P, QUARTER, 2], F32, name="packed%d" % q, offset=q * QB, align_bytes=64)
-            nc.scalar.copy(packed[q][:, j0 : j0 + CHUNK, :], bank[:].rearrange("p u j -> p j u"))
+                grouped[q] = reused.tile(
+                    [P, QUARTER, 2], F32, name="grouped%d" % q, offset=q * QUARTER_BYTES, align_bytes=64
+                )
+            nc.scalar.copy(grouped[q][:, j0 : j0 + CHUNK, :], bank[:].rearrange("m u j -> m j u"))
 
         def quantise(q):
             own = slice((q + 1) * QUARTER, (q + 2) * QUARTER)
             nc.vector.quantize_mx(
                 out=dh_w[:, own].bitcast(E5M2), scales=dh_s[:, own],
-                in_=packed[q][:].rearrange("p j u -> p (j u)").bitcast(BF16),
+                in_=grouped[q][:].rearrange("m j u -> m (j u)").bitcast(BF16),
             )
 
-        def back_to_tokens(q, kt, j0, n, bank, behind=None):
-            if behind is None:
-                dx = keep.tile([P, n], F32, name="dx%d_%d" % (q, kt), align_bytes=64)
-            elif isinstance(behind, str):
-                dx = keep.tile([P, n], F32, name="dx%d_%d" % (q, kt), tag=behind, align_bytes=64)
-            else:
-                dx = shared.tile([P, n], F32, name="dx%d_%d" % (q, kt), offset=behind * QB, align_bytes=64)
+        def back_to_tokens(q, kt, j0, n, bank, tag=None):
+            name = "dx%d_%d" % (q, kt)
+            dx = keep.tile([P, n], F32, name=name, tag=tag or name, align_bytes=64)
             e = q * QUARTER // C
             span = slice(q * QUARTER, (q + 2) * QUARTER)
             acc = psum.tile([P, BANK], F32, name="acc", tag=bank, bufs=1)
@@ -236,14 +211,12 @@ def tile_moe_adb_silu_kernel(
             nc.scalar.copy(dx[:], acc[:, first : first + n])
             nc.vector.tensor_copy(window[kt][:].indirect(entries(j0, n)), dx[:])
 
-        def frozen_product(kt, toks, name):
-            base = psum.tile([P, BANK], F32, name="base", tag=name, bufs=2 if name == "sums" else 1)
+        def frozen_product(base, kt, toks):
             nc.tensor.matmul_mx(
                 out=base[:], lhsT=wt_w[:, 2 * kt * P : 2 * (kt + 1) * P].bitcast(E2M1),
                 lhsT_scale=wt_s[:, kt * P : (kt + 1) * P],
                 rhs=dy_w[:, toks].bitcast(E5M2), rhs_scale=dy_s[:, toks], start=True, stop=True,
             )
-            return base
 
         token_halves = [slice(h * BANK, (h + 1) * BANK) for h in range(T // BANK)]
 
@@ -253,92 +226,91 @@ def tile_moe_adb_silu_kernel(
                 add(res[:], bases[h][:], window[kt][:, toks], ALU.add)
                 nc.sync.dma_start(out=out[kt * P : (kt + 1) * P, toks], in_=res[:])
 
-        def held_base():
-            held = []
-            for h, toks in enumerate(token_halves):
-                held.append(keep.tile([P, BANK], F32, name="held%d" % h))
-                nc.scalar.copy(held[h][:], frozen_product(0, toks, "sums")[:])
-            return held
+        def start_chunk(c, tag=None):
+            turn_a(c)
+            silu(c, tag)
+            times_silu(c)
 
-        def clock(name, src):
-            tick = keep.tile([P, 1], F32, name=name)
-            nc.gpsimd.tensor_copy(tick[:], src)
+        words, scale_bytes = dy_w[:].bitcast(U32), dy_s[:]
+        gather(scale_bytes, keep.tile([P, 5 * CHUNK], U8, name="got_s0", align_bytes=64), chunk_s)
+        gather(words, keep.tile([P, QUARTER], U32, name="got_w0", tag="got_w0", align_bytes=64), chunk_w)
+        gather(words, keep.tile([P, 2 * QUARTER], U32, name="got_w1", align_bytes=64), chunk_w)
 
-        gather_scales(0, 5 * CHUNK, keep.tile([P, 5 * CHUNK], U8, name="got_s0", align_bytes=64))
-        gather_words(0, QUARTER, "got_w0")
-        gather_words(QUARTER, C, "got_w1")
         turn_a(0)
         silu(0)
         tanh(0)
         turn_a(1)
         gate_cols = make_gate_cols()
-        gate_step(0, "gated0")
+        gate_on_gpsimd(0)
         silu(1)
         tanh(1)
-        gate_step(1)
+        gate_on_gpsimd(1)
         times_silu(0)
-        times_gated(0, nc.gpsimd)
+        times_gated(0, nc.gpsimd, chunk_tile("dh", 0, BF16))
         times_silu(1)
-        gather_scales(5 * CHUNK, 3 * CHUNK, keep.tile([P, 3 * CHUNK], U8, name="got_s1", tag="got_w0", align_bytes=64))
-        times_gated(1, nc.vector)
-        turn_a(2)
-        silu(2)
-        times_silu(2)
+        gather(scale_bytes, keep.tile([P, 3 * CHUNK], U8, name="got_s1", tag="got_w0", align_bytes=64), chunk_s)
+        times_gated(1, nc.vector, chunk_tile("dh", 1, BF16, "gated0"))
+
+        start_chunk(2)
         tanh(2)
-        gate_step(2, "partial1")
-        turn_a(3)
-        silu(3)
-        times_silu(3)
+        gate_on_gpsimd(2, "partial1")
+        start_chunk(3)
         tanh(3)
-        gate_step(3, "gated3")
+        gate_on_gpsimd(3)
         turn_dh(0)
-        turn_a(4)
-        silu(4)
-        times_silu(4)
+        start_chunk(4)
         turn_dh(1)
         quantise(0)
-        gather_words(3 * QUARTER, QUARTER, None)
-        times_gated(2, nc.gpsimd)
-        times_gated(3, nc.gpsimd)
-        turn_a(5)
-        silu(5, "gated0")
-        times_silu(5)
+
+        last_words = reused.tile([P, QUARTER], U32, name="got_w3", offset=QUARTER_BYTES // 2, align_bytes=64)
+        gather(words, last_words, chunk_w)
+        times_gated(2, nc.gpsimd, dh_behind_quantise(2, 0))
+        times_gated(3, nc.gpsimd, chunk_tile("dh", 3, BF16))
+        start_chunk(5, "gated0")
         tanh(4)
-        back_to_tokens(0, 0, 0, QUARTER, "3")
-        back_to_tokens(0, 1, 0, QUARTER, "4")
-        gate_step(4)
-        times_gated(4, nc.gpsimd)
+        for kt in range(K // P):
+            back_to_tokens(0, kt, 0, QUARTER, DH_BANK[kt])
+        gate_on_scalar(4)
+        times_gated(4, nc.gpsimd, chunk_tile("dh", 4, BF16))
         turn_dh(2)
         tanh(5)
-        gate_step(5)
-        times_gated(5, nc.gpsimd)
+        gate_on_scalar(5)
+        times_gated(5, nc.gpsimd, chunk_tile("dh", 5, BF16))
         turn_dh(3)
         quantise(1)
-        turn_a(6)
-        silu(6)
-        times_silu(6)
-        turn_a(7)
-        silu(7)
-        times_silu(7)
+
+        start_chunk(6)
+        start_chunk(7)
         turn_dh(4)
         tanh(6)
         turn_dh(5)
         quantise(2)
-        back_to_tokens(1, 0, QUARTER, QUARTER, "0", "dh5")
-        gate_step(6)
-        times_gated(6, nc.gpsimd)
+        back_to_tokens(1, 0, QUARTER, QUARTER, SPARE[0], "dh5")
+        gate_on_scalar(6)
+        times_gated(6, nc.gpsimd, dh_behind_quantise(6, 2))
         tanh(7)
-        back_to_tokens(1, 1, QUARTER, QUARTER, "1")
-        gate_step(7)
-        times_gated(7, nc.gpsimd)
-        back_to_tokens(2, 1, 2 * QUARTER, CHUNK, "4")
+        back_to_tokens(1, 1, QUARTER, QUARTER, SPARE[1])
+        gate_on_scalar(7)
+        times_gated(7, nc.gpsimd, chunk_tile("dh", 7, BF16))
+        back_to_tokens(2, 1, 4 * CHUNK, CHUNK, DH_BANK[1])
         turn_dh(6)
-        base_first = held_base()
-        base_second = [frozen_product(1, toks, "25"[h]) for h, toks in enumerate(token_halves)]
+
+        base_first, base_second = [], []
+        for h, toks in enumerate(token_halves):
+            held = keep.tile([P, BANK], F32, name="held%d" % h)
+            base = psum.tile([P, BANK], F32, name="base", tag="sums")
+            frozen_product(base, 0, toks)
+            nc.scalar.copy(held[:], base[:])
+            base_first.append(held)
+        for h, toks in enumerate(token_halves):
+            base = psum.tile([P, BANK], F32, name="base", tag=SPARE[2 + h], bufs=1)
+            frozen_product(base, 1, toks)
+            base_second.append(base)
         turn_dh(7)
         quantise(3)
-        back_to_tokens(2, 0, 2 * QUARTER, QUARTER, "0", "dh7")
-        back_to_tokens(3, 0, 3 * QUARTER, QUARTER, "1")
+
+        back_to_tokens(2, 0, 2 * QUARTER, QUARTER, SPARE[0], "dh7")
+        back_to_tokens(3, 0, 3 * QUARTER, QUARTER, SPARE[1])
         add_and_store(0, nc.gpsimd.tensor_tensor, base_first)
-        back_to_tokens(3, 1, 5 * CHUNK, 3 * CHUNK, "3")
+        back_to_tokens(3, 1, 5 * CHUNK, 3 * CHUNK, DH_BANK[0])
         add_and_store(1, nc.vector.tensor_tensor, base_second)

@@ -30,9 +30,10 @@ BANK = 512
 QUARTERS = E * C // QUARTER
 QUARTER_BYTES = QUARTER * PACK * 2
 
-SPARE = ("spare0", "spare1", "spare2", "spare3")
-DH_BANK = ("dh_even", "dh_odd")
-A_BANK = (SPARE[0], SPARE[1], DH_BANK[0], DH_BANK[1], SPARE[0], SPARE[1], SPARE[2], SPARE[3])
+BANK_BYTES = 4 * BANK
+TURN = [b * BANK_BYTES for b in (0, 1, 2, 3)]
+SUMS = [b * BANK_BYTES for b in (4, 5)]
+SPARE = [b * BANK_BYTES for b in (6, 7)]
 
 
 def tile_moe_adb_silu_kernel(
@@ -42,7 +43,7 @@ def tile_moe_adb_silu_kernel(
     with ExitStack() as ctx:
         keep = ctx.enter_context(tc.tile_pool(name="keep", bufs=1))
         reused = ctx.enter_context(tc.tile_pool(name="reused", bufs=1))
-        psum = ctx.enter_context(tc.psum_pool(name="psum", bufs=2))
+        psum = ctx.enter_context(tc.psum_pool(name="psum", bufs=1))
 
         offsets = keep.tile([P, E * C // LIST_ROWS], U16, name="offsets")
         dy_w = keep.tile([P, T], I32, name="dy_w", align_bytes=64)
@@ -67,8 +68,8 @@ def tile_moe_adb_silu_kernel(
         nc.vector.memset(wa_s[:].bitcast(I32), 0)
         nc.vector.memset(wt_s[:].bitcast(I32), 0)
 
-        def load_scales(tile, rows):
-            for r in range(4):
+        def load_scales(tile, rows, which=range(4)):
+            for r in which:
                 nc.sync.dma_start(out=tile[r:P:32].bitcast(I32), in_=rows[r].bitcast(I32))
 
         def load_a(q):
@@ -88,12 +89,14 @@ def tile_moe_adb_silu_kernel(
         nc.sync.dma_start(out=gate_rows[0:CHUNKS, :], in_=gate[0, :].rearrange("(c p) -> c p", p=CHUNK))
         load_a(1)
         load_wb(0)
-        load_scales(wb_s, wbt_scales.rearrange("e g (s r) i -> r s (e g) i", r=4))
+        wb_rows = wbt_scales.rearrange("e g (s r) i -> r s (e g) i", r=4)
+        load_scales(wb_s, wb_rows, range(3))
         load_a(2)
+        load_scales(wb_s, wb_rows, range(3, 4))
+        load_a(3)
         load_wb(1)
         nc.sync.dma_start(out=wa_w[:], in_=wat_words.rearrange("e g p k d -> p (e g) (k d)").bitcast(I32))
         load_scales(wa_s, wat_scales.rearrange("e g (s r) k -> r s (e g) k", r=4))
-        load_a(3)
         nc.sync.dma_start(out=wt_w[:].bitcast(I32), in_=wt_words[0].bitcast(I32))
         load_scales(wt_s, wt_scales[0].rearrange("(s r) k -> r s k", r=4))
 
@@ -107,28 +110,26 @@ def tile_moe_adb_silu_kernel(
             nc.vector.tensor_copy(got[:], table.indirect(entries(len(by_chunk) * CHUNK, n)))
             by_chunk.extend(got[:, j : j + CHUNK] for j in range(0, n, CHUNK))
 
-        dh_w = keep.tile([P, QUARTER + E * C], I32, name="dh_w", align_bytes=64)
-        dh_s = keep.tile([P, QUARTER + E * C], U8, name="dh_s", align_bytes=64)
-        nc.gpsimd.memset(dh_w[:, 0:QUARTER], 0)
-        nc.gpsimd.memset(dh_s[:, 0:QUARTER].bitcast(I32), 0)
         window = [keep.tile([P, T], F32, name="window%d" % kt) for kt in range(K // P)]
         a_t, silus, tanhs, gated, partial, dh = {}, {}, {}, {}, {}, {}
-        grouped = {}
+        dh_t, grouped, dh_w, dh_s, dx = {}, {}, {}, {}, {}
 
-        def chunk_tile(name, c, dtype, tag=None):
-            return keep.tile([P, H], dtype, name="%s%d" % (name, c), tag=tag or "%s%d" % (name, c), align_bytes=64)
+        def sb_tile(name, shape, dtype, tag=None):
+            if isinstance(tag, int):
+                return reused.tile(shape, dtype, name=name, offset=tag, align_bytes=64)
+            return keep.tile(shape, dtype, name=name, tag=tag or name, align_bytes=64)
 
         def turn_a(c):
             q, j0 = divmod(c * CHUNK, QUARTER)
-            a_t[c] = psum.tile([P, PACK, P], F32, name="a_t", tag=A_BANK[c], bufs=1)
+            a_t[c] = psum.tile([P, PACK, P], F32, name="a_t%d" % c, offset=TURN[c % 4])
             for t in range(PACK):
                 nc.tensor.transpose(a_t[c][:, t, :], a_sb[q][:, t, j0 : j0 + CHUNK], ident[:])
 
         def activate(dst, src, c, func, scale):
             nc.scalar.activation(dst, src, func, scale=scale, bias=zero_bias[:] if c == 0 else 0.0)
 
-        def silu(c, tag=None):
-            silus[c] = chunk_tile("silu", c, F32, tag)
+        def silu(c):
+            silus[c] = sb_tile("silu%d" % c, [P, H], F32)
             activate(
                 silus[c][:].rearrange("j (m t) -> j m t", t=PACK), a_t[c][:].rearrange("j t m -> j m t"),
                 c, ACT.Silu, -1.0,
@@ -138,179 +139,155 @@ def tile_moe_adb_silu_kernel(
             return tile[:].rearrange("j (u m o) -> j u m o", u=2, o=2)
 
         def tanh(c):
-            tanhs[c] = chunk_tile("tanh", c, F32)
+            tanhs[c] = sb_tile("tanh%d" % c, [P, H], F32)
             activate(by_pair(tanhs[c]), a_t[c][:].rearrange("j (u o) m -> j u m o", u=2), c, ACT.Tanh, 0.5)
 
         def make_gate_cols():
-            bank = psum.tile([P, 2, CHUNK], F32, name="gate_t", tag=SPARE[2], bufs=1)
+            bank = psum.tile([P, 2, CHUNK], F32, name="gate_t", offset=SPARE[0])
             nc.tensor.transpose(bank[:, 0, :], gate_rows[:], ident[:])
             cols = keep.tile([P, CHUNKS], F32, name="gate_cols")
             nc.scalar.activation(cols[:], bank[:, 0, 0:CHUNKS], ACT.Copy, scale=-0.5)
             return cols
 
+        def gate_step(c, tag=None):
+            g = gate_cols[:, c : c + 1]
+            gated[c] = sb_tile("gated%d" % c, [P, H], F32, tag)
+            nc.gpsimd.tensor_scalar(gated[c][:], tanhs[c][:], g, g, ALU.mult, ALU.add)
+
         def gate_on_scalar(c):
             g = gate_cols[:, c : c + 1]
-            gated[c] = chunk_tile("gated", c, F32)
+            gated[c] = sb_tile("gated%d" % c, [P, H], F32)
             nc.scalar.activation(gated[c][:], tanhs[c][:], ACT.Identity, bias=g, scale=g)
-
-        def gate_on_gpsimd(c, tag=None):
-            g = gate_cols[:, c : c + 1]
-            gated[c] = chunk_tile("gated", c, F32, tag)
-            nc.gpsimd.tensor_scalar(gated[c][:], tanhs[c][:], g, g, ALU.mult, ALU.add)
 
         def times_silu(c):
             e = c * CHUNK // C
-            sums = psum.tile([P, H], F32, name="sums")
+            sums = psum.tile([P, H], F32, name="sums%d" % c, offset=SUMS[c % 2])
             nc.tensor.matmul_mx(
                 out=sums[:], lhsT=chunk_w[c].bitcast(E5M2), lhsT_scale=chunk_s[c],
                 rhs=wb_w[e][:].bitcast(E4M3), rhs_scale=wb_s[:, e, :], start=True, stop=True,
             )
-            partial[c] = chunk_tile("partial", c, F32)
+            partial[c] = sb_tile("partial%d" % c, [P, H], F32)
             nc.vector.scalar_tensor_tensor(partial[c][:], silus[c][:], -1.0, sums[:], ALU.add, ALU.mult)
 
-        def times_gated(c, engine, dst):
-            dh[c] = dst
+        def times_gated(c, engine, tag=None):
+            dh[c] = sb_tile("dh%d" % c, [P, H], BF16, tag)
             engine.tensor_tensor(
-                by_pair(dst), by_pair(gated[c]), partial[c][:].rearrange("j (m u o) -> j u m o", u=2, o=2), ALU.mult
+                by_pair(dh[c]), by_pair(gated[c]), partial[c][:].rearrange("j (m u o) -> j u m o", u=2, o=2), ALU.mult
             )
 
-        def dh_behind_quantise(c, q):
-            return reused.tile([P, H], BF16, name="dh%d" % c, offset=q * QUARTER_BYTES, align_bytes=64)
+        def turn_dh(q, bank, tag=None):
+            dh_t[q] = psum.tile([P, 2, 2, CHUNK], F32, name="dh_t%d" % q, offset=bank)
+            for h in range(2):
+                pairs = dh[2 * q + h][:].bitcast(F32)
+                for u in range(2):
+                    nc.tensor.transpose(dh_t[q][:, h, u, :], pairs[:, u * P : (u + 1) * P], ident[:])
+            grouped[q] = sb_tile("grouped%d" % q, [P, 2, CHUNK, 2], F32, tag)
+            nc.scalar.copy(grouped[q][:], dh_t[q][:].rearrange("m h u j -> m h j u"))
 
-        def turn_dh(c):
-            q, j0 = divmod(c * CHUNK, QUARTER)
-            bank = psum.tile([P, 2, CHUNK], F32, name="dh_t", tag=DH_BANK[c % 2], bufs=1)
-            pairs = dh[c][:].bitcast(F32)
-            for u in range(2):
-                nc.tensor.transpose(bank[:, u, :], pairs[:, u * P : (u + 1) * P], ident[:])
-            if j0 == 0:
-                grouped[q] = reused.tile(
-                    [P, QUARTER, 2], F32, name="grouped%d" % q, offset=q * QUARTER_BYTES, align_bytes=64
-                )
-            nc.scalar.copy(grouped[q][:, j0 : j0 + CHUNK, :], bank[:].rearrange("m u j -> m j u"))
-
-        def quantise(q):
-            own = slice((q + 1) * QUARTER, (q + 2) * QUARTER)
+        def quantise(q, tag=None):
+            dh_w[q] = sb_tile("dh_w%d" % q, [P, QUARTER], I32, tag)
+            dh_s[q] = sb_tile("dh_s%d" % q, [P, QUARTER], U8)
             nc.vector.quantize_mx(
-                out=dh_w[:, own].bitcast(E5M2), scales=dh_s[:, own],
-                in_=grouped[q][:].rearrange("m j u -> m (j u)").bitcast(BF16),
+                out=dh_w[q][:].bitcast(E5M2), scales=dh_s[q][:],
+                in_=grouped[q][:].rearrange("m h j u -> m (h j u)").bitcast(BF16),
             )
 
-        def back_to_tokens(q, kt, j0, n, bank, tag=None):
-            name = "dx%d_%d" % (q, kt)
-            dx = keep.tile([P, n], F32, name=name, tag=tag or name, align_bytes=64)
+        def second_product(q, kt, bank, copy, tag=None):
             e = q * QUARTER // C
-            span = slice(q * QUARTER, (q + 2) * QUARTER)
-            acc = psum.tile([P, BANK], F32, name="acc", tag=bank, bufs=1)
+            acc = psum.tile([P, QUARTER], F32, name="acc%d_%d" % (q, kt), offset=bank)
             nc.tensor.matmul_mx(
                 out=acc[:], lhsT=wa_w[:, e, kt * P : (kt + 1) * P].bitcast(E4M3),
                 lhsT_scale=wa_s[:, e, kt * P : (kt + 1) * P],
-                rhs=dh_w[:, span].bitcast(E5M2), rhs_scale=dh_s[:, span], start=True, stop=True,
+                rhs=dh_w[q][:].bitcast(E5M2), rhs_scale=dh_s[q][:], start=True, stop=True,
             )
-            first = j0 - (q - 1) * QUARTER
-            nc.scalar.copy(dx[:], acc[:, first : first + n])
-            nc.vector.tensor_copy(window[kt][:].indirect(entries(j0, n)), dx[:])
+            dx[q, kt] = sb_tile("dx%d_%d" % (q, kt), [P, QUARTER], F32, tag)
+            copy(dx[q, kt][:], acc[:])
 
-        def frozen_product(base, kt, toks):
-            nc.tensor.matmul_mx(
-                out=base[:], lhsT=wt_w[:, 2 * kt * P : 2 * (kt + 1) * P].bitcast(E2M1),
-                lhsT_scale=wt_s[:, kt * P : (kt + 1) * P],
-                rhs=dy_w[:, toks].bitcast(E5M2), rhs_scale=dy_s[:, toks], start=True, stop=True,
-            )
+        def scatter(q, kt):
+            target = window[kt][:].indirect(entries(q * QUARTER, QUARTER))
+            if kt == 0:
+                nc.vector.tensor_copy(target, dx[q, kt][:])
+            else:
+                nc.scalar.activation(target, dx[q, kt][:], ACT.Copy)
 
-        token_halves = [slice(h * BANK, (h + 1) * BANK) for h in range(T // BANK)]
-
-        def add_and_store(kt, add, bases):
-            for h, toks in enumerate(token_halves):
+        def add_and_store(kt, banks):
+            for h in range(T // BANK):
+                toks = slice(h * BANK, (h + 1) * BANK)
+                base = psum.tile([P, BANK], F32, name="base%d_%d" % (kt, h), offset=banks[h])
+                nc.tensor.matmul_mx(
+                    out=base[:], lhsT=wt_w[:, 2 * kt * P : 2 * (kt + 1) * P].bitcast(E2M1),
+                    lhsT_scale=wt_s[:, kt * P : (kt + 1) * P],
+                    rhs=dy_w[:, toks].bitcast(E5M2), rhs_scale=dy_s[:, toks], start=True, stop=True,
+                )
                 res = keep.tile([P, BANK], F32, name="res%d_%d" % (kt, h))
-                add(res[:], bases[h][:], window[kt][:, toks], ALU.add)
+                nc.vector.tensor_tensor(res[:], base[:], window[kt][:, toks], ALU.add)
                 nc.sync.dma_start(out=out[kt * P : (kt + 1) * P, toks], in_=res[:])
 
-        def start_chunk(c, tag=None):
+        def factors(c):
             turn_a(c)
-            silu(c, tag)
-            times_silu(c)
+            tanh(c)
+            silu(c)
 
         words, scale_bytes = dy_w[:].bitcast(U32), dy_s[:]
-        gather(scale_bytes, keep.tile([P, 5 * CHUNK], U8, name="got_s0", align_bytes=64), chunk_s)
-        gather(words, keep.tile([P, QUARTER], U32, name="got_w0", tag="got_w0", align_bytes=64), chunk_w)
-        gather(words, keep.tile([P, 2 * QUARTER], U32, name="got_w1", align_bytes=64), chunk_w)
+        gather(scale_bytes, sb_tile("got_s0", [P, 3 * QUARTER], U8), chunk_s)
+        gather(words, sb_tile("got_w0", [P, QUARTER], U32), chunk_w)
+        gather(words, sb_tile("got_w1", [P, 3 * QUARTER], U32), chunk_w)
+        gather(scale_bytes, sb_tile("got_s1", [P, QUARTER], U8), chunk_s)
 
-        turn_a(0)
-        silu(0)
-        tanh(0)
-        turn_a(1)
+        factors(0)
         gate_cols = make_gate_cols()
-        gate_on_gpsimd(0)
-        silu(1)
-        tanh(1)
-        gate_on_gpsimd(1)
+        gate_step(0)
+        for c in (1, 2, 3):
+            factors(c)
+            gate_step(c)
         times_silu(0)
-        times_gated(0, nc.gpsimd, chunk_tile("dh", 0, BF16))
+        times_gated(0, nc.gpsimd)
         times_silu(1)
-        gather(scale_bytes, keep.tile([P, 3 * CHUNK], U8, name="got_s1", tag="got_w0", align_bytes=64), chunk_s)
-        times_gated(1, nc.vector, chunk_tile("dh", 1, BF16, "gated0"))
-
-        start_chunk(2)
-        tanh(2)
-        gate_on_gpsimd(2, "partial1")
-        start_chunk(3)
-        tanh(3)
-        gate_on_gpsimd(3)
-        turn_dh(0)
-        start_chunk(4)
-        turn_dh(1)
+        times_gated(1, nc.vector)
+        times_silu(2)
+        times_gated(2, nc.gpsimd)
+        times_silu(3)
+        times_gated(3, nc.vector, 1984)
+        factors(4)
+        gate_step(4, "partial0")
+        times_silu(4)
+        factors(5)
+        gate_step(5, "partial2")
+        times_gated(4, nc.gpsimd, "tanh5")
+        factors(6)
+        turn_dh(0, TURN[1])
         quantise(0)
+        times_silu(5)
+        times_silu(6)
+        times_gated(5, nc.vector, "grouped0")
+        gate_step(6)
+        factors(7)
+        times_gated(6, nc.gpsimd)
 
-        last_words = reused.tile([P, QUARTER], U32, name="got_w3", offset=QUARTER_BYTES // 2, align_bytes=64)
-        gather(words, last_words, chunk_w)
-        times_gated(2, nc.gpsimd, dh_behind_quantise(2, 0))
-        times_gated(3, nc.gpsimd, chunk_tile("dh", 3, BF16))
-        start_chunk(5, "gated0")
-        tanh(4)
-        for kt in range(K // P):
-            back_to_tokens(0, kt, 0, QUARTER, DH_BANK[kt])
-        gate_on_scalar(4)
-        times_gated(4, nc.gpsimd, chunk_tile("dh", 4, BF16))
-        turn_dh(2)
-        tanh(5)
-        gate_on_scalar(5)
-        times_gated(5, nc.gpsimd, chunk_tile("dh", 5, BF16))
-        turn_dh(3)
-        quantise(1)
-
-        start_chunk(6)
-        start_chunk(7)
-        turn_dh(4)
-        tanh(6)
-        turn_dh(5)
-        quantise(2)
-        back_to_tokens(1, 0, QUARTER, QUARTER, SPARE[0], "dh5")
-        gate_on_scalar(6)
-        times_gated(6, nc.gpsimd, dh_behind_quantise(6, 2))
-        tanh(7)
-        back_to_tokens(1, 1, QUARTER, QUARTER, SPARE[1])
+        second_product(0, 0, TURN[0], nc.scalar.copy)
         gate_on_scalar(7)
-        times_gated(7, nc.gpsimd, chunk_tile("dh", 7, BF16))
-        back_to_tokens(2, 1, 4 * CHUNK, CHUNK, DH_BANK[1])
-        turn_dh(6)
-
-        base_first, base_second = [], []
-        for h, toks in enumerate(token_halves):
-            held = keep.tile([P, BANK], F32, name="held%d" % h)
-            base = psum.tile([P, BANK], F32, name="base", tag="sums")
-            frozen_product(base, 0, toks)
-            nc.scalar.copy(held[:], base[:])
-            base_first.append(held)
-        for h, toks in enumerate(token_halves):
-            base = psum.tile([P, BANK], F32, name="base", tag=SPARE[2 + h], bufs=1)
-            frozen_product(base, 1, toks)
-            base_second.append(base)
-        turn_dh(7)
+        turn_dh(1, TURN[3])
+        second_product(0, 1, SPARE[1], nc.scalar.copy, 1984)
+        scatter(0, 0)
+        scatter(0, 1)
+        quantise(1, "dx0_0")
+        times_silu(7)
+        times_gated(7, nc.vector)
+        turn_dh(2, TURN[0], 0)
+        quantise(2)
+        second_product(1, 1, TURN[1], nc.scalar.copy, 2944)
+        second_product(1, 0, TURN[2], nc.vector.tensor_copy, 0)
+        scatter(1, 0)
+        scatter(1, 1)
+        turn_dh(3, TURN[3], 3904)
         quantise(3)
-
-        back_to_tokens(2, 0, 2 * QUARTER, QUARTER, SPARE[0], "dh7")
-        back_to_tokens(3, 0, 3 * QUARTER, QUARTER, SPARE[1])
-        add_and_store(0, nc.gpsimd.tensor_tensor, base_first)
-        back_to_tokens(3, 1, 5 * CHUNK, 3 * CHUNK, DH_BANK[0])
-        add_and_store(1, nc.vector.tensor_tensor, base_second)
+        second_product(2, 0, TURN[2], nc.vector.tensor_copy, 4928)
+        second_product(2, 1, TURN[0], nc.scalar.copy, 2048)
+        scatter(2, 0)
+        scatter(2, 1)
+        second_product(3, 0, TURN[1], nc.vector.tensor_copy)
+        second_product(3, 1, TURN[3], nc.scalar.copy, 2048)
+        scatter(3, 0)
+        scatter(3, 1)
+        add_and_store(0, SUMS)
+        add_and_store(1, SPARE)

@@ -34,6 +34,7 @@ BANK_BYTES = 4 * BANK
 TURN = [b * BANK_BYTES for b in (0, 1, 2, 3)]
 SUMS = [b * BANK_BYTES for b in (4, 5)]
 SPARE = [b * BANK_BYTES for b in (6, 7)]
+GROUPS = ((0, 1), (1, 1), (2, 2), (4, 2), (6, 2))
 
 
 def tile_moe_adb_silu_kernel(
@@ -94,9 +95,9 @@ def tile_moe_adb_silu_kernel(
         load_a(2)
         load_scales(wb_s, wb_rows, range(3, 4))
         load_a(3)
-        load_wb(1)
         nc.sync.dma_start(out=wa_w[:], in_=wat_words.rearrange("e g p k d -> p (e g) (k d)").bitcast(I32))
         load_scales(wa_s, wat_scales.rearrange("e g (s r) k -> r s (e g) k", r=4))
+        load_wb(1)
         nc.sync.dma_start(out=wt_w[:].bitcast(I32), in_=wt_words[0].bitcast(I32))
         load_scales(wt_s, wt_scales[0].rearrange("(s r) k -> r s k", r=4))
 
@@ -175,40 +176,48 @@ def tile_moe_adb_silu_kernel(
                 by_pair(dh[c]), by_pair(gated[c]), partial[c][:].rearrange("j (m u o) -> j u m o", u=2, o=2), ALU.mult
             )
 
-        def turn_dh(q, bank, tag=None):
-            dh_t[q] = psum.tile([P, 2, 2, CHUNK], F32, name="dh_t%d" % q, offset=bank)
-            for h in range(2):
-                pairs = dh[2 * q + h][:].bitcast(F32)
+        def turn_dh(g, bank, tag=None):
+            c0, n = GROUPS[g]
+            dh_t[g] = psum.tile([P, n, 2, CHUNK], F32, name="dh_t%d" % g, offset=bank)
+            for h in range(n):
+                pairs = dh[c0 + h][:].bitcast(F32)
                 for u in range(2):
-                    nc.tensor.transpose(dh_t[q][:, h, u, :], pairs[:, u * P : (u + 1) * P], ident[:])
-            grouped[q] = sb_tile("grouped%d" % q, [P, 2, CHUNK, 2], F32, tag)
-            nc.scalar.copy(grouped[q][:], dh_t[q][:].rearrange("m h u j -> m h j u"))
+                    nc.tensor.transpose(dh_t[g][:, h, u, :], pairs[:, u * P : (u + 1) * P], ident[:])
+            grouped[g] = sb_tile("grouped%d" % g, [P, n, CHUNK, 2], F32, tag)
+            nc.scalar.copy(grouped[g][:], dh_t[g][:].rearrange("m h u j -> m h j u"))
 
-        def quantise(q, tag=None):
-            dh_w[q] = sb_tile("dh_w%d" % q, [P, QUARTER], I32, tag)
-            dh_s[q] = sb_tile("dh_s%d" % q, [P, QUARTER], U8)
+        def quantise(g, tag=None):
+            slots = GROUPS[g][1] * CHUNK
+            dh_w[g] = sb_tile("dh_w%d" % g, [P, slots], I32, tag)
+            dh_s[g] = sb_tile("dh_s%d" % g, [P, slots], U8)
             nc.vector.quantize_mx(
-                out=dh_w[q][:].bitcast(E5M2), scales=dh_s[q][:],
-                in_=grouped[q][:].rearrange("m h j u -> m (h j u)").bitcast(BF16),
+                out=dh_w[g][:].bitcast(E5M2), scales=dh_s[g][:],
+                in_=grouped[g][:].rearrange("m h j u -> m (h j u)").bitcast(BF16),
             )
 
-        def second_product(q, kt, bank, copy, tag=None):
-            e = q * QUARTER // C
-            acc = psum.tile([P, QUARTER], F32, name="acc%d_%d" % (q, kt), offset=bank)
-            nc.tensor.matmul_mx(
-                out=acc[:], lhsT=wa_w[:, e, kt * P : (kt + 1) * P].bitcast(E4M3),
-                lhsT_scale=wa_s[:, e, kt * P : (kt + 1) * P],
-                rhs=dh_w[q][:].bitcast(E5M2), rhs_scale=dh_s[q][:], start=True, stop=True,
-            )
-            dx[q, kt] = sb_tile("dx%d_%d" % (q, kt), [P, QUARTER], F32, tag)
-            copy(dx[q, kt][:], acc[:])
+        def second_product(g, halves, bank, copy, tag=None):
+            c0, n = GROUPS[g]
+            e = c0 * CHUNK // C
+            name = "%d_%d" % (g, halves[0])
+            acc = psum.tile([P, len(halves), n * CHUNK], F32, name="acc" + name, offset=bank)
+            for x, kt in enumerate(halves):
+                nc.tensor.matmul_mx(
+                    out=acc[:, x, :], lhsT=wa_w[:, e, kt * P : (kt + 1) * P].bitcast(E4M3),
+                    lhsT_scale=wa_s[:, e, kt * P : (kt + 1) * P],
+                    rhs=dh_w[g][:].bitcast(E5M2), rhs_scale=dh_s[g][:], start=True, stop=True,
+                )
+            held = sb_tile("dx" + name, [P, len(halves), n * CHUNK], F32, tag)
+            copy(held[:], acc[:])
+            for x, kt in enumerate(halves):
+                dx[g, kt] = held[:, x, :]
 
-        def scatter(q, kt):
-            target = window[kt][:].indirect(entries(q * QUARTER, QUARTER))
-            if kt == 0:
-                nc.vector.tensor_copy(target, dx[q, kt][:])
+        def scatter(g, kt, on_scalar):
+            c0, n = GROUPS[g]
+            target = window[kt][:].indirect(entries(c0 * CHUNK, n * CHUNK))
+            if on_scalar:
+                nc.scalar.activation(target, dx[g, kt], ACT.Copy)
             else:
-                nc.scalar.activation(target, dx[q, kt][:], ACT.Copy)
+                nc.vector.tensor_copy(target, dx[g, kt])
 
         def add_and_store(kt, banks):
             for h in range(T // BANK):
@@ -237,57 +246,49 @@ def tile_moe_adb_silu_kernel(
         factors(0)
         gate_cols = make_gate_cols()
         gate_step(0)
-        for c in (1, 2, 3):
+        for c in range(1, 5):
             factors(c)
             gate_step(c)
-        times_silu(0)
-        times_gated(0, nc.gpsimd)
-        times_silu(1)
-        times_gated(1, nc.vector)
-        times_silu(2)
-        times_gated(2, nc.gpsimd)
-        times_silu(3)
-        times_gated(3, nc.vector, 1984)
-        factors(4)
-        gate_step(4, "partial0")
-        times_silu(4)
+        for c in range(2):
+            times_silu(c)
+            times_gated(c, nc.vector)
         factors(5)
-        gate_step(5, "partial2")
-        times_gated(4, nc.gpsimd, "tanh5")
+        gate_step(5)
         factors(6)
-        turn_dh(0, TURN[1])
-        quantise(0)
-        times_silu(5)
-        times_silu(6)
-        times_gated(5, nc.vector, "grouped0")
         gate_step(6)
+        turn_dh(0, SPARE[0])
+        quantise(0)
+        turn_dh(1, SPARE[1])
+        quantise(1)
         factors(7)
-        times_gated(6, nc.gpsimd)
+        gate_step(7)
+        for c in range(2, 8):
+            times_silu(c)
+            times_gated(c, nc.vector)
 
-        second_product(0, 0, TURN[0], nc.scalar.copy)
-        gate_on_scalar(7)
-        turn_dh(1, TURN[3])
-        second_product(0, 1, SPARE[1], nc.scalar.copy, 1984)
-        scatter(0, 0)
-        scatter(0, 1)
-        quantise(1, "dx0_0")
-        times_silu(7)
-        times_gated(7, nc.vector)
-        turn_dh(2, TURN[0], 0)
-        quantise(2)
-        second_product(1, 1, TURN[1], nc.scalar.copy, 2944)
-        second_product(1, 0, TURN[2], nc.vector.tensor_copy, 0)
-        scatter(1, 0)
-        scatter(1, 1)
-        turn_dh(3, TURN[3], 3904)
-        quantise(3)
-        second_product(2, 0, TURN[2], nc.vector.tensor_copy, 4928)
-        second_product(2, 1, TURN[0], nc.scalar.copy, 2048)
-        scatter(2, 0)
-        scatter(2, 1)
-        second_product(3, 0, TURN[1], nc.vector.tensor_copy)
-        second_product(3, 1, TURN[3], nc.scalar.copy, 2048)
-        scatter(3, 0)
-        scatter(3, 1)
+        second_product(0, (0, 1), TURN[0], nc.scalar.copy)
+        scatter(0, 0, True)
+        scatter(0, 1, True)
+        turn_dh(2, TURN[2])
+        quantise(2, "partial5")
+        second_product(1, (0, 1), TURN[1], nc.scalar.copy, "dh3")
+        scatter(1, 0, True)
+        scatter(1, 1, True)
+        turn_dh(3, TURN[3])
+        second_product(2, (0,), SPARE[0], nc.vector.tensor_copy, "gated7")
+        quantise(3, "partial7")
+        scatter(2, 0, False)
+        turn_dh(4, TURN[0])
+        second_product(2, (1,), SPARE[1], nc.scalar.copy, "dh7")
+        second_product(3, (1,), TURN[2], nc.scalar.copy)
+        second_product(3, (0,), TURN[1], nc.vector.tensor_copy)
+        quantise(4)
+        scatter(2, 1, True)
+        scatter(3, 0, False)
+        second_product(4, (0,), TURN[3], nc.vector.tensor_copy)
+        second_product(4, (1,), TURN[0], nc.scalar.copy)
+        scatter(3, 1, True)
+        scatter(4, 0, False)
+        scatter(4, 1, True)
         add_and_store(0, SUMS)
         add_and_store(1, SPARE)

@@ -32,8 +32,8 @@ QUARTER_BYTES = QUARTER * PACK * 2
 
 BANK_BYTES = 4 * BANK
 TURN = [b * BANK_BYTES for b in (0, 1, 2, 3)]
-SUMS = [b * BANK_BYTES for b in (4, 5)]
-SPARE = [b * BANK_BYTES for b in (6, 7)]
+SUMS = [b * BANK_BYTES for b in (4, 5, 6)]
+SPARE = [b * BANK_BYTES for b in (7,)]
 GROUPS = ((0, 1), (1, 1), (2, 2), (4, 2), (6, 2))
 
 
@@ -95,9 +95,9 @@ def tile_moe_adb_silu_kernel(
         load_a(2)
         load_scales(wb_s, wb_rows, range(3, 4))
         load_a(3)
+        load_wb(1)
         nc.sync.dma_start(out=wa_w[:], in_=wat_words.rearrange("e g p k d -> p (e g) (k d)").bitcast(I32))
         load_scales(wa_s, wat_scales.rearrange("e g (s r) k -> r s (e g) k", r=4))
-        load_wb(1)
         nc.sync.dma_start(out=wt_w[:].bitcast(I32), in_=wt_words[0].bitcast(I32))
         load_scales(wt_s, wt_scales[0].rearrange("(s r) k -> r s k", r=4))
 
@@ -111,7 +111,7 @@ def tile_moe_adb_silu_kernel(
             nc.vector.tensor_copy(got[:], table.indirect(entries(len(by_chunk) * CHUNK, n)))
             by_chunk.extend(got[:, j : j + CHUNK] for j in range(0, n, CHUNK))
 
-        window = [keep.tile([P, T], F32, name="window%d" % kt) for kt in range(K // P)]
+        window = {}
         a_t, silus, tanhs, gated, partial, dh = {}, {}, {}, {}, {}, {}
         dh_t, grouped, dh_w, dh_s, dx = {}, {}, {}, {}, {}
 
@@ -162,7 +162,7 @@ def tile_moe_adb_silu_kernel(
 
         def times_silu(c):
             e = c * CHUNK // C
-            sums = psum.tile([P, H], F32, name="sums%d" % c, offset=SUMS[c % 2])
+            sums = psum.tile([P, H], F32, name="sums%d" % c, offset=SUMS[c % 3])
             nc.tensor.matmul_mx(
                 out=sums[:], lhsT=chunk_w[c].bitcast(E5M2), lhsT_scale=chunk_s[c],
                 rhs=wb_w[e][:].bitcast(E4M3), rhs_scale=wb_s[:, e, :], start=True, stop=True,
@@ -195,29 +195,28 @@ def tile_moe_adb_silu_kernel(
                 in_=grouped[g][:].rearrange("m h j u -> m (h j u)").bitcast(BF16),
             )
 
-        def second_product(g, halves, bank, copy, tag=None):
+        def second_product(g, halves, bank, copy, dst):
             c0, n = GROUPS[g]
             e = c0 * CHUNK // C
-            name = "%d_%d" % (g, halves[0])
-            acc = psum.tile([P, len(halves), n * CHUNK], F32, name="acc" + name, offset=bank)
+            acc = psum.tile([P, len(halves), n * CHUNK], F32, name="acc%d_%d" % (g, halves[0]), offset=bank)
             for x, kt in enumerate(halves):
                 nc.tensor.matmul_mx(
                     out=acc[:, x, :], lhsT=wa_w[:, e, kt * P : (kt + 1) * P].bitcast(E4M3),
                     lhsT_scale=wa_s[:, e, kt * P : (kt + 1) * P],
                     rhs=dh_w[g][:].bitcast(E5M2), rhs_scale=dh_s[g][:], start=True, stop=True,
                 )
-            held = sb_tile("dx" + name, [P, len(halves), n * CHUNK], F32, tag)
-            copy(held[:], acc[:])
-            for x, kt in enumerate(halves):
-                dx[g, kt] = held[:, x, :]
+            copy(dst, acc[:])
 
-        def scatter(g, kt, on_scalar):
-            c0, n = GROUPS[g]
-            target = window[kt][:].indirect(entries(c0 * CHUNK, n * CHUNK))
+        def dx_tile(q, kt, tag=None):
+            dx[q, kt] = sb_tile("dx%d_%d" % (q, kt), [P, 1, QUARTER], F32, tag)
+            return dx[q, kt][:]
+
+        def scatter(q, kt, on_scalar):
+            target = window[kt][:].indirect(entries(q * QUARTER, QUARTER))
             if on_scalar:
-                nc.scalar.activation(target, dx[g, kt], ACT.Copy)
+                nc.scalar.activation(target, dx[q, kt][:, 0, :], ACT.Copy)
             else:
-                nc.vector.tensor_copy(target, dx[g, kt])
+                nc.vector.tensor_copy(target, dx[q, kt][:, 0, :])
 
         def add_and_store(kt, banks):
             for h in range(T // BANK):
@@ -246,49 +245,62 @@ def tile_moe_adb_silu_kernel(
         factors(0)
         gate_cols = make_gate_cols()
         gate_step(0)
-        for c in range(1, 5):
+        for c in range(1, 4):
             factors(c)
             gate_step(c)
-        for c in range(2):
-            times_silu(c)
-            times_gated(c, nc.vector)
+        factors(4)
+        times_silu(0)
+        times_silu(1)
+        times_gated(0, nc.vector)
+        times_gated(1, nc.gpsimd)
+        gate_step(4, "partial1")
         factors(5)
         gate_step(5)
+        times_silu(2)
+        times_silu(3)
         factors(6)
-        gate_step(6)
         turn_dh(0, SPARE[0])
         quantise(0)
-        turn_dh(1, SPARE[1])
+        turn_dh(1, SPARE[0])
         quantise(1)
         factors(7)
-        gate_step(7)
-        for c in range(2, 8):
+        times_gated(2, nc.vector)
+        times_gated(3, nc.vector)
+        for c in range(4, 8):
             times_silu(c)
-            times_gated(c, nc.vector)
-
-        second_product(0, (0, 1), TURN[0], nc.scalar.copy)
-        scatter(0, 0, True)
-        scatter(0, 1, True)
+        times_gated(4, nc.gpsimd)
+        gate_step(6, "partial4")
+        gate_step(7)
+        times_gated(5, nc.vector)
         turn_dh(2, TURN[2])
-        quantise(2, "partial5")
-        second_product(1, (0, 1), TURN[1], nc.scalar.copy, "dh3")
-        scatter(1, 0, True)
-        scatter(1, 1, True)
+        quantise(2, "silu7")
+        times_gated(6, nc.vector)
+        times_gated(7, nc.vector)
+
+        first = sb_tile("dx0", [P, K // P, QUARTER], F32)
+        for kt in range(K // P):
+            dx[0, kt] = first[:, kt : kt + 1, :]
+        second_product(0, (0, 1), TURN[0], nc.scalar.copy, first[:, :, 0:CHUNK])
+        second_product(1, (0, 1), TURN[1], nc.scalar.copy, first[:, :, CHUNK:QUARTER])
+        window[0] = sb_tile("window0", [P, T], F32)
+        scatter(0, 0, True)
         turn_dh(3, TURN[3])
-        second_product(2, (0,), SPARE[0], nc.vector.tensor_copy, "gated7")
-        quantise(3, "partial7")
-        scatter(2, 0, False)
+        window[1] = sb_tile("window1", [P, T], F32, "dh5")
+        scatter(0, 1, True)
+        second_product(2, (0,), SPARE[0], nc.vector.tensor_copy, dx_tile(1, 0, "partial7"))
+        quantise(3, "gated7")
+        scatter(1, 0, False)
         turn_dh(4, TURN[0])
-        second_product(2, (1,), SPARE[1], nc.scalar.copy, "dh7")
-        second_product(3, (1,), TURN[2], nc.scalar.copy)
-        second_product(3, (0,), TURN[1], nc.vector.tensor_copy)
+        second_product(2, (1,), SUMS[0], nc.scalar.copy, dx_tile(1, 1, "dh7"))
+        second_product(3, (1,), TURN[2], nc.scalar.copy, dx_tile(2, 1))
+        second_product(3, (0,), TURN[1], nc.vector.tensor_copy, dx_tile(2, 0))
         quantise(4)
+        scatter(1, 1, True)
+        scatter(2, 0, False)
+        second_product(4, (0,), TURN[3], nc.vector.tensor_copy, dx_tile(3, 0))
+        second_product(4, (1,), TURN[0], nc.scalar.copy, dx_tile(3, 1))
         scatter(2, 1, True)
         scatter(3, 0, False)
-        second_product(4, (0,), TURN[3], nc.vector.tensor_copy)
-        second_product(4, (1,), TURN[0], nc.scalar.copy)
         scatter(3, 1, True)
-        scatter(4, 0, False)
-        scatter(4, 1, True)
-        add_and_store(0, SUMS)
-        add_and_store(1, SPARE)
+        add_and_store(0, SUMS[1:])
+        add_and_store(1, (SPARE[0], SUMS[0]))

@@ -69,8 +69,8 @@ def tile_moe_adb_silu_kernel(
         nc.vector.memset(wa_s[:].bitcast(I32), 0)
         nc.vector.memset(wt_s[:].bitcast(I32), 0)
 
-        def load_scales(tile, rows, which=range(4)):
-            for r in which:
+        def load_scales(tile, rows):
+            for r in range(4):
                 nc.sync.dma_start(out=tile[r:P:32].bitcast(I32), in_=rows[r].bitcast(I32))
 
         def load_a(q):
@@ -89,11 +89,9 @@ def tile_moe_adb_silu_kernel(
         nc.sync.dma_start(out=dy_w[:], in_=dy_words[0].rearrange("p t d -> p (t d)").bitcast(I32))
         nc.sync.dma_start(out=gate_rows[0:CHUNKS, :], in_=gate[0, :].rearrange("(c p) -> c p", p=CHUNK))
         load_a(1)
-        load_wb(0)
-        wb_rows = wbt_scales.rearrange("e g (s r) i -> r s (e g) i", r=4)
-        load_scales(wb_s, wb_rows, range(3))
         load_a(2)
-        load_scales(wb_s, wb_rows, range(3, 4))
+        load_wb(0)
+        load_scales(wb_s, wbt_scales.rearrange("e g (s r) i -> r s (e g) i", r=4))
         load_a(3)
         load_wb(1)
         nc.sync.dma_start(out=wa_w[:], in_=wat_words.rearrange("e g p k d -> p (e g) (k d)").bitcast(I32))
@@ -111,7 +109,7 @@ def tile_moe_adb_silu_kernel(
             nc.vector.tensor_copy(got[:], table.indirect(entries(len(by_chunk) * CHUNK, n)))
             by_chunk.extend(got[:, j : j + CHUNK] for j in range(0, n, CHUNK))
 
-        window = {}
+        window = [keep.tile([P, T], F32, name="window%d" % kt) for kt in range(K // P)]
         a_t, silus, tanhs, gated, partial, dh = {}, {}, {}, {}, {}, {}
         dh_t, grouped, dh_w, dh_s, dx = {}, {}, {}, {}, {}
 
@@ -207,16 +205,19 @@ def tile_moe_adb_silu_kernel(
                 )
             copy(dst, acc[:])
 
-        def dx_tile(q, kt, tag=None):
-            dx[q, kt] = sb_tile("dx%d_%d" % (q, kt), [P, 1, QUARTER], F32, tag)
-            return dx[q, kt][:]
+        def dx_tile(g, halves, tag=None):
+            held = sb_tile("dx%d_%d" % (g, halves[0]), [P, len(halves), GROUPS[g][1] * CHUNK], F32, tag)
+            for x, kt in enumerate(halves):
+                dx[g, kt] = held[:, x, :]
+            return held[:]
 
-        def scatter(q, kt, on_scalar):
-            target = window[kt][:].indirect(entries(q * QUARTER, QUARTER))
+        def scatter(g, kt, on_scalar):
+            c0, n = GROUPS[g]
+            target = window[kt][:].indirect(entries(c0 * CHUNK, n * CHUNK))
             if on_scalar:
-                nc.scalar.activation(target, dx[q, kt][:, 0, :], ACT.Copy)
+                nc.scalar.activation(target, dx[g, kt], ACT.Copy)
             else:
-                nc.vector.tensor_copy(target, dx[q, kt][:, 0, :])
+                nc.vector.tensor_copy(target, dx[g, kt])
 
         def add_and_store(kt, banks):
             for h in range(T // BANK):
@@ -245,62 +246,47 @@ def tile_moe_adb_silu_kernel(
         factors(0)
         gate_cols = make_gate_cols()
         gate_step(0)
-        for c in range(1, 4):
+        for c in range(1, 7):
             factors(c)
             gate_step(c)
-        factors(4)
+
         times_silu(0)
-        times_silu(1)
-        times_gated(0, nc.vector)
-        times_gated(1, nc.gpsimd)
-        gate_step(4, "partial1")
-        factors(5)
-        gate_step(5)
-        times_silu(2)
-        times_silu(3)
-        factors(6)
-        turn_dh(0, SPARE[0])
-        quantise(0)
-        turn_dh(1, SPARE[0])
-        quantise(1)
+        for c in range(2):
+            times_silu(c + 1)
+            times_gated(c, nc.vector)
+            turn_dh(c, SPARE[0])
         factors(7)
-        times_gated(2, nc.vector)
-        times_gated(3, nc.vector)
-        for c in range(4, 8):
-            times_silu(c)
-        times_gated(4, nc.gpsimd)
-        gate_step(6, "partial4")
         gate_step(7)
-        times_gated(5, nc.vector)
+        for c in range(2, 7):
+            times_silu(c + 1)
+            times_gated(c, nc.vector)
+            if c < 4:
+                quantise(c - 2, "partial%d" % c)
         turn_dh(2, TURN[2])
         quantise(2, "silu7")
-        times_gated(6, nc.vector)
         times_gated(7, nc.vector)
 
-        first = sb_tile("dx0", [P, K // P, QUARTER], F32)
-        for kt in range(K // P):
-            dx[0, kt] = first[:, kt : kt + 1, :]
-        second_product(0, (0, 1), TURN[0], nc.scalar.copy, first[:, :, 0:CHUNK])
-        second_product(1, (0, 1), TURN[1], nc.scalar.copy, first[:, :, CHUNK:QUARTER])
-        window[0] = sb_tile("window0", [P, T], F32)
+        second_product(0, (0, 1), TURN[0], nc.scalar.copy, dx_tile(0, (0, 1)))
         scatter(0, 0, True)
-        turn_dh(3, TURN[3])
-        window[1] = sb_tile("window1", [P, T], F32, "dh5")
         scatter(0, 1, True)
-        second_product(2, (0,), SPARE[0], nc.vector.tensor_copy, dx_tile(1, 0, "partial7"))
-        quantise(3, "gated7")
-        scatter(1, 0, False)
-        turn_dh(4, TURN[0])
-        second_product(2, (1,), SUMS[0], nc.scalar.copy, dx_tile(1, 1, "dh7"))
-        second_product(3, (1,), TURN[2], nc.scalar.copy, dx_tile(2, 1))
-        second_product(3, (0,), TURN[1], nc.vector.tensor_copy, dx_tile(2, 0))
-        quantise(4)
+        turn_dh(3, TURN[3])
+        second_product(1, (0, 1), TURN[1], nc.scalar.copy, dx_tile(1, (0, 1), "dh5"))
+        scatter(1, 0, True)
         scatter(1, 1, True)
+        second_product(2, (0,), SPARE[0], nc.vector.tensor_copy, dx_tile(2, (0,), "partial7"))
+        quantise(3, "gated7")
         scatter(2, 0, False)
-        second_product(4, (0,), TURN[3], nc.vector.tensor_copy, dx_tile(3, 0))
-        second_product(4, (1,), TURN[0], nc.scalar.copy, dx_tile(3, 1))
+        turn_dh(4, TURN[0])
+        second_product(2, (1,), SUMS[0], nc.scalar.copy, dx_tile(2, (1,), "dh7"))
+        second_product(3, (1,), TURN[2], nc.scalar.copy, dx_tile(3, (1,)))
+        second_product(3, (0,), TURN[1], nc.vector.tensor_copy, dx_tile(3, (0,)))
+        quantise(4)
         scatter(2, 1, True)
         scatter(3, 0, False)
+        second_product(4, (0,), TURN[3], nc.vector.tensor_copy, dx_tile(4, (0,)))
+        second_product(4, (1,), TURN[0], nc.scalar.copy, dx_tile(4, (1,)))
         scatter(3, 1, True)
+        scatter(4, 0, False)
+        scatter(4, 1, True)
         add_and_store(0, SUMS[1:])
         add_and_store(1, (SPARE[0], SUMS[0]))

@@ -89,9 +89,9 @@ def tile_moe_adb_silu_kernel(
         nc.sync.dma_start(out=dy_w[:], in_=dy_words[0].rearrange("p t d -> p (t d)").bitcast(I32))
         nc.sync.dma_start(out=gate_rows[0:CHUNKS, :], in_=gate[0, :].rearrange("(c p) -> c p", p=CHUNK))
         load_a(1)
+        load_scales(wb_s, wbt_scales.rearrange("e g (s r) i -> r s (e g) i", r=4))
         load_a(2)
         load_wb(0)
-        load_scales(wb_s, wbt_scales.rearrange("e g (s r) i -> r s (e g) i", r=4))
         load_a(3)
         load_wb(1)
         nc.sync.dma_start(out=wa_w[:], in_=wat_words.rearrange("e g p k d -> p (e g) (k d)").bitcast(I32))
@@ -269,8 +269,8 @@ def tile_moe_adb_silu_kernel(
         second_product(0, (0, 1), TURN[0], nc.scalar.copy, dx_tile(0, (0, 1)))
         scatter(0, 0, True)
         scatter(0, 1, True)
-        turn_dh(3, TURN[3])
         second_product(1, (0, 1), TURN[1], nc.scalar.copy, dx_tile(1, (0, 1), "dh5"))
+        turn_dh(3, TURN[3])
         scatter(1, 0, True)
         scatter(1, 1, True)
         second_product(2, (0,), SPARE[0], nc.vector.tensor_copy, dx_tile(2, (0,), "partial7"))

@@ -26,15 +26,18 @@ LIST_ROWS = 16
 CHUNK = 128
 CHUNKS = E * C // CHUNK
 QUARTER = 2 * CHUNK
-BANK = 512
 QUARTERS = E * C // QUARTER
-QUARTER_BYTES = QUARTER * PACK * 2
+BANK = 512
 
-BANK_BYTES = 4 * BANK
-TURN = [b * BANK_BYTES for b in (0, 1, 2, 3)]
-SUMS = [b * BANK_BYTES for b in (4, 5, 6)]
-SPARE = [b * BANK_BYTES for b in (7,)]
 GROUPS = ((0, 1), (1, 1), (2, 2), (4, 2), (6, 2))
+
+A_BANKS = [4 * BANK * b for b in range(4)]
+SUM_BANKS = [4 * BANK * b for b in range(4, 7)]
+GATE_BANK = 4 * BANK * 7
+
+SHARED = 64
+DH3_AT = 4 * T - SHARED
+WINDOW_AT = (0, DH3_AT + 2 * H - SHARED)
 
 
 def tile_moe_adb_silu_kernel(
@@ -43,7 +46,7 @@ def tile_moe_adb_silu_kernel(
     nc = tc.nc
     with ExitStack() as ctx:
         keep = ctx.enter_context(tc.tile_pool(name="keep", bufs=1))
-        reused = ctx.enter_context(tc.tile_pool(name="reused", bufs=1))
+        placed = ctx.enter_context(tc.tile_pool(name="placed", bufs=1))
         psum = ctx.enter_context(tc.psum_pool(name="psum", bufs=1))
 
         offsets = keep.tile([P, E * C // LIST_ROWS], U16, name="offsets")
@@ -89,8 +92,8 @@ def tile_moe_adb_silu_kernel(
         nc.sync.dma_start(out=dy_w[:], in_=dy_words[0].rearrange("p t d -> p (t d)").bitcast(I32))
         nc.sync.dma_start(out=gate_rows[0:CHUNKS, :], in_=gate[0, :].rearrange("(c p) -> c p", p=CHUNK))
         load_a(1)
-        load_scales(wb_s, wbt_scales.rearrange("e g (s r) i -> r s (e g) i", r=4))
         load_a(2)
+        load_scales(wb_s, wbt_scales.rearrange("e g (s r) i -> r s (e g) i", r=4))
         load_wb(0)
         load_a(3)
         load_wb(1)
@@ -109,18 +112,16 @@ def tile_moe_adb_silu_kernel(
             nc.vector.tensor_copy(got[:], table.indirect(entries(len(by_chunk) * CHUNK, n)))
             by_chunk.extend(got[:, j : j + CHUNK] for j in range(0, n, CHUNK))
 
-        window = [keep.tile([P, T], F32, name="window%d" % kt) for kt in range(K // P)]
         a_t, silus, tanhs, gated, partial, dh = {}, {}, {}, {}, {}, {}
-        dh_t, grouped, dh_w, dh_s, dx = {}, {}, {}, {}, {}
+        grouped, dh_w, dh_s = {}, {}, {}
+        dx = {}
 
         def sb_tile(name, shape, dtype, tag=None):
-            if isinstance(tag, int):
-                return reused.tile(shape, dtype, name=name, offset=tag, align_bytes=64)
             return keep.tile(shape, dtype, name=name, tag=tag or name, align_bytes=64)
 
         def turn_a(c):
             q, j0 = divmod(c * CHUNK, QUARTER)
-            a_t[c] = psum.tile([P, PACK, P], F32, name="a_t%d" % c, offset=TURN[c % 4])
+            a_t[c] = psum.tile([P, PACK, P], F32, name="a_t%d" % c, offset=A_BANKS[c % len(A_BANKS)])
             for t in range(PACK):
                 nc.tensor.transpose(a_t[c][:, t, :], a_sb[q][:, t, j0 : j0 + CHUNK], ident[:])
 
@@ -142,25 +143,20 @@ def tile_moe_adb_silu_kernel(
             activate(by_pair(tanhs[c]), a_t[c][:].rearrange("j (u o) m -> j u m o", u=2), c, ACT.Tanh, 0.5)
 
         def make_gate_cols():
-            bank = psum.tile([P, 2, CHUNK], F32, name="gate_t", offset=SPARE[0])
+            bank = psum.tile([P, 2, CHUNK], F32, name="gate_t", offset=GATE_BANK)
             nc.tensor.transpose(bank[:, 0, :], gate_rows[:], ident[:])
             cols = keep.tile([P, CHUNKS], F32, name="gate_cols")
             nc.scalar.activation(cols[:], bank[:, 0, 0:CHUNKS], ACT.Copy, scale=-0.5)
             return cols
 
-        def gate_step(c, tag=None):
-            g = gate_cols[:, c : c + 1]
-            gated[c] = sb_tile("gated%d" % c, [P, H], F32, tag)
-            nc.gpsimd.tensor_scalar(gated[c][:], tanhs[c][:], g, g, ALU.mult, ALU.add)
-
-        def gate_on_scalar(c):
+        def gate_step(c):
             g = gate_cols[:, c : c + 1]
             gated[c] = sb_tile("gated%d" % c, [P, H], F32)
-            nc.scalar.activation(gated[c][:], tanhs[c][:], ACT.Identity, bias=g, scale=g)
+            nc.gpsimd.tensor_scalar(gated[c][:], tanhs[c][:], g, g, ALU.mult, ALU.add)
 
         def times_silu(c):
             e = c * CHUNK // C
-            sums = psum.tile([P, H], F32, name="sums%d" % c, offset=SUMS[c % 3])
+            sums = psum.tile([P, H], F32, name="sums%d" % c, offset=SUM_BANKS[c % len(SUM_BANKS)])
             nc.tensor.matmul_mx(
                 out=sums[:], lhsT=chunk_w[c].bitcast(E5M2), lhsT_scale=chunk_s[c],
                 rhs=wb_w[e][:].bitcast(E4M3), rhs_scale=wb_s[:, e, :], start=True, stop=True,
@@ -168,21 +164,24 @@ def tile_moe_adb_silu_kernel(
             partial[c] = sb_tile("partial%d" % c, [P, H], F32)
             nc.vector.scalar_tensor_tensor(partial[c][:], silus[c][:], -1.0, sums[:], ALU.add, ALU.mult)
 
-        def times_gated(c, engine, tag=None):
-            dh[c] = sb_tile("dh%d" % c, [P, H], BF16, tag)
-            engine.tensor_tensor(
+        def times_gated(c):
+            if c == 3:
+                dh[c] = placed.tile([P, H], BF16, name="dh3", offset=DH3_AT, align_bytes=64)
+            else:
+                dh[c] = sb_tile("dh%d" % c, [P, H], BF16)
+            nc.vector.tensor_tensor(
                 by_pair(dh[c]), by_pair(gated[c]), partial[c][:].rearrange("j (m u o) -> j u m o", u=2, o=2), ALU.mult
             )
 
-        def turn_dh(g, bank, tag=None):
+        def turn_dh(g, bank):
             c0, n = GROUPS[g]
-            dh_t[g] = psum.tile([P, n, 2, CHUNK], F32, name="dh_t%d" % g, offset=bank)
+            turned = psum.tile([P, n, 2, CHUNK], F32, name="dh_t%d" % g, offset=bank)
             for h in range(n):
                 pairs = dh[c0 + h][:].bitcast(F32)
                 for u in range(2):
-                    nc.tensor.transpose(dh_t[g][:, h, u, :], pairs[:, u * P : (u + 1) * P], ident[:])
-            grouped[g] = sb_tile("grouped%d" % g, [P, n, CHUNK, 2], F32, tag)
-            nc.scalar.copy(grouped[g][:], dh_t[g][:].rearrange("m h u j -> m h j u"))
+                    nc.tensor.transpose(turned[:, h, u, :], pairs[:, u * P : (u + 1) * P], ident[:])
+            grouped[g] = sb_tile("grouped%d" % g, [P, n, CHUNK, 2], F32)
+            nc.scalar.copy(grouped[g][:], turned[:].rearrange("m h u j -> m h j u"))
 
         def quantise(g, tag=None):
             slots = GROUPS[g][1] * CHUNK
@@ -193,31 +192,30 @@ def tile_moe_adb_silu_kernel(
                 in_=grouped[g][:].rearrange("m h j u -> m (h j u)").bitcast(BF16),
             )
 
-        def second_product(g, halves, bank, copy, dst):
+        def second_product(g, halves, bank, copy, tag=None):
             c0, n = GROUPS[g]
             e = c0 * CHUNK // C
-            acc = psum.tile([P, len(halves), n * CHUNK], F32, name="acc%d_%d" % (g, halves[0]), offset=bank)
+            name = "%d_%d" % (g, halves[0])
+            held = sb_tile("dx" + name, [P, len(halves), n * CHUNK], F32, tag)
+            acc = psum.tile([P, len(halves), n * CHUNK], F32, name="acc" + name, offset=bank)
             for x, kt in enumerate(halves):
+                dx[g, kt] = held[:, x, :]
                 nc.tensor.matmul_mx(
                     out=acc[:, x, :], lhsT=wa_w[:, e, kt * P : (kt + 1) * P].bitcast(E4M3),
                     lhsT_scale=wa_s[:, e, kt * P : (kt + 1) * P],
                     rhs=dh_w[g][:].bitcast(E5M2), rhs_scale=dh_s[g][:], start=True, stop=True,
                 )
-            copy(dst, acc[:])
+            copy(held[:], acc[:])
 
-        def dx_tile(g, halves, tag=None):
-            held = sb_tile("dx%d_%d" % (g, halves[0]), [P, len(halves), GROUPS[g][1] * CHUNK], F32, tag)
-            for x, kt in enumerate(halves):
-                dx[g, kt] = held[:, x, :]
-            return held[:]
-
-        def scatter(g, kt, on_scalar):
+        def tokens_of(g, kt):
             c0, n = GROUPS[g]
-            target = window[kt][:].indirect(entries(c0 * CHUNK, n * CHUNK))
-            if on_scalar:
-                nc.scalar.activation(target, dx[g, kt], ACT.Copy)
-            else:
-                nc.vector.tensor_copy(target, dx[g, kt])
+            return window[kt][:].indirect(entries(c0 * CHUNK, n * CHUNK))
+
+        def scatter_on_scalar(g, kt):
+            nc.scalar.activation(tokens_of(g, kt), dx[g, kt], ACT.Copy)
+
+        def scatter_on_vector(g, kt):
+            nc.vector.tensor_copy(tokens_of(g, kt), dx[g, kt])
 
         def add_and_store(kt, banks):
             for h in range(T // BANK):
@@ -246,47 +244,56 @@ def tile_moe_adb_silu_kernel(
         factors(0)
         gate_cols = make_gate_cols()
         gate_step(0)
-        for c in range(1, 7):
+        for c in range(1, CHUNKS - 1):
             factors(c)
             gate_step(c)
 
         times_silu(0)
         for c in range(2):
             times_silu(c + 1)
-            times_gated(c, nc.vector)
-            turn_dh(c, SPARE[0])
-        factors(7)
-        gate_step(7)
-        for c in range(2, 7):
+            times_gated(c)
+            turn_dh(c, GATE_BANK)
+        factors(CHUNKS - 1)
+        gate_step(CHUNKS - 1)
+        for c in (2, 3):
             times_silu(c + 1)
-            times_gated(c, nc.vector)
-            if c < 4:
-                quantise(c - 2, "partial%d" % c)
-        turn_dh(2, TURN[2])
-        quantise(2, "silu7")
-        times_gated(7, nc.vector)
+            times_gated(c)
+            quantise(c - 2, "partial%d" % c)
+        for c in (4, 5):
+            times_silu(c + 1)
+            times_gated(c)
+        turn_dh(2, A_BANKS[2])
+        quantise(2, "silu6")
+        times_silu(7)
+        times_gated(6)
+        times_gated(7)
 
-        second_product(0, (0, 1), TURN[0], nc.scalar.copy, dx_tile(0, (0, 1)))
-        scatter(0, 0, True)
-        scatter(0, 1, True)
-        second_product(1, (0, 1), TURN[1], nc.scalar.copy, dx_tile(1, (0, 1), "dh5"))
-        turn_dh(3, TURN[3])
-        scatter(1, 0, True)
-        scatter(1, 1, True)
-        second_product(2, (0,), SPARE[0], nc.vector.tensor_copy, dx_tile(2, (0,), "partial7"))
+        window = [
+            placed.tile([P, T], F32, name="window%d" % kt, offset=WINDOW_AT[kt], align_bytes=64)
+            for kt in range(K // P)
+        ]
+        second_product(0, (0, 1), A_BANKS[0], nc.scalar.copy)
+        scatter_on_scalar(0, 0)
+        scatter_on_scalar(0, 1)
+        second_product(1, (0, 1), A_BANKS[1], nc.scalar.copy, "dh5")
+        turn_dh(3, A_BANKS[3])
+        scatter_on_scalar(1, 0)
+        scatter_on_scalar(1, 1)
+
+        second_product(2, (0,), GATE_BANK, nc.vector.tensor_copy, "partial6")
         quantise(3, "gated7")
-        scatter(2, 0, False)
-        turn_dh(4, TURN[0])
-        second_product(2, (1,), SUMS[0], nc.scalar.copy, dx_tile(2, (1,), "dh7"))
-        second_product(3, (1,), TURN[2], nc.scalar.copy, dx_tile(3, (1,)))
-        second_product(3, (0,), TURN[1], nc.vector.tensor_copy, dx_tile(3, (0,)))
+        scatter_on_vector(2, 0)
+        turn_dh(4, A_BANKS[0])
+        second_product(2, (1,), SUM_BANKS[0], nc.scalar.copy, "dh7")
+        second_product(3, (1,), A_BANKS[2], nc.scalar.copy)
+        second_product(3, (0,), A_BANKS[1], nc.vector.tensor_copy)
         quantise(4)
-        scatter(2, 1, True)
-        scatter(3, 0, False)
-        second_product(4, (0,), TURN[3], nc.vector.tensor_copy, dx_tile(4, (0,)))
-        second_product(4, (1,), TURN[0], nc.scalar.copy, dx_tile(4, (1,)))
-        scatter(3, 1, True)
-        scatter(4, 0, False)
-        scatter(4, 1, True)
-        add_and_store(0, SUMS[1:])
-        add_and_store(1, (SPARE[0], SUMS[0]))
+        scatter_on_scalar(2, 1)
+        scatter_on_vector(3, 0)
+        second_product(4, (0,), A_BANKS[3], nc.vector.tensor_copy)
+        second_product(4, (1,), A_BANKS[0], nc.scalar.copy)
+        scatter_on_scalar(3, 1)
+        scatter_on_vector(4, 0)
+        scatter_on_scalar(4, 1)
+        add_and_store(0, SUM_BANKS[1:])
+        add_and_store(1, (GATE_BANK, SUM_BANKS[0]))

@@ -89,16 +89,16 @@ def tile_moe_adb_silu_kernel(
         nc.sync.dma_start(offsets[:], offs)
         load_a(0)
         load_scales(dy_s, dy_scales[0].rearrange("(s r) t -> r s t", r=4))
-        nc.sync.dma_start(out=dy_w[:], in_=dy_words[0].rearrange("p t d -> p (t d)").bitcast(I32))
         nc.sync.dma_start(out=gate_rows[0:CHUNKS, :], in_=gate[0, :].rearrange("(c p) -> c p", p=CHUNK))
+        nc.sync.dma_start(out=dy_w[:], in_=dy_words[0].rearrange("p t d -> p (t d)").bitcast(I32))
         load_a(1)
         load_a(2)
         load_scales(wb_s, wbt_scales.rearrange("e g (s r) i -> r s (e g) i", r=4))
         load_wb(0)
         load_a(3)
         load_wb(1)
-        nc.sync.dma_start(out=wa_w[:], in_=wat_words.rearrange("e g p k d -> p (e g) (k d)").bitcast(I32))
         load_scales(wa_s, wat_scales.rearrange("e g (s r) k -> r s (e g) k", r=4))
+        nc.sync.dma_start(out=wa_w[:], in_=wat_words.rearrange("e g p k d -> p (e g) (k d)").bitcast(I32))
         nc.sync.dma_start(out=wt_w[:].bitcast(I32), in_=wt_words[0].bitcast(I32))
         load_scales(wt_s, wt_scales[0].rearrange("(s r) k -> r s k", r=4))
 

@@ -29,15 +29,12 @@ QUARTER = 2 * CHUNK
 QUARTERS = E * C // QUARTER
 BANK = 512
 
-GROUPS = ((0, 1), (1, 1), (2, 2), (4, 2), (6, 2))
-
-A_BANKS = [4 * BANK * b for b in range(4)]
-SUM_BANKS = [4 * BANK * b for b in range(4, 7)]
-GATE_BANK = 4 * BANK * 7
-
-SHARED = 64
-DH3_AT = 4 * T - SHARED
-WINDOW_AT = (0, DH3_AT + 2 * H - SHARED)
+BANKS = [4 * BANK * b for b in range(8)]
+A_BANKS = [BANKS[b] for b in (0, 1, 0, 1, 0, 1, 6, 0)]
+GATE_BANK = BANKS[7]
+SUM_BANKS = [BANKS[b] for b in (2, 3, 6, 2, 3, 2, 6, 3)]
+TURN_BANKS = BANKS[4:6]
+DX_BANKS = [BANKS[7], BANKS[1]]
 
 
 def tile_moe_adb_silu_kernel(
@@ -46,7 +43,6 @@ def tile_moe_adb_silu_kernel(
     nc = tc.nc
     with ExitStack() as ctx:
         keep = ctx.enter_context(tc.tile_pool(name="keep", bufs=1))
-        placed = ctx.enter_context(tc.tile_pool(name="placed", bufs=1))
         psum = ctx.enter_context(tc.psum_pool(name="psum", bufs=1))
 
         offsets = keep.tile([P, E * C // LIST_ROWS], U16, name="offsets")
@@ -59,10 +55,11 @@ def tile_moe_adb_silu_kernel(
         wt_w = keep.tile([P, 2 * K], U8, name="wt_w", align_bytes=64)
         wt_s = keep.tile([P, K], U8, name="wt_s", align_bytes=64)
         a_sb = [keep.tile([P, PACK, QUARTER], F32, name="a_sb%d" % q) for q in range(QUARTERS)]
-        gate_rows = keep.tile([P, P], F32, name="gate_rows")
+        gate_rows = keep.tile([P, P], F32, name="gate_rows", align_bytes=64)
         ident = keep.tile([P, P], F32, name="ident")
         zero_bias = keep.tile([P, 1], F32, name="zero_bias", align_bytes=64)
         zero_in = keep.tile([P, 1], F32, name="zero_in")
+        window = [keep.tile([P, T], F32, name="window%d" % kt, align_bytes=64) for kt in range(K // P)]
 
         nc.gpsimd.memset(dy_s[:].bitcast(I32), 0)
         nc.vector.memset(gate_rows[:], 0.0)
@@ -92,13 +89,13 @@ def tile_moe_adb_silu_kernel(
         nc.sync.dma_start(out=gate_rows[0:CHUNKS, :], in_=gate[0, :].rearrange("(c p) -> c p", p=CHUNK))
         nc.sync.dma_start(out=dy_w[:], in_=dy_words[0].rearrange("p t d -> p (t d)").bitcast(I32))
         load_a(1)
-        load_a(2)
         load_scales(wb_s, wbt_scales.rearrange("e g (s r) i -> r s (e g) i", r=4))
         load_wb(0)
+        load_a(2)
         load_a(3)
-        load_wb(1)
         load_scales(wa_s, wat_scales.rearrange("e g (s r) k -> r s (e g) k", r=4))
         nc.sync.dma_start(out=wa_w[:], in_=wat_words.rearrange("e g p k d -> p (e g) (k d)").bitcast(I32))
+        load_wb(1)
         nc.sync.dma_start(out=wt_w[:].bitcast(I32), in_=wt_words[0].bitcast(I32))
         load_scales(wt_s, wt_scales[0].rearrange("(s r) k -> r s k", r=4))
 
@@ -112,35 +109,18 @@ def tile_moe_adb_silu_kernel(
             nc.vector.tensor_copy(got[:], table.indirect(entries(len(by_chunk) * CHUNK, n)))
             by_chunk.extend(got[:, j : j + CHUNK] for j in range(0, n, CHUNK))
 
-        a_t, silus, tanhs, gated, partial, dh = {}, {}, {}, {}, {}, {}
-        grouped, dh_w, dh_s = {}, {}, {}
-        dx = {}
+        silus, gated, sums, partial, turned = {}, {}, {}, {}, {}
+        dh, dh_w, dh_s, dx = {}, {}, {}, {}
 
         def sb_tile(name, shape, dtype, tag=None):
             return keep.tile(shape, dtype, name=name, tag=tag or name, align_bytes=64)
 
-        def turn_a(c):
-            q, j0 = divmod(c * CHUNK, QUARTER)
-            a_t[c] = psum.tile([P, PACK, P], F32, name="a_t%d" % c, offset=A_BANKS[c % len(A_BANKS)])
-            for t in range(PACK):
-                nc.tensor.transpose(a_t[c][:, t, :], a_sb[q][:, t, j0 : j0 + CHUNK], ident[:])
-
-        def activate(dst, src, c, func, scale):
-            nc.scalar.activation(dst, src, func, scale=scale, bias=zero_bias[:] if c == 0 else 0.0)
-
-        def silu(c):
-            silus[c] = sb_tile("silu%d" % c, [P, H], F32)
-            activate(
-                silus[c][:].rearrange("j (m t) -> j m t", t=PACK), a_t[c][:].rearrange("j t m -> j m t"),
-                c, ACT.Silu, -1.0,
+        def silu(q):
+            silus[q] = sb_tile("silu%d" % q, [P, QUARTER, PACK], F32, "gate_rows" if q == 1 else None)
+            nc.scalar.activation(
+                silus[q][:].rearrange("m (c i) t -> m c t i", i=2), a_sb[q][:].rearrange("m t (c i) -> m c t i", i=2),
+                ACT.Silu, scale=-1.0, bias=zero_bias[:] if q == 0 else 0.0,
             )
-
-        def by_pair(tile):
-            return tile[:].rearrange("j (u m o) -> j u m o", u=2, o=2)
-
-        def tanh(c):
-            tanhs[c] = sb_tile("tanh%d" % c, [P, H], F32)
-            activate(by_pair(tanhs[c]), a_t[c][:].rearrange("j (u o) m -> j u m o", u=2), c, ACT.Tanh, 0.5)
 
         def make_gate_cols():
             bank = psum.tile([P, 2, CHUNK], F32, name="gate_t", offset=GATE_BANK)
@@ -149,73 +129,79 @@ def tile_moe_adb_silu_kernel(
             nc.scalar.activation(cols[:], bank[:, 0, 0:CHUNKS], ACT.Copy, scale=-0.5)
             return cols
 
-        def gate_step(c):
-            g = gate_cols[:, c : c + 1]
-            gated[c] = sb_tile("gated%d" % c, [P, H], F32)
-            nc.gpsimd.tensor_scalar(gated[c][:], tanhs[c][:], g, g, ALU.mult, ALU.add)
+        def tanh(c):
+            q, j0 = divmod(c * CHUNK, QUARTER)
+            a_t = psum.tile([P, PACK, P], F32, name="a_t%d" % c, offset=A_BANKS[c])
+            for t in range(PACK):
+                nc.tensor.transpose(a_t[:, t, :], a_sb[q][:, t, j0 : j0 + CHUNK], ident[:])
+            th = sb_tile("tanh%d" % c, [P, H], F32)
+            nc.scalar.activation(th[:], a_t[:].rearrange("j t m -> j (t m)"), ACT.Tanh, scale=0.5)
+            return th
 
-        def times_silu(c):
+        def gate_step(c, th):
+            g = gate_cols[:, c : c + 1]
+            gated[c] = sb_tile("gated%d" % c, [P, PACK, P], F32)
+            nc.gpsimd.tensor_scalar(gated[c][:].rearrange("j t m -> j (t m)"), th[:], g, g, ALU.mult, ALU.add)
+
+        def first_product(c):
             e = c * CHUNK // C
-            sums = psum.tile([P, H], F32, name="sums%d" % c, offset=SUM_BANKS[c % len(SUM_BANKS)])
+            sums[c] = psum.tile([P, H], F32, name="sums%d" % c, offset=SUM_BANKS[c])
             nc.tensor.matmul_mx(
-                out=sums[:], lhsT=chunk_w[c].bitcast(E5M2), lhsT_scale=chunk_s[c],
+                out=sums[c][:], lhsT=chunk_w[c].bitcast(E5M2), lhsT_scale=chunk_s[c],
                 rhs=wb_w[e][:].bitcast(E4M3), rhs_scale=wb_s[:, e, :], start=True, stop=True,
             )
-            partial[c] = sb_tile("partial%d" % c, [P, H], F32)
-            nc.vector.scalar_tensor_tensor(partial[c][:], silus[c][:], -1.0, sums[:], ALU.add, ALU.mult)
 
-        def times_gated(c):
-            if c == 3:
-                dh[c] = placed.tile([P, H], BF16, name="dh3", offset=DH3_AT, align_bytes=64)
-            else:
-                dh[c] = sb_tile("dh%d" % c, [P, H], BF16)
+        def times_gated(c, turn=True):
+            partial[c] = sb_tile("partial%d" % c, [P, PACK, P], F32)
             nc.vector.tensor_tensor(
-                by_pair(dh[c]), by_pair(gated[c]), partial[c][:].rearrange("j (m u o) -> j u m o", u=2, o=2), ALU.mult
+                partial[c][:], sums[c][:].rearrange("j (m t) -> j t m", t=PACK), gated[c][:], ALU.mult
+            )
+            if turn:
+                turn_partial(c)
+
+        def turn_partial(c):
+            turned[c] = psum.tile([P, PACK, CHUNK], F32, name="turned%d" % c, offset=TURN_BANKS[c % 2])
+            for t in range(PACK):
+                nc.tensor.transpose(turned[c][:, t, :], partial[c][:, t, :], ident[:])
+
+        def times_silu(c):
+            q, j0 = divmod(c * CHUNK, QUARTER)
+            if j0 == 0:
+                dh[q] = sb_tile("dh%d" % q, [P, QUARTER, PACK], BF16)
+            nc.vector.scalar_tensor_tensor(
+                dh[q][:, j0 : j0 + CHUNK, :], silus[q][:, j0 : j0 + CHUNK, :], -1.0,
+                turned[c][:].rearrange("m t j -> m j t"), ALU.add, ALU.mult,
             )
 
-        def turn_dh(g, bank):
-            c0, n = GROUPS[g]
-            turned = psum.tile([P, n, 2, CHUNK], F32, name="dh_t%d" % g, offset=bank)
-            for h in range(n):
-                pairs = dh[c0 + h][:].bitcast(F32)
-                for u in range(2):
-                    nc.tensor.transpose(turned[:, h, u, :], pairs[:, u * P : (u + 1) * P], ident[:])
-            grouped[g] = sb_tile("grouped%d" % g, [P, n, CHUNK, 2], F32)
-            nc.scalar.copy(grouped[g][:], turned[:].rearrange("m h u j -> m h j u"))
-
-        def quantise(g, tag=None):
-            slots = GROUPS[g][1] * CHUNK
-            dh_w[g] = sb_tile("dh_w%d" % g, [P, slots], I32, tag)
-            dh_s[g] = sb_tile("dh_s%d" % g, [P, slots], U8)
+        def quantise(q):
+            dh_w[q] = sb_tile("dh_w%d" % q, [P, QUARTER], I32)
+            dh_s[q] = sb_tile("dh_s%d" % q, [P, QUARTER], U8)
             nc.vector.quantize_mx(
-                out=dh_w[g][:].bitcast(E5M2), scales=dh_s[g][:],
-                in_=grouped[g][:].rearrange("m h j u -> m (h j u)").bitcast(BF16),
+                out=dh_w[q][:].bitcast(E5M2), scales=dh_s[q][:], in_=dh[q][:].rearrange("m j t -> m (j t)")
             )
 
-        def second_product(g, halves, bank, copy, tag=None):
-            c0, n = GROUPS[g]
-            e = c0 * CHUNK // C
-            name = "%d_%d" % (g, halves[0])
-            held = sb_tile("dx" + name, [P, len(halves), n * CHUNK], F32, tag)
-            acc = psum.tile([P, len(halves), n * CHUNK], F32, name="acc" + name, offset=bank)
+        def second_product(q, halves, bank, copy):
+            e = q * QUARTER // C
+            name = "%d_%d" % (q, halves[0])
+            held = sb_tile("dx" + name, [P, len(halves), QUARTER], F32)
+            acc = psum.tile([P, len(halves), QUARTER], F32, name="acc" + name, offset=bank)
             for x, kt in enumerate(halves):
-                dx[g, kt] = held[:, x, :]
+                dx[q, kt] = held[:, x, :]
                 nc.tensor.matmul_mx(
                     out=acc[:, x, :], lhsT=wa_w[:, e, kt * P : (kt + 1) * P].bitcast(E4M3),
                     lhsT_scale=wa_s[:, e, kt * P : (kt + 1) * P],
-                    rhs=dh_w[g][:].bitcast(E5M2), rhs_scale=dh_s[g][:], start=True, stop=True,
+                    rhs=dh_w[q][:].bitcast(E5M2), rhs_scale=dh_s[q][:], start=True, stop=True,
                 )
             copy(held[:], acc[:])
 
-        def tokens_of(g, kt):
-            c0, n = GROUPS[g]
-            return window[kt][:].indirect(entries(c0 * CHUNK, n * CHUNK))
+        def tokens_of(q, kt):
+            return window[kt][:].indirect(entries(q * QUARTER, QUARTER))
 
-        def scatter_on_scalar(g, kt):
-            nc.scalar.activation(tokens_of(g, kt), dx[g, kt], ACT.Copy)
+        def scatter_on_scalar(q, kt):
+            nc.scalar.activation(tokens_of(q, kt), dx[q, kt], ACT.Copy)
 
-        def scatter_on_vector(g, kt):
-            nc.vector.tensor_copy(tokens_of(g, kt), dx[g, kt])
+        def scatter_on_vector(q, kt):
+            nc.vector.tensor_copy(tokens_of(q, kt), dx[q, kt])
 
         def add_and_store(kt, banks):
             for h in range(T // BANK):
@@ -230,70 +216,72 @@ def tile_moe_adb_silu_kernel(
                 nc.vector.tensor_tensor(res[:], base[:], window[kt][:, toks], ALU.add)
                 nc.sync.dma_start(out=out[kt * P : (kt + 1) * P, toks], in_=res[:])
 
-        def factors(c):
-            turn_a(c)
-            tanh(c)
-            silu(c)
+        def adapters_on_scalar(q):
+            second_product(q, (0, 1), DX_BANKS[q], nc.scalar.copy)
+            scatter_on_scalar(q, 0)
+            scatter_on_scalar(q, 1)
 
         words, scale_bytes = dy_w[:].bitcast(U32), dy_s[:]
         gather(scale_bytes, sb_tile("got_s0", [P, 3 * QUARTER], U8), chunk_s)
         gather(words, sb_tile("got_w0", [P, QUARTER], U32), chunk_w)
-        gather(words, sb_tile("got_w1", [P, 3 * QUARTER], U32), chunk_w)
-        gather(scale_bytes, sb_tile("got_s1", [P, QUARTER], U8), chunk_s)
+        gather(words, sb_tile("got_w1", [P, QUARTER], U32), chunk_w)
 
-        factors(0)
+        silu(0)
+        first = [tanh(0), tanh(1)]
         gate_cols = make_gate_cols()
-        gate_step(0)
-        for c in range(1, CHUNKS - 1):
-            factors(c)
-            gate_step(c)
-
+        gate_step(0, first[0])
+        gate_step(1, first[1])
+        silu(1)
+        gate_step(2, tanh(2))
+        first_product(0)
+        first_product(1)
+        silu(2)
+        gate_step(3, tanh(3))
+        silu(3)
+        times_gated(0)
+        first_product(2)
+        times_gated(1)
+        gather(scale_bytes, sb_tile("got_s1", [P, QUARTER], U8, "gated0"), chunk_s)
+        gate_step(4, tanh(4))
+        gate_step(5, tanh(5))
+        first_product(3)
         times_silu(0)
-        for c in range(2):
-            times_silu(c + 1)
-            times_gated(c)
-            turn_dh(c, GATE_BANK)
-        factors(CHUNKS - 1)
-        gate_step(CHUNKS - 1)
-        for c in (2, 3):
-            times_silu(c + 1)
-            times_gated(c)
-            quantise(c - 2, "partial%d" % c)
-        for c in (4, 5):
-            times_silu(c + 1)
-            times_gated(c)
-        turn_dh(2, A_BANKS[2])
-        quantise(2, "silu6")
+        times_gated(2)
+        gate_step(6, tanh(6))
+        gate_step(7, tanh(7))
+        times_silu(1)
+        times_gated(3)
+        quantise(0)
+        adapters_on_scalar(0)
+        times_silu(2)
+        times_silu(3)
+        gather(words, sb_tile("got_w2", [P, QUARTER], U32, "dh_w0"), chunk_w)
+        first_product(4)
+        first_product(5)
+        quantise(1)
+        adapters_on_scalar(1)
+        gather(words, sb_tile("got_w3", [P, QUARTER], U32, "dh_s0"), chunk_w)
+        first_product(6)
+        times_gated(4)
+        first_product(7)
+        times_gated(5)
+        times_gated(6, turn=False)
+        times_silu(4)
+        turn_partial(6)
+        times_gated(7, turn=False)
+        times_silu(5)
+        turn_partial(7)
+        times_silu(6)
+        quantise(2)
         times_silu(7)
-        times_gated(6)
-        times_gated(7)
-
-        window = [
-            placed.tile([P, T], F32, name="window%d" % kt, offset=WINDOW_AT[kt], align_bytes=64)
-            for kt in range(K // P)
-        ]
-        second_product(0, (0, 1), A_BANKS[0], nc.scalar.copy)
-        scatter_on_scalar(0, 0)
-        scatter_on_scalar(0, 1)
-        second_product(1, (0, 1), A_BANKS[1], nc.scalar.copy, "dh5")
-        turn_dh(3, A_BANKS[3])
-        scatter_on_scalar(1, 0)
-        scatter_on_scalar(1, 1)
-
-        second_product(2, (0,), GATE_BANK, nc.vector.tensor_copy, "partial6")
-        quantise(3, "gated7")
+        second_product(2, (0,), TURN_BANKS[0], nc.vector.tensor_copy)
+        second_product(2, (1,), BANKS[0], nc.scalar.copy)
+        quantise(3)
         scatter_on_vector(2, 0)
-        turn_dh(4, A_BANKS[0])
-        second_product(2, (1,), SUM_BANKS[0], nc.scalar.copy, "dh7")
-        second_product(3, (1,), A_BANKS[2], nc.scalar.copy)
-        second_product(3, (0,), A_BANKS[1], nc.vector.tensor_copy)
-        quantise(4)
         scatter_on_scalar(2, 1)
+        second_product(3, (0,), BANKS[3], nc.vector.tensor_copy)
+        second_product(3, (1,), TURN_BANKS[1], nc.scalar.copy)
         scatter_on_vector(3, 0)
-        second_product(4, (0,), A_BANKS[3], nc.vector.tensor_copy)
-        second_product(4, (1,), A_BANKS[0], nc.scalar.copy)
         scatter_on_scalar(3, 1)
-        scatter_on_vector(4, 0)
-        scatter_on_scalar(4, 1)
-        add_and_store(0, SUM_BANKS[1:])
-        add_and_store(1, (GATE_BANK, SUM_BANKS[0]))
+        add_and_store(0, DX_BANKS)
+        add_and_store(1, (BANKS[2], BANKS[6]))

@@ -59,7 +59,6 @@ def tile_moe_adb_silu_kernel(
         ident = keep.tile([P, P], F32, name="ident")
         zero_bias = keep.tile([P, 1], F32, name="zero_bias", align_bytes=64)
         zero_in = keep.tile([P, 1], F32, name="zero_in")
-        window = [keep.tile([P, T], F32, name="window%d" % kt, align_bytes=64) for kt in range(K // P)]
 
         nc.gpsimd.memset(dy_s[:].bitcast(I32), 0)
         nc.vector.memset(gate_rows[:], 0.0)
@@ -110,7 +109,7 @@ def tile_moe_adb_silu_kernel(
             by_chunk.extend(got[:, j : j + CHUNK] for j in range(0, n, CHUNK))
 
         silus, gated, sums, partial, turned = {}, {}, {}, {}, {}
-        dh, dh_w, dh_s, dx = {}, {}, {}, {}
+        dh, dh_w, dh_s, sums_k, dx, window = {}, {}, {}, {}, {}, {}
 
         def sb_tile(name, shape, dtype, tag=None):
             return keep.tile(shape, dtype, name=name, tag=tag or name, align_bytes=64)
@@ -174,34 +173,36 @@ def tile_moe_adb_silu_kernel(
             )
 
         def quantise(q):
-            dh_w[q] = sb_tile("dh_w%d" % q, [P, QUARTER], I32)
+            dh_w[q] = sb_tile("dh_w%d" % q, [P, QUARTER], I32, "got_w1" if q == 0 else None)
             dh_s[q] = sb_tile("dh_s%d" % q, [P, QUARTER], U8)
             nc.vector.quantize_mx(
                 out=dh_w[q][:].bitcast(E5M2), scales=dh_s[q][:], in_=dh[q][:].rearrange("m j t -> m (j t)")
             )
 
-        def second_product(q, halves, bank, copy):
-            e = q * QUARTER // C
-            name = "%d_%d" % (q, halves[0])
-            held = sb_tile("dx" + name, [P, len(halves), QUARTER], F32)
-            acc = psum.tile([P, len(halves), QUARTER], F32, name="acc" + name, offset=bank)
-            for x, kt in enumerate(halves):
-                dx[q, kt] = held[:, x, :]
+        def second_product(parts, bank):
+            q0, kt0 = parts[0]
+            acc = psum.tile([P, len(parts), QUARTER], F32, name="acc%d_%d" % (q0, kt0), offset=bank)
+            for x, (q, kt) in enumerate(parts):
+                e = q * QUARTER // C
+                sums_k[q, kt] = acc[:, x, :]
                 nc.tensor.matmul_mx(
                     out=acc[:, x, :], lhsT=wa_w[:, e, kt * P : (kt + 1) * P].bitcast(E4M3),
                     lhsT_scale=wa_s[:, e, kt * P : (kt + 1) * P],
                     rhs=dh_w[q][:].bitcast(E5M2), rhs_scale=dh_s[q][:], start=True, stop=True,
                 )
-            copy(held[:], acc[:])
+
+        def hold(q, kt, copy):
+            dx[q, kt] = sb_tile("dx%d_%d" % (q, kt), [P, QUARTER], F32)
+            copy(dx[q, kt][:], sums_k[q, kt])
 
         def tokens_of(q, kt):
             return window[kt][:].indirect(entries(q * QUARTER, QUARTER))
 
         def scatter_on_scalar(q, kt):
-            nc.scalar.activation(tokens_of(q, kt), dx[q, kt], ACT.Copy)
+            nc.scalar.activation(tokens_of(q, kt), dx[q, kt][:], ACT.Copy)
 
         def scatter_on_vector(q, kt):
-            nc.vector.tensor_copy(tokens_of(q, kt), dx[q, kt])
+            nc.vector.tensor_copy(tokens_of(q, kt), dx[q, kt][:])
 
         def add_and_store(kt, banks):
             for h in range(T // BANK):
@@ -215,11 +216,6 @@ def tile_moe_adb_silu_kernel(
                 res = keep.tile([P, BANK], F32, name="res%d_%d" % (kt, h))
                 nc.vector.tensor_tensor(res[:], base[:], window[kt][:, toks], ALU.add)
                 nc.sync.dma_start(out=out[kt * P : (kt + 1) * P, toks], in_=res[:])
-
-        def adapters_on_scalar(q):
-            second_product(q, (0, 1), DX_BANKS[q], nc.scalar.copy)
-            scatter_on_scalar(q, 0)
-            scatter_on_scalar(q, 1)
 
         words, scale_bytes = dy_w[:].bitcast(U32), dy_s[:]
         gather(scale_bytes, sb_tile("got_s0", [P, 3 * QUARTER], U8), chunk_s)
@@ -252,14 +248,24 @@ def tile_moe_adb_silu_kernel(
         times_silu(1)
         times_gated(3)
         quantise(0)
-        adapters_on_scalar(0)
+        second_product(((0, 0), (0, 1)), DX_BANKS[0])
+        hold(0, 0, nc.scalar.copy)
+        hold(0, 1, nc.scalar.copy)
+        window[0] = sb_tile("window0", [P, T], F32)
+        scatter_on_scalar(0, 0)
         times_silu(2)
         times_silu(3)
-        gather(words, sb_tile("got_w2", [P, QUARTER], U32, "dh_w0"), chunk_w)
+        gather(words, sb_tile("got_w2", [P, QUARTER], U32, "got_w1"), chunk_w)
         first_product(4)
         first_product(5)
         quantise(1)
-        adapters_on_scalar(1)
+        second_product(((1, 0), (1, 1)), DX_BANKS[1])
+        window[1] = sb_tile("window1", [P, T], F32, "dh_w1")
+        hold(1, 0, nc.scalar.copy)
+        hold(1, 1, nc.scalar.copy)
+        scatter_on_scalar(0, 1)
+        scatter_on_scalar(1, 0)
+        scatter_on_scalar(1, 1)
         gather(words, sb_tile("got_w3", [P, QUARTER], U32, "dh_s0"), chunk_w)
         first_product(6)
         times_gated(4)
@@ -274,14 +280,17 @@ def tile_moe_adb_silu_kernel(
         times_silu(6)
         quantise(2)
         times_silu(7)
-        second_product(2, (0,), TURN_BANKS[0], nc.vector.tensor_copy)
-        second_product(2, (1,), BANKS[0], nc.scalar.copy)
+        second_product(((2, 0),), TURN_BANKS[0])
+        hold(2, 0, nc.vector.tensor_copy)
         quantise(3)
         scatter_on_vector(2, 0)
-        scatter_on_scalar(2, 1)
-        second_product(3, (0,), BANKS[3], nc.vector.tensor_copy)
-        second_product(3, (1,), TURN_BANKS[1], nc.scalar.copy)
+        second_product(((3, 0),), BANKS[3])
+        second_product(((2, 1), (3, 1)), TURN_BANKS[1])
+        hold(3, 0, nc.vector.tensor_copy)
+        hold(2, 1, nc.scalar.copy)
+        hold(3, 1, nc.scalar.copy)
         scatter_on_vector(3, 0)
+        scatter_on_scalar(2, 1)
         scatter_on_scalar(3, 1)
         add_and_store(0, DX_BANKS)
         add_and_store(1, (BANKS[2], BANKS[6]))

@@ -29,6 +29,8 @@ QUARTER = 2 * CHUNK
 QUARTERS = E * C // QUARTER
 BANK = 512
 
+SPLIT = 448
+
 BANKS = [4 * BANK * b for b in range(8)]
 A_BANKS = [BANKS[b] for b in (0, 1, 0, 1, 0, 1, 6, 0)]
 GATE_BANK = BANKS[7]
@@ -64,7 +66,6 @@ def tile_moe_adb_silu_kernel(
         nc.vector.memset(gate_rows[:], 0.0)
         nc.vector.memset(wb_s[:].bitcast(I32), 0)
         nc.vector.memset(zero_in[:], 0.0)
-        nc.scalar.activation(zero_bias[:], zero_in[:], ACT.Silu)
         nc.vector.memset(wa_s[:].bitcast(I32), 0)
         nc.vector.memset(wt_s[:].bitcast(I32), 0)
 
@@ -83,8 +84,9 @@ def tile_moe_adb_silu_kernel(
         make_identity(nc, ident[:])
 
         nc.sync.dma_start(offsets[:], offs)
-        load_a(0)
         load_scales(dy_s, dy_scales[0].rearrange("(s r) t -> r s t", r=4))
+        load_a(0)
+        nc.scalar.activation(zero_bias[:], zero_in[:], ACT.Silu)
         nc.sync.dma_start(out=gate_rows[0:CHUNKS, :], in_=gate[0, :].rearrange("(c p) -> c p", p=CHUNK))
         nc.sync.dma_start(out=dy_w[:], in_=dy_words[0].rearrange("p t d -> p (t d)").bitcast(I32))
         load_a(1)
@@ -109,7 +111,8 @@ def tile_moe_adb_silu_kernel(
             by_chunk.extend(got[:, j : j + CHUNK] for j in range(0, n, CHUNK))
 
         silus, gated, sums, partial, turned = {}, {}, {}, {}, {}
-        dh, dh_w, dh_s, sums_k, dx, window = {}, {}, {}, {}, {}, {}
+        dh, dh_w, dh_s, sums_k, window = {}, {}, {}, {}, {}
+        dx = [keep.tile([P, E * C], F32, name="dx%d" % kt) for kt in range(K // P)]
 
         def sb_tile(name, shape, dtype, tag=None):
             return keep.tile(shape, dtype, name=name, tag=tag or name, align_bytes=64)
@@ -192,17 +195,13 @@ def tile_moe_adb_silu_kernel(
                 )
 
         def hold(q, kt, copy):
-            dx[q, kt] = sb_tile("dx%d_%d" % (q, kt), [P, QUARTER], F32)
-            copy(dx[q, kt][:], sums_k[q, kt])
+            copy(dx[kt][:, q * QUARTER : (q + 1) * QUARTER], sums_k[q, kt])
 
-        def tokens_of(q, kt):
-            return window[kt][:].indirect(entries(q * QUARTER, QUARTER))
+        def scatter_on_scalar(kt, j0, n):
+            nc.scalar.activation(window[kt][:].indirect(entries(j0, n)), dx[kt][:, j0 : j0 + n], ACT.Copy)
 
-        def scatter_on_scalar(q, kt):
-            nc.scalar.activation(tokens_of(q, kt), dx[q, kt][:], ACT.Copy)
-
-        def scatter_on_vector(q, kt):
-            nc.vector.tensor_copy(tokens_of(q, kt), dx[q, kt][:])
+        def scatter_on_vector(kt, j0, n):
+            nc.vector.tensor_copy(window[kt][:].indirect(entries(j0, n)), dx[kt][:, j0 : j0 + n])
 
         def add_and_store(kt, banks):
             for h in range(T // BANK):
@@ -219,8 +218,10 @@ def tile_moe_adb_silu_kernel(
 
         words, scale_bytes = dy_w[:].bitcast(U32), dy_s[:]
         gather(scale_bytes, sb_tile("got_s0", [P, 3 * QUARTER], U8), chunk_s)
+        gather(scale_bytes, sb_tile("got_s1", [P, QUARTER], U8), chunk_s)
         gather(words, sb_tile("got_w0", [P, QUARTER], U32), chunk_w)
         gather(words, sb_tile("got_w1", [P, QUARTER], U32), chunk_w)
+        gather(words, sb_tile("got_w2", [P, 2 * QUARTER], U32), chunk_w)
 
         silu(0)
         first = [tanh(0), tanh(1)]
@@ -229,20 +230,20 @@ def tile_moe_adb_silu_kernel(
         gate_step(1, first[1])
         silu(1)
         gate_step(2, tanh(2))
+        gate_step(3, tanh(3))
         first_product(0)
         first_product(1)
+        first_product(2)
         silu(2)
-        gate_step(3, tanh(3))
         silu(3)
         times_gated(0)
-        first_product(2)
         times_gated(1)
-        gather(scale_bytes, sb_tile("got_s1", [P, QUARTER], U8, "gated0"), chunk_s)
         gate_step(4, tanh(4))
-        gate_step(5, tanh(5))
         first_product(3)
+        gate_step(5, tanh(5))
+        times_gated(2, turn=False)
         times_silu(0)
-        times_gated(2)
+        turn_partial(2)
         gate_step(6, tanh(6))
         gate_step(7, tanh(7))
         times_silu(1)
@@ -252,10 +253,9 @@ def tile_moe_adb_silu_kernel(
         hold(0, 0, nc.scalar.copy)
         hold(0, 1, nc.scalar.copy)
         window[0] = sb_tile("window0", [P, T], F32)
-        scatter_on_scalar(0, 0)
+        scatter_on_scalar(0, 0, QUARTER)
         times_silu(2)
         times_silu(3)
-        gather(words, sb_tile("got_w2", [P, QUARTER], U32, "got_w1"), chunk_w)
         first_product(4)
         first_product(5)
         quantise(1)
@@ -263,10 +263,9 @@ def tile_moe_adb_silu_kernel(
         window[1] = sb_tile("window1", [P, T], F32, "dh_w1")
         hold(1, 0, nc.scalar.copy)
         hold(1, 1, nc.scalar.copy)
-        scatter_on_scalar(0, 1)
-        scatter_on_scalar(1, 0)
-        scatter_on_scalar(1, 1)
-        gather(words, sb_tile("got_w3", [P, QUARTER], U32, "dh_s0"), chunk_w)
+        scatter_on_scalar(1, 0, QUARTER)
+        scatter_on_scalar(0, QUARTER, SPLIT - QUARTER)
+        scatter_on_scalar(1, QUARTER, QUARTER)
         first_product(6)
         times_gated(4)
         first_product(7)
@@ -283,14 +282,14 @@ def tile_moe_adb_silu_kernel(
         second_product(((2, 0),), TURN_BANKS[0])
         hold(2, 0, nc.vector.tensor_copy)
         quantise(3)
-        scatter_on_vector(2, 0)
+        scatter_on_vector(0, SPLIT, 3 * QUARTER - SPLIT)
         second_product(((3, 0),), BANKS[3])
         second_product(((2, 1), (3, 1)), TURN_BANKS[1])
         hold(3, 0, nc.vector.tensor_copy)
         hold(2, 1, nc.scalar.copy)
         hold(3, 1, nc.scalar.copy)
-        scatter_on_vector(3, 0)
-        scatter_on_scalar(2, 1)
-        scatter_on_scalar(3, 1)
+        scatter_on_vector(0, 3 * QUARTER, QUARTER)
+        scatter_on_scalar(1, 2 * QUARTER, QUARTER)
+        scatter_on_scalar(1, 3 * QUARTER, QUARTER)
         add_and_store(0, DX_BANKS)
         add_and_store(1, (BANKS[2], BANKS[6]))

from contextlib import ExitStack

import concourse.mybir as mybir
from concourse.masks import make_identity

K, T, E, C, H, N = 256, 1024, 2, 512, 512, 512
FLOPS = 2 * N * K * T + 2 * N * H * E * C + 2 * H * K * E * C
BYTES = (N * T + N * T // 32 + N * K // 2 + N * K // 32 + E * N * H + E * N * H // 32 + E * H * K + E * H * K // 32
         + 4 * H * E * C + 4 * E * C + 2 * 128 * (E * C // 16) + 4 * K * T)

F32 = mybir.dt.float32
BF16 = mybir.dt.bfloat16
I32 = mybir.dt.int32
U32 = mybir.dt.uint32
U16 = mybir.dt.uint16
U8 = mybir.dt.uint8
E4M3 = mybir.dt.float8_e4m3fn_x4
E5M2 = mybir.dt.float8_e5m2_x4
E2M1 = mybir.dt.float4_e2m1fn_x4
ACT = mybir.ActivationFunctionType
ALU = mybir.AluOpType

P = 128
PACK = 4
LIST_ROWS = 16
CHUNK = 128
CHUNKS = E * C // CHUNK
QUARTER = 2 * CHUNK
QUARTERS = E * C // QUARTER
BANK = 512

SPLIT = 448

BANKS = [4 * BANK * b for b in range(8)]
A_BANKS = [BANKS[b] for b in (0, 1, 0, 1, 0, 1, 6, 0)]
GATE_BANK = BANKS[7]
SUM_BANKS = [BANKS[b] for b in (2, 3, 6, 2, 3, 2, 6, 3)]
TURN_BANKS = BANKS[4:6]
DX_BANKS = [BANKS[7], BANKS[1]]


def tile_moe_adb_silu_kernel(
    tc, dy_words, dy_scales, wt_words, wt_scales, wbt_words, wbt_scales, wat_words, wat_scales, a, gate, offs, out
):
    nc = tc.nc
    with ExitStack() as ctx:
        keep = ctx.enter_context(tc.tile_pool(name="keep", bufs=1))
        psum = ctx.enter_context(tc.psum_pool(name="psum", bufs=1))

        offsets = keep.tile([P, E * C // LIST_ROWS], U16, name="offsets")
        dy_w = keep.tile([P, T], I32, name="dy_w", align_bytes=64)
        dy_s = keep.tile([P, T], U8, name="dy_s", align_bytes=64)
        wb_w = [keep.tile([P, H], I32, name="wb_w%d" % e, align_bytes=64) for e in range(E)]
        wb_s = keep.tile([P, E, H], U8, name="wb_s", align_bytes=64)
        wa_w = keep.tile([P, E, K], I32, name="wa_w", align_bytes=64)
        wa_s = keep.tile([P, E, K], U8, name="wa_s", align_bytes=64)
        wt_w = keep.tile([P, 2 * K], U8, name="wt_w", align_bytes=64)
        wt_s = keep.tile([P, K], U8, name="wt_s", align_bytes=64)
        a_sb = [keep.tile([P, PACK, QUARTER], F32, name="a_sb%d" % q) for q in range(QUARTERS)]
        gate_rows = keep.tile([P, P], F32, name="gate_rows", align_bytes=64)
        ident = keep.tile([P, P], F32, name="ident")
        zero_bias = keep.tile([P, 1], F32, name="zero_bias", align_bytes=64)
        zero_in = keep.tile([P, 1], F32, name="zero_in")

        nc.gpsimd.memset(dy_s[:].bitcast(I32), 0)
        nc.vector.memset(gate_rows[:], 0.0)
        nc.vector.memset(wb_s[:].bitcast(I32), 0)
        nc.vector.memset(zero_in[:], 0.0)
        nc.vector.memset(wa_s[:].bitcast(I32), 0)
        nc.vector.memset(wt_s[:].bitcast(I32), 0)

        def load_scales(tile, rows):
            for r in range(4):
                nc.sync.dma_start(out=tile[r:P:32].bitcast(I32), in_=rows[r].bitcast(I32))

        def load_a(q):
            nc.sync.dma_start(
                out=a_sb[q][:], in_=a[:, q * QUARTER : (q + 1) * QUARTER].rearrange("(m t) j -> m t j", t=PACK)
            )

        def load_wb(e):
            nc.sync.dma_start(out=wb_w[e][:], in_=wbt_words[e, 0].rearrange("p i d -> p (i d)").bitcast(I32))

        make_identity(nc, ident[:])

        nc.sync.dma_start(offsets[:], offs)
        load_scales(dy_s, dy_scales[0].rearrange("(s r) t -> r s t", r=4))
        load_a(0)
        nc.scalar.activation(zero_bias[:], zero_in[:], ACT.Silu)
        nc.sync.dma_start(out=gate_rows[0:CHUNKS, :], in_=gate[0, :].rearrange("(c p) -> c p", p=CHUNK))
        nc.sync.dma_start(out=dy_w[:], in_=dy_words[0].rearrange("p t d -> p (t d)").bitcast(I32))
        load_a(1)
        load_scales(wb_s, wbt_scales.rearrange("e g (s r) i -> r s (e g) i", r=4))
        load_wb(0)
        load_a(2)
        load_a(3)
        load_scales(wa_s, wat_scales.rearrange("e g (s r) k -> r s (e g) k", r=4))
        nc.sync.dma_start(out=wa_w[:], in_=wat_words.rearrange("e g p k d -> p (e g) (k d)").bitcast(I32))
        load_wb(1)
        nc.sync.dma_start(out=wt_w[:].bitcast(I32), in_=wt_words[0].bitcast(I32))
        load_scales(wt_s, wt_scales[0].rearrange("(s r) k -> r s k", r=4))

        def entries(j0, n):
            return offsets[:, j0 // LIST_ROWS : (j0 + n) // LIST_ROWS]

        chunk_w, chunk_s = [], []

        def gather(table, got, by_chunk):
            n = got.shape[1]
            nc.vector.tensor_copy(got[:], table.indirect(entries(len(by_chunk) * CHUNK, n)))
            by_chunk.extend(got[:, j : j + CHUNK] for j in range(0, n, CHUNK))

        silus, gated, sums, partial, turned = {}, {}, {}, {}, {}
        dh, dh_w, dh_s, sums_k, window = {}, {}, {}, {}, {}
        dx = [keep.tile([P, E * C], F32, name="dx%d" % kt) for kt in range(K // P)]

        def sb_tile(name, shape, dtype, tag=None):
            return keep.tile(shape, dtype, name=name, tag=tag or name, align_bytes=64)

        def silu(q):
            silus[q] = sb_tile("silu%d" % q, [P, QUARTER, PACK], F32, "gate_rows" if q == 1 else None)
            nc.scalar.activation(
                silus[q][:].rearrange("m (c i) t -> m c t i", i=2), a_sb[q][:].rearrange("m t (c i) -> m c t i", i=2),
                ACT.Silu, scale=-1.0, bias=zero_bias[:] if q == 0 else 0.0,
            )

        def make_gate_cols():
            bank = psum.tile([P, 2, CHUNK], F32, name="gate_t", offset=GATE_BANK)
            nc.tensor.transpose(bank[:, 0, :], gate_rows[:], ident[:])
            cols = keep.tile([P, CHUNKS], F32, name="gate_cols")
            nc.scalar.activation(cols[:], bank[:, 0, 0:CHUNKS], ACT.Copy, scale=-0.5)
            return cols

        def tanh(c):
            q, j0 = divmod(c * CHUNK, QUARTER)
            a_t = psum.tile([P, PACK, P], F32, name="a_t%d" % c, offset=A_BANKS[c])
            for t in range(PACK):
                nc.tensor.transpose(a_t[:, t, :], a_sb[q][:, t, j0 : j0 + CHUNK], ident[:])
            th = sb_tile("tanh%d" % c, [P, H], F32)
            nc.scalar.activation(th[:], a_t[:].rearrange("j t m -> j (t m)"), ACT.Tanh, scale=0.5)
            return th

        def gate_step(c, th):
            g = gate_cols[:, c : c + 1]
            gated[c] = sb_tile("gated%d" % c, [P, PACK, P], F32)
            nc.gpsimd.tensor_scalar(gated[c][:].rearrange("j t m -> j (t m)"), th[:], g, g, ALU.mult, ALU.add)

        def first_product(c):
            e = c * CHUNK // C
            sums[c] = psum.tile([P, H], F32, name="sums%d" % c, offset=SUM_BANKS[c])
            nc.tensor.matmul_mx(
                out=sums[c][:], lhsT=chunk_w[c].bitcast(E5M2), lhsT_scale=chunk_s[c],
                rhs=wb_w[e][:].bitcast(E4M3), rhs_scale=wb_s[:, e, :], start=True, stop=True,
            )

        def times_gated(c, turn=True):
            partial[c] = sb_tile("partial%d" % c, [P, PACK, P], F32)
            nc.vector.tensor_tensor(
                partial[c][:], sums[c][:].rearrange("j (m t) -> j t m", t=PACK), gated[c][:], ALU.mult
            )
            if turn:
                turn_partial(c)

        def turn_partial(c):
            turned[c] = psum.tile([P, PACK, CHUNK], F32, name="turned%d" % c, offset=TURN_BANKS[c % 2])
            for t in range(PACK):
                nc.tensor.transpose(turned[c][:, t, :], partial[c][:, t, :], ident[:])

        def times_silu(c):
            q, j0 = divmod(c * CHUNK, QUARTER)
            if j0 == 0:
                dh[q] = sb_tile("dh%d" % q, [P, QUARTER, PACK], BF16)
            nc.vector.scalar_tensor_tensor(
                dh[q][:, j0 : j0 + CHUNK, :], silus[q][:, j0 : j0 + CHUNK, :], -1.0,
                turned[c][:].rearrange("m t j -> m j t"), ALU.add, ALU.mult,
            )

        def quantise(q):
            dh_w[q] = sb_tile("dh_w%d" % q, [P, QUARTER], I32, "got_w1" if q == 0 else None)
            dh_s[q] = sb_tile("dh_s%d" % q, [P, QUARTER], U8)
            nc.vector.quantize_mx(
                out=dh_w[q][:].bitcast(E5M2), scales=dh_s[q][:], in_=dh[q][:].rearrange("m j t -> m (j t)")
            )

        def second_product(parts, bank):
            q0, kt0 = parts[0]
            acc = psum.tile([P, len(parts), QUARTER], F32, name="acc%d_%d" % (q0, kt0), offset=bank)
            for x, (q, kt) in enumerate(parts):
                e = q * QUARTER // C
                sums_k[q, kt] = acc[:, x, :]
                nc.tensor.matmul_mx(
                    out=acc[:, x, :], lhsT=wa_w[:, e, kt * P : (kt + 1) * P].bitcast(E4M3),
                    lhsT_scale=wa_s[:, e, kt * P : (kt + 1) * P],
                    rhs=dh_w[q][:].bitcast(E5M2), rhs_scale=dh_s[q][:], start=True, stop=True,
                )

        def hold(q, kt, copy):
            copy(dx[kt][:, q * QUARTER : (q + 1) * QUARTER], sums_k[q, kt])

        def scatter_on_scalar(kt, j0, n):
            nc.scalar.activation(window[kt][:].indirect(entries(j0, n)), dx[kt][:, j0 : j0 + n], ACT.Copy)

        def scatter_on_vector(kt, j0, n):
            nc.vector.tensor_copy(window[kt][:].indirect(entries(j0, n)), dx[kt][:, j0 : j0 + n])

        def add_and_store(kt, banks):
            for h in range(T // BANK):
                toks = slice(h * BANK, (h + 1) * BANK)
                base = psum.tile([P, BANK], F32, name="base%d_%d" % (kt, h), offset=banks[h])
                nc.tensor.matmul_mx(
                    out=base[:], lhsT=wt_w[:, 2 * kt * P : 2 * (kt + 1) * P].bitcast(E2M1),
                    lhsT_scale=wt_s[:, kt * P : (kt + 1) * P],
                    rhs=dy_w[:, toks].bitcast(E5M2), rhs_scale=dy_s[:, toks], start=True, stop=True,
                )
                res = keep.tile([P, BANK], F32, name="res%d_%d" % (kt, h))
                nc.vector.tensor_tensor(res[:], base[:], window[kt][:, toks], ALU.add)
                nc.sync.dma_start(out=out[kt * P : (kt + 1) * P, toks], in_=res[:])

        words, scale_bytes = dy_w[:].bitcast(U32), dy_s[:]
        gather(scale_bytes, sb_tile("got_s0", [P, 3 * QUARTER], U8), chunk_s)
        gather(scale_bytes, sb_tile("got_s1", [P, QUARTER], U8), chunk_s)
        gather(words, sb_tile("got_w0", [P, QUARTER], U32), chunk_w)
        gather(words, sb_tile("got_w1", [P, QUARTER], U32), chunk_w)
        gather(words, sb_tile("got_w2", [P, 2 * QUARTER], U32), chunk_w)

        silu(0)
        first = [tanh(0), tanh(1)]
        gate_cols = make_gate_cols()
        gate_step(0, first[0])
        gate_step(1, first[1])
        silu(1)
        gate_step(2, tanh(2))
        gate_step(3, tanh(3))
        first_product(0)
        first_product(1)
        first_product(2)
        silu(2)
        silu(3)
        times_gated(0)
        times_gated(1)
        gate_step(4, tanh(4))
        first_product(3)
        gate_step(5, tanh(5))
        times_gated(2, turn=False)
        times_silu(0)
        turn_partial(2)
        gate_step(6, tanh(6))
        gate_step(7, tanh(7))
        times_silu(1)
        times_gated(3)
        quantise(0)
        second_product(((0, 0), (0, 1)), DX_BANKS[0])
        hold(0, 0, nc.scalar.copy)
        hold(0, 1, nc.scalar.copy)
        window[0] = sb_tile("window0", [P, T], F32)
        scatter_on_scalar(0, 0, QUARTER)
        times_silu(2)
        times_silu(3)
        first_product(4)
        first_product(5)
        quantise(1)
        second_product(((1, 0), (1, 1)), DX_BANKS[1])
        window[1] = sb_tile("window1", [P, T], F32, "dh_w1")
        hold(1, 0, nc.scalar.copy)
        hold(1, 1, nc.scalar.copy)
        scatter_on_scalar(1, 0, QUARTER)
        scatter_on_scalar(0, QUARTER, SPLIT - QUARTER)
        scatter_on_scalar(1, QUARTER, QUARTER)
        first_product(6)
        times_gated(4)
        first_product(7)
        times_gated(5)
        times_gated(6, turn=False)
        times_silu(4)
        turn_partial(6)
        times_gated(7, turn=False)
        times_silu(5)
        turn_partial(7)
        times_silu(6)
        quantise(2)
        times_silu(7)
        second_product(((2, 0),), TURN_BANKS[0])
        hold(2, 0, nc.vector.tensor_copy)
        quantise(3)
        scatter_on_vector(0, SPLIT, 3 * QUARTER - SPLIT)
        second_product(((3, 0),), BANKS[3])
        second_product(((2, 1), (3, 1)), TURN_BANKS[1])
        hold(3, 0, nc.vector.tensor_copy)
        hold(2, 1, nc.scalar.copy)
        hold(3, 1, nc.scalar.copy)
        scatter_on_vector(0, 3 * QUARTER, QUARTER)
        scatter_on_scalar(1, 2 * QUARTER, QUARTER)
        scatter_on_scalar(1, 3 * QUARTER, QUARTER)
        add_and_store(0, DX_BANKS)
        add_and_store(1, (BANKS[2], BANKS[6]))
